import numpy as np, ml_dtypes
CORES = [8,136,40,168]
N = 4
BF = ml_dtypes.bfloat16
S, V, KW, L, ST = 2048, 512, 512, 256, 6
def parts(rng):
    lev = rng.integers(0, 256, (N, 8, 1, S)); x = np.clip(lev + rng.integers(-48, 49, (N, 8, 16, S)), 0, 255)
    order = np.argsort(lev[:, :, 0], axis=-1); w = S // 8
    pos = rng.integers(0, S - w + 1, (N, 8, 1, 2 * V)) + rng.integers(0, w, (N, 8, 16, 2 * V))
    near = np.take_along_axis(order, pos.reshape(N, 8, -1), 2).reshape(pos.shape)
    b = np.where(rng.random((N, 8, 1, 2 * V)) < 0.6, near, rng.integers(0, S, (N, 8, 16, 2 * V)))
    k = rng.integers(0, S, (N, 8, 16, KW))
    return x, b, k, rng.integers(0, S, (N, 8, L)), rng.integers(0, V, (N, 8, L)), rng.integers(0, 2, (N, 8, L))
def pack(x, b, k, c, v, d):
    return {"x": np.ascontiguousarray(x.reshape(N, 128, S)).astype(np.float32).astype(BF), "bnd": np.ascontiguousarray(b.reshape(N, 128, 2 * V)).astype(np.int32),
            "kt": np.ascontiguousarray(k.reshape(N, 128, KW)).astype(np.int32), "lc": c.astype(np.int32), "lv": v.astype(np.int32), "ld": d.astype(np.int32)}
def setup_inputs(rng):
    return pack(*parts(rng))
def setup_inputs_spread(rng):
    x, b, k, c, v, d = parts(rng)
    x = np.minimum((np.exp2(8.2 * rng.random((N, 8, 1, S))) * rng.random((N, 8, 16, S))).astype(np.int64), 255)
    def low(n, shape): return np.minimum((n * rng.random(shape) ** 3).astype(np.int64), n - 1)
    b = np.where(rng.random(b.shape) < 0.5, low(S, b.shape), b); k = np.where(rng.random(k.shape) < 0.5, low(S, k.shape), k)
    return pack(x, b, k, low(S, c.shape), low(V, v.shape), (rng.random(d.shape) < rng.random((N, 8, 1))).astype(np.int64))
def setup_inputs_ends(rng):
    def ends(hi, shape):
        u = rng.random(shape)
        return np.where(u < 0.37, 0, np.where(u < 0.75, hi, rng.integers(0, hi + 1, shape)))
    kind = rng.integers(0, 3, (N, 8, 1, S)); kind[..., 1:S - 1:2] = 2
    kind[..., S - 1] = 1; kind[:, 1, :, S - 1] = 0; kind[..., S - 2] = 0; kind[..., 0] = 0; kind[:, 3, :, 0] = 1; kind[:, 7, :, 0] = 1
    x = np.where(kind == 2, 255 * rng.integers(0, 2, (N, 8, 16, S)), 255 * kind)
    b = ends(S - 1, (N, 8, 16, 2 * V)); k = ends(S - 1, (N, 8, 16, KW)); c = ends(S - 1, (N, 8, L)); v = ends(V - 1, (N, 8, L)); d = rng.integers(0, 2, (N, 8, L))
    b[..., 0] = 0; b[..., 1] = 0; b[..., 2 * V - 2] = S - 2
    b[:, :, :15, 2 * V - 1] = 1 + 2 * rng.integers(0, S // 2 - 1, (N, 8, 15)); b[:, :, 15, 2 * V - 1] = S - 1
    for i, w, s in ((0, 0, 1), (1, 0, 0), (L - 2, V - 1, 1), (L - 1, V - 1, 0)):
        c[..., i] = S - 1; v[..., i] = w; d[..., i] = s
    b[..., 10] = S - 1; b[:, :, 15, 10] = S - 2; c[..., 2] = S - 2; v[..., 2] = 5; d[..., 2] = 1
    return pack(x, b, k, c, v, d)
def setup_inputs_corners(rng):
    base = rng.choice(np.array([1, 4, 100, 128, 254]), (N, 8, 1, 1)); sh = np.arange(S); h = S // 4
    m = 8 + (sh // 2) % 3; sgn = np.where(sh % 2 == 0, 1, -1)
    rk = np.argsort(rng.random((N, 8, 16, S)), axis=2)
    x = base + np.where(sh < h, 0, sgn * np.where(rk < m, rng.integers(0, 2, rk.shape), -1))
    kind = rng.integers(0, 5, (N, 8, 1, 2 * V)); at = rng.choice(np.array([0, 7, 15]), kind.shape); hit = np.arange(16)[:, None] == at
    mm = np.where(kind == 4, rng.integers(8, 11, (N, 8, 16, 2 * V)), np.where(kind == 1, 9, np.where((kind == 2) & hit, 10, np.where((kind == 3) & hit, 9, 8))))
    b = 6 * rng.integers((h + 5) // 6, (S - 6) // 6 + 1, mm.shape) + 2 * (mm - 8) + (1 - np.arange(2 * V) % 2)
    few = np.array([0, h - 1, h // 2, S - 1])
    k = np.where(rng.random((N, 8, 16, KW)) < 0.7, rng.integers(0, h, (N, 8, 16, KW)), rng.choice(few, (N, 8, 16, KW)))
    c = np.where(rng.random((N, 8, L)) < 0.7, rng.integers(0, h, (N, 8, L)), rng.choice(few, (N, 8, L)))
    v = np.where(rng.random((N, 8, L)) < 0.7, rng.integers(0, V, (N, 8, L)), rng.choice(np.array([0, V - 1]), (N, 8, L))); d = rng.integers(0, 2, (N, 8, L))
    for i in range(8):
        v[..., i] = V - 1 - i; d[..., i] = i % 2; w = 2 * (V - 1 - i) + 1 - i % 2
        if i < 4: b[:, :, :, w] = c[:, :, i][:, :, None]
        else: b[:, :, 15, w] = c[:, :, i]
    return pack(x, b, k, c, v, d)
def setup_inputs_crowd(rng):
    x, b, k, c, v, d = parts(rng)
    for q in range(N):
        for g in range(8):
            kind = (g + q) % 8; o = rng.permutation(S); s = int(rng.integers(0, 2)); w = int(rng.choice(np.array([0, V - 1, V // 2, 5])))
            one = int(rng.choice(np.array([0, L // 2, L - 1])))
            if kind < 4:
                top = 255 if s == 0 else 0
                a, z, e = o[:48], o[48:96], o[96:112]
                x[q, g][:, a] = top; x[q, g][:, z] = 255 - top; x[q, g][:, e] = np.clip(x[q, g][:, e], 1, 254)
                b[q, g, :, 2 * w + 1 - s] = e; v[q, g] = w; d[q, g] = s
                u, y = (a, z) if kind < 2 else (z, a)
                c[q, g] = u[0] if (kind + q) % 2 == 0 and q % 4 < 2 else rng.choice(u, L)
                if kind % 2 == 1: c[q, g, one] = y[3]
            elif kind == 4: v[q, g] = rng.choice(np.array([0, V - 1, 7, w]), L); c[q, g] = rng.choice(np.array([0, S - 1, int(o[0]), int(o[1])]), L)
            elif kind == 5: k[q, g] = k[q, g, :, :1]
            elif kind == 6: k[q, g] = rng.choice(np.array([0, S - 1]), (16, KW))
            else: c[q, g] = o[0]; v[q, g] = w; d[q, g] = s
    return pack(x, b, k, c, v, d)
def setup_inputs_limits(rng):
    x, b, k, c, v, d = parts(rng); w = S // 8
    for q in range(N):
        for g in range(8):
            o = rng.permutation(S - w); z = o[:14]; at = np.arange(S); at[z] = o[14:28]
            if g % 2 == 1:
                at[S - w:] = o[28:28 + w]; x[q, g][:, S - w:] = 255 * rng.integers(0, 2, (16, 1)); x[q, g, 15, S - w:] = 255
            b[q, g] = at[b[q, g]]; k[q, g] = at[k[q, g]]; c[q, g] = at[c[q, g]]
            x[q, g][:, z] = np.array([255, 255, 255, 255, 0, 0, 0, 0, 200, 200, 200, 200, 40, 160])
            f = int(rng.integers(0, 16)); x[q, g, f, z[1]] = 254; x[q, g, f, z[5]] = 1; x[q, g, f, z[6]] = 3
            x[q, g, rng.permutation(16)[:8], z[3]] = 254
            r = rng.permutation(V - 1); u = [int(a) for a in r[:9]] + [V - 1]; v[q, g] = r[9 + rng.integers(0, V - 10, L)]
            for n, (i, own, s, rest, row, one) in enumerate(((0, 0, 0, 1, 15, 2), (L - 1, 0, 1, 1, 15, 2), (1, 3, 1, 2, 15, 4), (L - 2, 3, 1, 2, 0, 6), (2, 0, 0, 4, 15, 5), (L - 3, 7, 1, 2, 15, 1))):
                c[q, g, i] = z[own]; v[q, g, i] = u[n]; d[q, g, i] = s
                b[q, g, :, 2 * u[n] + 1 - s] = z[rest]; b[q, g, row, 2 * u[n] + 1 - s] = z[one]
            for n, j in enumerate((16, 32, 64, 128)):
                c[q, g, j - 1] = z[12]; c[q, g, j] = z[13]; v[q, g, j - 1:j + 1] = u[6 + n]; d[q, g, j - 1:j + 1] = 0
                b[q, g, :, 2 * u[6 + n] + 1] = z[8 + n]
    return pack(x, b, k, c, v, d)
def check_inputs(d):
    bad = []
    for k, hi in (("x", 255), ("bnd", S - 1), ("kt", S - 1), ("lc", S - 1), ("lv", V - 1), ("ld", 1)):
        a = np.asarray(d[k]).astype(np.float32)
        if not (np.min(a) >= 0 and np.max(a) <= hi): bad.append("range of " + k)
        elif k == "x" and np.any(np.floor(a) != a): bad.append("whole numbers in x")
    return bad
def first(w):
    return ~np.any((w[..., :, None] == w[..., None, :]) & np.tril(np.ones((L, L), bool), -1), axis=-1)
def append(b, col, val, t):
    n, g, i = np.nonzero(first(col)); b[n, g, (5 * t + i) & 15, col[n, g, i]] = val[n, g, i]
def reference(x, bnd, kt, lc, lv, ld):
    X = x.astype(np.float32).astype(np.int32).reshape(N, 8, 16, S).copy(); B = bnd.astype(np.int32).reshape(N, 8, 16, 2 * V).copy(); K = kt.astype(np.int32).reshape(N, 8, 16, KW)
    c, v, d = lc.astype(np.int64), lv.astype(np.int64), ld.astype(np.int64); A = np.zeros((N, 8), np.int64); miss = []
    for t in range(ST):
        q = np.take_along_axis(X, c[:, :, None, :], 3)
        E = np.take_along_axis(B, (2 * v + 1 - d)[:, :, None, :], 3).astype(np.int64)
        xe = np.take_along_axis(X, E.reshape(N, 8, 1, 16 * L), 3).reshape(N, 8, 16, 16, L)
        qq = q[:, :, :, None, :]
        fits = np.where((d == 0)[:, :, None, None, :], qq <= xe, xe <= qq)
        good = np.add.reduce(fits.astype(np.int32), axis=2) >= (9 + (A & 1))[:, :, None, None]
        M = np.add.reduce(np.minimum(xe, qq), axis=2); D = np.add.reduce(np.abs(xe - qq), axis=2)
        hit = np.any(good, axis=2)
        ks = np.where(hit, np.argmax(np.where(good, M, -1), axis=2), np.argmin(D, axis=2))[:, :, None, :]
        e = np.take_along_axis(E, ks, 2)[:, :, 0]; p = (np.take_along_axis(D, ks, 2)[:, :, 0] & 15).astype(np.int64)
        y = np.take_along_axis(X, e[:, :, None, :], 3)
        place = np.where(hit, e, c); value = np.where(hit[:, :, None, :], np.abs(y - (q >> 2)), (q + y) >> 1)
        n, g, i = np.nonzero(first(place)); X[n, g, :, place[n, g, i]] = value[n, g, :, i]
        append(B, 2 * v + d, c, t)
        kc = np.take_along_axis(K, (c & (KW - 1))[:, :, None, :], 3).astype(np.int64); ke = np.take_along_axis(K, (e & (KW - 1))[:, :, None, :], 3).astype(np.int64)
        pair = []
        for z in (p, p ^ 1):
            pair.append((np.take_along_axis(kc, z[:, :, None, :], 2)[:, :, 0], np.take_along_axis(ke, z[:, :, None, :], 2)[:, :, 0] & (V - 1), d ^ (z & 1)))
        c2, v2, d2 = [np.roll(a, 1 + t % (N - 1), axis=0) for a in pair[1]]
        append(B, 2 * v2 + d2, c2, t)
        c, v, d = pair[0]; A = np.add.reduce((~hit).astype(np.int64), axis=2); miss.append(A)
    ys = np.add.reduce(X.reshape(N, 8, 16, 8, S // 8), axis=4)
    return {"yb": B.reshape(N, 128, 2 * V).astype(np.float32), "yc": c.astype(np.float32), "yv": v.astype(np.float32), "yd": d.astype(np.float32),
            "ys": ys.reshape(N, 128, 8).astype(np.float32), "ym": np.stack(miss, axis=2).astype(np.float32)}

@@ -1,0 +1,553 @@
+from concourse.mybir import AluOpType as OP, ActivationFunctionType as AF
+
+ST = 6
+H = "float16"
+MAGIC = 12582912.0
+S0 = 64
+XPRE = 10
+
+F, B16, I32, U16 = "float32", "bfloat16", "int32", "uint16"
+SCRATCH = {}
+
+
+def _sb(name, cols, dtype):
+    SCRATCH[name] = ("sbuf", [128, cols], dtype)
+
+
+for _n, _c, _d in [
+    ("X", 2064, B16), ("Bi", 1024, I32), ("Bf", 1040, F), ("Ki", 512, I32), ("Kw", 512, I32), ("Kc", 2048, F), ("KV", 4096, F),
+    ("l8", 768, I32), ("v8", 256, F), ("Y8", 768, H),
+    ("Eu", 256, U16), ("Ef", 256, F), ("xe", 4096, B16), ("tt", 4096, F), ("q", 256, B16), ("yy", 256, B16),
+    ("kc", 256, F), ("ke", 256, F), ("sx", 256, B16), ("ax", 512, B16),
+    ("Mk", 256, F), ("aa", 256, F), ("pl", 256, F), ("key", 256, F), ("ks", 256, F), ("oh", 256, F), ("sl", 256, F), ("ss", 256, F),
+    ("Pi", 16, I32), ("eT", 16, I32), ("pT", 16, I32), ("parT", 16, I32), ("hd", 32, F), ("misT", 16, B16), ("A0", 16, F), ("A1", 16, F),
+    ("dh", 32, H), ("xp", 128, H), ("xp2", 256, H), ("op2", 256, B16), ("m2s", 256, B16), ("Y2", 512, H), ("Y1", 512, H),
+    ("lke", 16, U16), ("ly", 16, U16), ("lsel", 16, U16), ("lw", 32, U16),
+    ("W1", 32, H), ("w2", 16, H), ("wp", 16, H), ("d2k", 16, H), ("hitW", 16, F), ("t1", 16, F), ("t2", 16, F),
+    ("EQ", 256, H), ("EQb", 256, B16), ("ab", 256, F), ("L1b", 144, B16), ("I32n", 128, B16), ("oX", 32, U16), ("oO", 48, U16), ("cro", 256, F), ("Ag", 256, F), ("Um", 512, F), ("val", 256, B16),
+    ("o8", 768, F), ("ysb", 8, F), ("ymb", 48, F), ("junk", 256, B16),
+    ("sc", 256 * ST, F), ("rc", 256 * ST, F), ("so", 48 * ST, U16), ("ro", 48 * ST, U16),
+    ("row", 272, F), ("row1", 128, F), ("xg", 128, F), ("xa", 272, F), ("xa1", 256, F), ("x7", 128, F),
+    ("pi", 8, I32), ("pc", 16, F),
+    ("Ib", 128, B16), ("Ih", 128, H), ("If", 128, F), ("Im", 128, F), ("I32b", 128, B16), ("I16b", 128, B16), ("I16s", 128, B16),
+    ("Iq", 128, B16), ("Ihalf", 128, B16), ("Iopp", 128, H), ("Iown", 128, H), ("Perm", 128, B16),
+    ("Gq", 256, B16), ("G16", 8, F), ("Gx", 16, B16), ("Gh", 16, H), ("IN", 128, H), ("Dm", 2048, H), ("s12", 32, F),
+    ("L1", 144, H), ("L2", 240, H), ("L8", 144, H), ("NM", 272, F), ("RST", 256, F), ("cZ", 256, B16), ("cS", 512, B16), ("cU", 512, B16),
+    ("mb", 128, F), ("mb2", 256, F), ("lane", 16, H), ("one", 128, B16), ("oneh", 16, H),
+    ("LK", 16, U16), ("LT", 16, U16), ("LE", 16, U16),
+]:
+    _sb(_n, _c, _d)
+for _b in range(8):
+    SCRATCH["P%d" % _b] = ("psum", [128, 512], F)
+
+SEMAPHORES = (["sV", "sS", "sP", "sG", "sent", "dl", "dx", "db", "dk", "dr1", "dr2", "dout"]
+              + ["ac%d" % _t for _t in range(ST)] + ["ao%d" % _t for _t in range(ST)])
+
+
+def rank_program(g, core, T, topo):
+    rank = T.rank_of(core)
+    if rank is None:
+        return
+    N = len(T.cores)
+    Q = {"V": g.vector, "S": g.scalar, "P": g.tensor, "G": g, "Y": g.sync}
+    cnt = {"V": 0, "S": 0, "P": 0, "G": 0}
+    seen = {e: {} for e in Q}
+    hist = {}
+
+    def R(name, lo=0, hi=None, step=1, p1=128):
+        if hi is None:
+            hi = SCRATCH[name][1][1]
+        return (name, lo, hi, T[name][0:p1, lo:hi:step] if step != 1 else T[name][0:p1, lo:hi])
+
+    def wait(e, tok):
+        if seen[e].get(tok[0], 0) < tok[1]:
+            Q[e].wait_ge(T.sem[tok[0]], tok[1])
+            seen[e][tok[0]] = tok[1]
+
+    def deps(e, reads, writes):
+        need = {}
+        for regs, w in ((reads, False), (writes, True)):
+            for r in regs:
+                ps = SCRATCH[r[0]][0] == "psum"
+                for (lo, hi, e2, tok, w2) in hist.get(r[0], []):
+                    clash = lo < r[2] and r[1] < hi and (w or w2)
+                    if e2 != e:
+                        clash = clash or ps
+                    elif e == "P":
+                        clash = False
+                    if clash:
+                        need[tok[0]] = max(need.get(tok[0], 0), tok[1])
+        for k in sorted(need):
+            wait(e, (k, need[k]))
+
+    def note(e, tok, reads, writes):
+        for regs, w in ((reads, False), (writes, True)):
+            for r in regs:
+                old = hist.get(r[0], [])
+                keep = [x for x in old if not (r[1] <= x[0] and x[1] <= r[2] and x[2] == e and x[3][0] == tok[0] and (w or not x[4]))]
+                hist[r[0]] = keep + [(r[1], r[2], e, tok, w)]
+
+    def emit(e, reads, writes, call):
+        deps(e, reads, writes)
+        cnt[e] += 1
+        call().then_inc(T.sem["s" + e], 1)
+        note(e, ("s" + e, cnt[e]), reads, writes)
+
+    def ind(win, off):
+        return ([win, off], win[3].indirect(off[3]))
+
+    def sides(x):
+        return (x[0], x[1]) if len(x) == 2 else ([x], x[3])
+
+    def outs(o):
+        return ([o[0][0]], [o[0][1]], o[1]) if len(o) == 2 else ([o], [], o[3])
+
+    def cp(o, i):
+        w, r0, oa = outs(o)
+        r, ia = sides(i)
+        emit("V", r + r0, w, lambda: g.vector.tensor_copy(oa, ia))
+
+    def tt(o, a, b, op):
+        w, r0, oa = outs(o)
+        r, ia = sides(a)
+        emit("V", r + r0 + [b], w, lambda: g.vector.tensor_tensor(oa, ia, b[3], op))
+
+    def ts(o, a, s1, op0, s2=None, op1=None):
+        r, ia = sides(a)
+        rs = [s for s in (s1, s2) if isinstance(s, tuple)]
+        a1 = s1[3] if isinstance(s1, tuple) else s1
+        a2 = s2[3] if isinstance(s2, tuple) else s2
+        if op1 is None:
+            emit("V", r + rs, [o], lambda: g.vector.tensor_scalar(o[3], ia, a1, None, op0))
+        else:
+            emit("V", r + rs, [o], lambda: g.vector.tensor_scalar(o[3], ia, a1, a2, op0, op1))
+
+    def scan(o, d0, d1):
+        emit("V", [d0, d1], [o], lambda: g.vector.tensor_tensor_scan(o[3], d0[3], d1[3], 0.0, OP.min, OP.max))
+
+    def mset(o, v):
+        emit("V", [], [o], lambda: g.vector.memset(o[3], v))
+
+    def act(o, i, fn=AF.Identity, bias=0.0, scale=1.0, acc=None):
+        r, ia = sides(i)
+        rs = [bias] if isinstance(bias, tuple) else []
+        ba = bias[3] if isinstance(bias, tuple) else bias
+        if acc is None:
+            emit("S", r + rs, [o], lambda: g.scalar.activation(o[3], ia, fn, bias=ba, scale=scale))
+        else:
+            emit("S", r + rs, [o, acc], lambda: g.scalar.activation(o[3], ia, fn, bias=ba, scale=scale, accum_out=acc[3]))
+
+    def mm(o, l, r, start, stop):
+        emit("P", [l, r], [o], lambda: g.tensor.matmul(o[3], l[3], r[3], start, stop))
+
+    def iota(o, pat, base=0, cm=0):
+        if SCRATCH[o[0]][2] != I32:
+            emit("G", [], [o], lambda: g.iota(o[3], pat, base, cm, allow_small_or_imprecise_dtypes=True))
+        else:
+            emit("G", [], [o], lambda: g.iota(o[3], pat, base, cm))
+
+    def dma(e, sem, total, out_ap, in_ap, reads, writes):
+        deps(e, reads, writes)
+        Q[e].dma_start(out_ap, in_ap).then_inc(T.sem[sem], 16)
+        note("D", (sem, total), reads, writes)
+
+    PCOL, ACOL, GCOL, PARC, HC, L1C, L2C, L8C, LANEC, DXC, DBC, FLIPC = [R("pc", j, j + 1) for j in range(12)]
+    LOPP, LCW, WO, WC = R("lw", 0, 16), R("lw", 16, 32), R("W1", 0, 16), R("W1", 16, 32)
+
+    dma("Y", "dl", 48, T.l8[0:8, 0:256], T.lv[:], [], [R("l8", 0, 256)])
+    dma("S", "dl", 48, T.l8[0:8, 256:512], T.lc[:], [], [R("l8", 256, 512)])
+    dma("Y", "dl", 48, T.l8[0:8, 512:768], T.ld[:], [], [R("l8", 512, 768)])
+    dma("S", "db", 16, T.Bi[:], T.bnd[:], [], [R("Bi")])
+    dma("Y", "dx", 16, T.X[:, 0:2048], T.x[:], [], [R("X", 0, 2048)])
+    dma("S", "dk", 16, T.Ki[:], T.kt[:], [], [R("Ki")])
+
+    pi = lambda j: R("pi", j, j + 1)
+    iota(pi(0), [[0, 1]], 0, 1)
+    iota(R("row", 0, 144), [[1, 144]])
+    iota(R("xg"), [[1, 8], [0, 16]])
+    iota(R("xa"), [[0, 17], [1, 16]])
+    iota(R("row", 144, 272), [[1, 128]], 144)
+    iota(R("x7"), [[0, 16], [1, 8]])
+    iota(R("row1"), [[2, 64], [-1, 2]], 1)
+    iota(R("xa1"), [[0, 16], [2, 8], [-1, 2]], 1)
+    iota(R("one"), [[0, 128]], 1)
+    iota(R("cU"), [[0, 512]], 1)
+    ts(pi(1), pi(0), 15, OP.bitwise_and)
+    ts(pi(2), pi(0), 4, OP.arith_shift_right)
+    ts(pi(3), pi(0), 1, OP.bitwise_and)
+    ts(pi(4), pi(0), 8, OP.bitwise_and)
+    mset(R("X", 2048, 2064), 0.0)
+    cp(R("pc", 0, 5), R("pi", 0, 5))
+    mset(R("Bf", 1024, 1040), 0.0)
+    ts(L8C, PCOL, 16.0, OP.mult, 15.0, OP.add)
+    act(L1C, GCOL, scale=16.0, bias=15.0)
+    act(L2C, ACOL, bias=112.0)
+    act(LANEC, ACOL, bias=128.0)
+    act(DXC, ACOL, bias=2048.0)
+    act(DBC, ACOL, bias=1024.0)
+    act(FLIPC, PARC, scale=-2.0, bias=1.0)
+    ts(R("Ib"), R("row", 0, 128), PCOL, OP.is_equal)
+    ts(R("L8", 0, 144), R("row", 0, 144), L8C, OP.is_equal)
+    cp(R("Ih"), R("Ib"))
+    cp(R("LT"), R("row", 0, 16))
+    ts(R("Gq", 0, 128), R("xg"), GCOL, OP.is_equal, 16.0, OP.mult)
+    ts(R("G16"), R("row", 0, 8), GCOL, OP.is_equal, 16.0, OP.mult)
+    ts(R("L1b"), R("row", 0, 144), L1C, OP.is_equal)
+    ts(R("s12", 0, 16), R("row", 0, 16), ACOL, OP.is_ge)
+    ts(R("s12", 16, 32), R("row", 0, 16), ACOL, OP.is_equal)
+    act(R("I32n"), R("Ib"), scale=-32.0)
+    act(R("I16s"), R("Ib"), scale=-128.0)
+    act(R("cZ"), R("xa", 0, 256), scale=-1.0, bias=15.0)
+    for h in range(2):
+        act(R("cS", 256 * h, 256 * h + 128), R("xa", 0, 128), scale=-1.0, bias=31.0)
+        act(R("cS", 256 * h + 128, 256 * h + 256), R("xa", 0, 128), scale=-256.0, bias=3840.0)
+    act(R("Gq", 128, 256), R("Gq", 0, 128), scale=128.0)
+    act(R("Gx", 0, 8), R("G16"))
+    act(R("Gx", 8, 16), R("G16"), scale=128.0)
+    mm(R("P6", 0, 128), R("Ib"), R("Gq", 0, 128), True, False)
+    mm(R("P6", 0, 128), R("Ib"), R("I32n"), False, True)
+
+    def Lsl(name, a, p1=128):
+        return R(name, 15 - a, 143 - a, p1=p1)
+
+    def y_to_w(out, ybuf, lo, hi, start, L="L1", p1=128):
+        for a in range(16):
+            mm(out, Lsl(L, a, p1), R(ybuf, lo + a, hi, 16, p1=p1), start and a == 0, a == 15)
+
+    def rot(ybuf, lo, t, dst, L="L1", p1=128):
+        for a in range(16):
+            mm(R("P5", a, 256, 16), Lsl(L, (5 * t + a) % 16, p1), R(ybuf, lo + a, lo + 256, 16, p1=p1), True, True)
+        act(dst, R("P5", 0, 256))
+
+    def t_to_w(out, xbuf, n, start, stop, lo=0):
+        for gg in range(8):
+            mm(out, R("L2", 112 - 16 * gg, 240 - 16 * gg), R(xbuf, lo + n * gg, lo + n * gg + n), start and gg == 0, stop and gg == 7)
+
+    def diff(w, bank="P6"):
+        for a in range(1, 16):
+            mm(R(bank, 16 * a, 16 * a + 16), R("Dm", 128 * a, 128 * a + 128), w, True, True)
+
+    def eq():
+        ts(R("EQ", 16, 256), R("P6", 16, 256), 0.0, OP.is_equal, 4096.0, OP.mult)
+
+    def eq_s(bank="P6"):
+        act(R("ab", 16, 256), R(bank, 16, 256), AF.Abs)
+        act(R("EQb", 16, 256), R("ab", 16, 256), AF.Relu, scale=-4096.0, bias=4096.0)
+
+    def losers(out, w, own=False, sc=False):
+        mm(out, R("Ih"), w, True, False)
+        if own:
+            mm(out, R("Iown"), R("d2k"), False, False)
+        for a in range(1, 16):
+            mm(out, Lsl("L1b" if sc else "L1", a), R("EQb" if sc else "EQ", 16 * a, 16 * a + 16), False, a == 15)
+
+    def offs(o, src, dummy, sub=-1.0):
+        ts(o, src, sub, OP.add, dummy, OP.min)
+
+    def old_columns(off, o, t):
+        s = (5 * t) % 16
+        tt(R("Ag"), ind(R("Bf"), R(off, o, o + 16)), R("NM", s, s + 256), OP.mult)
+
+    def put_b(off, o, crot, c, b):
+        tt(ind(R("Bf"), R(off, o + 16 + 2 * b, o + 17 + 2 * b)), R("Ag", 16 * b, 16 * b + 16), R(crot, c + 16 * b, c + 16 * b + 16), OP.add)
+
+    def put_x(b):
+        cp(ind(R("X"), R("oX", 2 * b, 2 * b + 1)), R("val", 16 * b, 16 * b + 16))
+
+    def prep_side(t):
+        act(R("sx"), ind(R("hd", 16, 32), R("LT")), scale=1.0 / 256, bias=-1.0 / 512)
+        mm(R("P1", 0, 256), R("Ib"), R("cZ"), True, False)
+        mm(R("P1", 0, 256), R("I16s"), R("sx"), False, False)
+        if t > 0:
+            act(R("ax", 0, 256), ind(R("A0"), R("LT")))
+            act(R("ax", 256, 512), ind(R("A1"), R("LT")), bias=-MAGIC)
+            mm(R("P1", 0, 256), R("I32b"), R("ax", 0, 256), False, False)
+            mm(R("P1", 0, 256), R("I16b"), R("ax", 256, 512), False, False)
+        mm(R("P2"), R("Ib"), R("cS"), True, False)
+
+    def prep_q():
+        act(R("q"), ind(R("X"), LCW))
+        mm(R("P0", 0, 256), R("Ib"), R("q"), True, False)
+        for h in range(2):
+            mm(R("P0", 128 * h, 128 * h + 128), R("sx", 128 * h, 128 * h + 128), R("Ib"), False, h == 1)
+        for h in range(2):
+            mm(R("P2", 256 * h, 256 * h + 256), R("q", 128 * h, 128 * h + 128), R("Gq"), False, False)
+
+    def own_diff():
+        diff(WO)
+
+    def own_offsets():
+        offs(R("oO", 0, 16), R("P4", 320, 336), DBC, -2.0)
+        offs(R("oO", 16, 48, 2), R("P4", 320, 336), DBC, -2.0)
+
+    ts(R("v8", p1=8), R("l8", 0, 256, p1=8), 2.0, OP.mult, 1.0, OP.add)
+    cp(R("Y8", 256, 512, p1=8), R("l8", 256, 512, p1=8))
+    tt(R("Y8", 0, 256, p1=8), R("v8", p1=8), R("l8", 512, 768, p1=8), OP.subtract)
+    ts(R("Y8", 512, 768, p1=8), R("l8", 512, 768, p1=8), 2048.0, OP.mult)
+    y_to_w(R("P4", 256, 304), "Y8", 0, 768, True, "L8", 8)
+    for h in range(2):
+        mm(R("P7", 8 * h, 8 * h + 8), R("Y8", 512 + 128 * h, 640 + 128 * h, p1=8), R("Ih", 0, 8, p1=8), True, True)
+    cp(R("lw"), R("P4", 256, 288))
+    ts(R("hd", 16, 32), R("P7", 0, 16), 1.0 / 2048, OP.mult)
+
+    def consts_a():
+        ts(R("IN"), R("P6", 0, 128), 1.0 / 16, OP.mult)
+        ts(R("W1"), R("P4", 256, 288), 1.0, OP.add)
+        cp(R("d2k"), R("P4", 288, 304))
+        cp(R("Kc", 0, 512), R("Ki"))
+        ts(R("Kw"), R("Ki"), 511, OP.bitwise_and)
+        ts(R("Iown"), R("Ih"), 1.0 / 1024, OP.mult)
+        ts(R("KV", 0, 512), R("Kw"), 2.0, OP.mult, PARC, OP.add)
+        for j in range(1, 4):
+            dma("Y", "dr1", 48, T.Kc[:, 512 * j:512 * j + 512], T.Kc[:, 0:512], [R("Kc", 0, 512)], [R("Kc", 512 * j, 512 * j + 512)])
+        ts(R("mb"), R("x7"), GCOL, OP.is_equal)
+
+    def consts_d():
+        for a in range(1, 16):
+            ts(R("Dm", 128 * a, 128 * a + 128), R("IN"), R("s12", a, a + 1), OP.mult, R("s12", 16 + a, 17 + a), OP.min)
+
+    def consts_s():
+        act(R("KV", 2048, 2560), R("KV", 0, 512), bias=FLIPC)
+        for s in (0, 2048):
+            for j in range(1, 4):
+                dma("Y", "dr2", 96, T.KV[:, s + 512 * j:s + 512 * j + 512], T.KV[:, s:s + 512],
+                    [R("KV", s, s + 512)], [R("KV", s + 512 * j, s + 512 * j + 512)])
+        act(R("RST"), R("xa", 0, 256), scale=1.0e8, bias=-5.0e7)
+        act(R("Im"), R("Ib"), scale=-256.0)
+        act(R("Iq"), R("Ib"), scale=-0.25)
+        act(R("Ihalf"), R("Ib"), scale=0.5)
+        act(R("cU", 0, 256), R("cU", 0, 256), scale=0.375)
+        act(R("cU", 256, 512), R("cU", 256, 512), scale=-0.25)
+        act(R("I32b"), R("Ib"), scale=1.0 / 32)
+        act(R("I16b"), R("Ib"), scale=-1.0 / 16)
+        act(R("If"), R("Ib"))
+        act(R("mb2", 0, 128), R("mb"), scale=-128.0)
+        act(R("mb2", 128, 256), R("mb"), scale=2048.0)
+
+    def consts_b():
+        cp(R("Bf", 0, 1024), R("Bi"))
+        ts(R("NM"), R("xa"), ACOL, OP.not_equal)
+        ts(R("LK"), R("row", 0, 16), 16.0, OP.mult, 15.0, OP.add)
+        ts(R("L2"), R("row", 0, 240), L2C, OP.is_equal)
+        ts(R("LE", 0, 8), R("row", 0, 8), HC, OP.add)
+        ts(R("LE", 8, 16), R("row", 16, 24), HC, OP.add)
+        cp(R("L1"), R("L1b"))
+        ts(R("oneh"), R("row", 0, 16), 0.0, OP.mult, 1.0, OP.add)
+        ts(R("Perm"), R("row1"), PCOL, OP.is_equal)
+        ts(R("lane"), R("row", 0, 16), 16.0, OP.mult, LANEC, OP.add)
+        ts(R("Iopp"), R("Ih"), -1.0 / 1024, OP.mult)
+        mset(R("so"), 0)
+
+    prep_side(0)
+    nsent = 0
+    for t in range(ST):
+        last = t == ST - 1
+        dst = T.cores[(rank + 1 + t % (N - 1)) % N]
+        rid, pid = topo.addr(dst, core)
+        msk = topo.mask(core, dst)
+        neng = len(topo.engines(core, dst))
+        nin = len(topo.engines(T.cores[(rank - 1 - t % (N - 1)) % N], core))
+
+        def send(reg, rname, sem):
+            deps("G", [reg], [])
+            g.remote_dma(T[rname][:, reg[1]:reg[2]], reg[3], T.sem[sem], T.sem.sent, pid, rid, msk)
+
+        cp(R("Eu"), ind(R("Bi") if t == 0 else R("Bf"), LOPP))
+        prep_q()
+        s0 = 128 if t == 0 else S0
+        act(R("xe", 0, 16 * s0), ind(R("X"), R("Eu", 0, s0)))
+        if t == 0:
+            consts_a()
+        else:
+            cp(R("xe", 16 * s0, 2048), ind(R("X"), R("Eu", s0, 128)))
+        act(R("xe", 2048, 4096), ind(R("X"), R("Eu", 128, 256)))
+        if t == 0:
+            consts_s()
+        else:
+            act(R("Ef"), ind(R("Bf", 0, 1024), LOPP))
+        for h in range(2):
+            for k in range(16):
+                o = 2048 * h + 128 * k
+                tt(R("tt", o, o + 128), R("xe", 2048 * h + k, 2048 * h + 2048, 16), R("P0", 128 * h, 128 * h + 128), OP.min)
+                mm(R("P2", 256 * h + k, 256 * h + 256, 16), R("xe", 2048 * h + k, 2048 * h + 2048, 16), R("Gx"), False, h == 1 and k == 15)
+                mm(R("P1", 128 * h + k, 128 * h + 128, 16), R("tt", o, o + 128), R("G16"), False, h == 1 and k == 15)
+            if t == 0 and h == 0:
+                consts_d()
+                rot("Y8", 256, 0, R("cro"), "L8", 8)
+                own_diff()
+                eq_s()
+        if t == 0:
+            losers(R("P4", 320, 336), WO, True, True)
+            consts_b()
+            cp(R("Ef"), R("Eu"))
+            own_offsets()
+        act(R("kc"), ind(R("Kc"), LCW))
+        old_columns("oO", 0, t)
+        nb = [16]
+
+        def own(n=1):
+            for _ in range(n):
+                if nb[0]:
+                    nb[0] -= 1
+                    put_b("oO", 0, "cro", 0, nb[0])
+
+        Z, NG = R("P1", 0, 256), R("P1", 256, 512)
+        own()
+        ts(R("Mk"), Z, MAGIC, OP.add, MAGIC, OP.subtract)
+        own()
+        for h in range(2):
+            tt(R("aa", 128 * h, 128 * h + 128), R("Mk", 128 * h, 128 * h + 128), R("P2", 256 * h, 256 * h + 128), OP.subtract)
+        for h in range(2):
+            act(R("pl", 128 * h, 128 * h + 128), R("P2", 256 * h + 128, 256 * h + 256))
+        mm(R("P5", 0, 256), R("Im"), R("Mk"), True, False)
+        for h in range(2):
+            mm(R("P5", 128 * h, 128 * h + 128), R("Ef", 128 * h, 128 * h + 128), R("If"), False, False)
+        mm(R("P5", 0, 256), R("If"), R("pl"), False, True)
+        mm(R("P3"), R("Ib"), R("cU"), True, False)
+        mm(R("P3", 0, 256), R("Iq"), R("q"), False, False)
+        mm(R("P3", 256, 512), R("Ihalf"), R("q"), False, False)
+        tt(NG, R("Mk"), Z, OP.is_le)
+        own()
+        tt(NG, R("aa"), NG, OP.mult)
+        own()
+        tt(R("key"), R("Mk"), NG, OP.add)
+        own()
+        scan(R("ks"), R("RST"), R("key"))
+        act(R("hd", 0, 16), R("ks", 15, 256, 16), AF.Sign, bias=0.5)
+        act(R("misT"), R("hd", 0, 16), scale=-0.5, bias=0.5)
+        own()
+        tt(R("oh"), ind(R("ks"), R("LK")), R("key"), OP.is_equal)
+        own()
+        tt(R("sl"), R("oh"), R("P5", 0, 256), OP.mult)
+        tt(R("xp2", 0, 128), ind(R("hd", 0, 16), R("LE", 0, 8)), R("mb2", 0, 128), OP.mult)
+        mm(R("P4", 256, 272), R("Ih"), R("lane"), True, False)
+        t_to_w(R("P4", 256, 272), "xp2", 16, False, True)
+        for j in range(2):
+            for h in range(2):
+                mm(R("P6", 256 + 8 * j, 264 + 8 * j), R("one"), R("misT", 8 * h, 8 * h + 8), h == 0, h == 1)
+        act(R("A0"), R("P6", 256, 272))
+        act(R("ymb", t, 48, 6, p1=1), R("A0", 0, 8, p1=1))
+        if not last:
+            act(R("A1"), R("A0"), scale=0.499, bias=MAGIC)
+        scan(R("ss"), R("RST"), R("sl"))
+        ts(R("hitW"), R("P4", 256, 272), 256.0, OP.is_lt)
+        cp(R("Pi"), R("ss", 15, 256, 16))
+        cp(R("lsel"), R("P4", 256, 272))
+        ts(R("eT"), R("Pi"), 2047, OP.bitwise_and)
+        ts(R("pT"), R("Pi"), 11, OP.arith_shift_right, 15, OP.bitwise_and)
+        tt(R("xp"), ind(R("eT"), R("LE", 0, 8)), R("mb"), OP.mult)
+        mm(R("P7", 0, 16), R("Ih"), R("d2k"), True, False)
+        t_to_w(R("P7", 0, 16), "xp", 16, False, True)
+        tt(R("op2"), ind(R("pT"), R("LT")), R("xa1"), OP.is_equal)
+        cp(R("lke"), R("P7", 0, 16))
+        act(R("ke"), ind(R("KV"), R("lke")))
+        for h in range(2):
+            mm(R("P4", 128 * h, 128 * h + 128), R("op2", 128 * h, 128 * h + 128), R("Ib"), True, True)
+        for h in range(2):
+            mm(R("P0", 128 * h, 128 * h + 128), R("op2", 128 * h, 128 * h + 128), R("Ib"), True, True)
+        mm(R("P7", 64, 80), R("Ih"), R("oneh"), True, False)
+        t_to_w(R("P7", 64, 80), "xp", 16, False, True)
+        own()
+        tt(R("Y2", 0, 256), R("kc"), R("P4", 0, 256), OP.mult)
+        act(R("m2s"), R("P0", 0, 256))
+        tt(R("t1"), R("P7", 64, 80), WC, OP.subtract)
+        ts(R("ly"), R("P7", 64, 80), -1.0, OP.add)
+        tt(R("Y2", 256, 512), R("ke"), R("P4", 0, 256), OP.mult)
+        rot("Y2", 0, t, R("sc", 256 * t, 256 * t + 256))
+        send(R("sc", 256 * t, 256 * t + 256), "rc", "ac%d" % t)
+        tt(R("t2"), R("t1"), R("hitW"), OP.mult)
+        y_to_w(R("P7", 16, 32), "Y2", 256, 512, True)
+        act(R("yy"), ind(R("X"), R("ly")))
+        ts(R("parT"), R("pT"), 1, OP.bitwise_and)
+        tt(R("wp"), R("t2"), WC, OP.add)
+        tt(R("hd", 16, 32), R("hd", 16, 32), R("parT"), OP.not_equal)
+        mm(R("P1", 0, 256), R("Perm"), R("m2s"), True, True)
+        own()
+        ts(R("w2"), R("P7", 16, 32), 1.0, OP.add)
+        diff(R("w2"))
+        diff(R("wp"), "P2")
+        eq_s("P2")
+        tt(R("xp2", 128, 256), ind(R("hd"), R("LE", 8, 16)), R("mb2", 128, 256), OP.mult)
+        tt(R("Y1", 256, 512), R("kc"), R("P1", 0, 256), OP.mult)
+        eq()
+        losers(R("P7", 32, 48), R("w2"))
+        mm(R("P3", 0, 256), R("Ib"), R("yy"), False, False)
+        mm(R("P3", 256, 512), R("Ihalf"), R("yy"), False, True)
+        act(R("Um"), R("P3"), bias=MAGIC)
+        act(R("val"), ind(R("Um"), R("lsel")), AF.Abs, bias=-MAGIC)
+        losers(R("P4", 336, 352), R("wp"), False, True)
+        t_to_w(R("P0", 256, 272), "xp2", 16, True, True, 128)
+        tt(R("Y1", 0, 256), R("ke"), R("P1", 0, 256), OP.mult)
+        own()
+        offs(R("so", 48 * t, 48 * t + 16), R("P7", 32, 48), DBC)
+        offs(R("so", 48 * t + 16, 48 * t + 48, 2), R("P7", 32, 48), DBC)
+        send(R("so", 48 * t, 48 * t + 48), "ro", "ao%d" % t)
+        nsent += 2 * neng
+        nx = [16]
+
+        def shape():
+            if nx[0]:
+                nx[0] -= 1
+                put_x(nx[0])
+
+        own()
+        offs(R("oX", 0, 32, 2), R("P4", 336, 352), DXC)
+        own()
+        cp(R("d2k"), R("P0", 256, 272))
+        if not last:
+            y_to_w(R("P7", 112, 128), "Y1", 256, 512, True)
+            mm(R("P7", 96, 112), R("Iopp"), R("d2k"), True, False)
+            mm(R("P7", 96, 112), R("Ih"), R("oneh"), False, False)
+            y_to_w(R("P7", 96, 112), "Y1", 0, 256, False)
+            prep_side(t + 1)
+        while nb[0]:
+            own()
+            shape()
+        if not last:
+            ts(R("W1"), R("P7", 96, 128), 1.0, OP.add)
+            shape()
+            cp(R("lw"), R("P7", 96, 128))
+            own_diff()
+            eq_s()
+            rot("Y1", 256, t + 1, R("cro"))
+            losers(R("P4", 320, 336), WO, True, True)
+        else:
+            ts(R("Gh", 0, 8), R("G16"), 1.0 / 16, OP.mult)
+            ts(R("Gh", 8, 16), R("G16"), 1.0 / 32, OP.mult)
+            cp(R("dh", 0, 16), R("hd", 16, 32))
+            ts(R("dh", 16, 32), R("hd", 16, 32), -0.5, OP.mult)
+            mm(R("P5", 0, 256, p1=8), R("Gh", 0, 8), R("Y1", 256, 512), True, True)
+            mm(R("P5", 256, 512, p1=8), R("Gh", 8, 16), R("Y1", 0, 256), True, False)
+            for h in range(2):
+                mm(R("P5", 256 + 128 * h, 384 + 128 * h, p1=8), R("dh", 16 + 8 * h, 24 + 8 * h), R("Ih"), False, h == 1)
+            for h in range(2):
+                mm(R("P6", 256 + 128 * h, 384 + 128 * h, p1=8), R("dh", 8 * h, 8 * h + 8), R("Ih"), True, True)
+            act(R("o8", 0, 512, p1=8), R("P5", p1=8))
+            act(R("o8", 512, 768, p1=8), R("P6", 256, 512, p1=8))
+        while nx[0] > 16 - XPRE:
+            shape()
+        wait("V", ("ao%d" % t, nin))
+        wait("V", ("ac%d" % t, nin))
+        old_columns("ro", 48 * t, t)
+        for b in range(15, -1, -1):
+            if nx[0]:
+                shape()
+            elif b == 3 and not last:
+                own_offsets()
+            put_b("ro", 48 * t, "rc", 256 * t, b)
+        if last:
+            for b in range(8):
+                act(R("junk"), R("X", 256 * b, 256 * b + 256), acc=R("ysb", b, b + 1))
+
+    tot = 16 * 7
+    dma("Y", "dout", tot, T.yc[:], T.o8[0:8, 0:256], [R("o8")], [])
+    dma("Y", "dout", tot, T.yv[:], T.o8[0:8, 256:512], [R("o8")], [])
+    dma("Y", "dout", tot, T.yd[:], T.o8[0:8, 512:768], [R("o8")], [])
+    dma("Y", "dout", tot, T.ym[:], T.ymb[0:1, 0:48], [R("ymb")], [])
+    dma("Y", "dout", tot, T.yb[0:64, :], T.Bf[0:64, 0:1024], [R("Bf")], [])
+    dma("S", "dout", tot, T.ys[:], T.ysb[:], [R("ysb")], [])
+    dma("S", "dout", tot, T.yb[64:128, :], T.Bf[64:128, 0:1024], [R("Bf")], [])
+    g.wait_ge(T.sem.sent, nsent)
+    for e in ("V", "S", "P", "G"):
+        wait("G", ("s" + e, cnt[e]))
+    g.wait_ge(T.sem.dout, tot)

@@ -3,8 +3,8 @@ from concourse.mybir import AluOpType as OP, ActivationFunctionType as AF
 ST = 6
 H = "float16"
 MAGIC = 12582912.0
-S0 = 64
-XPRE = 10
+S0 = 68
+XPRE = 7
 
 F, B16, I32, U16 = "float32", "bfloat16", "int32", "uint16"
 SCRATCH = {}
@@ -26,7 +26,8 @@ for _n, _c, _d in [
     ("W1", 32, H), ("w2", 16, H), ("wp", 16, H), ("d2k", 16, H), ("hitW", 16, F), ("t1", 16, F), ("t2", 16, F),
     ("EQ", 256, H), ("EQb", 256, B16), ("ab", 256, F), ("L1b", 144, B16), ("I32n", 128, B16), ("oX", 32, U16), ("oO", 48, U16), ("cro", 256, F), ("Ag", 256, F), ("Um", 512, F), ("val", 256, B16),
     ("o8", 768, F), ("ysb", 8, F), ("ymb", 48, F), ("junk", 256, B16),
-    ("sc", 256 * ST, F), ("rc", 256 * ST, F), ("so", 48 * ST, U16), ("ro", 48 * ST, U16),
+    ("sc", 16 * ST, F), ("rc", 16 * ST, F), ("so", 16 * ST, U16), ("ro", 16 * ST, U16),
+    ("cb", 256, F), ("crr", 256, F), ("oR", 32, U16), ("NMb", 272, B16),
     ("row", 272, F), ("row1", 128, F), ("xg", 128, F), ("xa", 272, F), ("xa1", 256, F), ("x7", 128, F),
     ("pi", 8, I32), ("pc", 16, F),
     ("Ib", 128, B16), ("Ih", 128, H), ("If", 128, F), ("Im", 128, F), ("I32b", 128, B16), ("I16b", 128, B16), ("I16s", 128, B16),
@@ -217,7 +218,8 @@ def rank_program(g, core, T, topo):
     def rot(ybuf, lo, t, dst, L="L1", p1=128):
         for a in range(16):
             mm(R("P5", a, 256, 16), Lsl(L, (5 * t + a) % 16, p1), R(ybuf, lo + a, lo + 256, 16, p1=p1), True, True)
-        act(dst, R("P5", 0, 256))
+        if dst is not None:
+            act(dst, R("P5", 0, 256))
 
     def t_to_w(out, xbuf, n, start, stop, lo=0):
         for gg in range(8):
@@ -336,7 +338,7 @@ def rank_program(g, core, T, topo):
         ts(R("Perm"), R("row1"), PCOL, OP.is_equal)
         ts(R("lane"), R("row", 0, 16), 16.0, OP.mult, LANEC, OP.add)
         ts(R("Iopp"), R("Ih"), -1.0 / 1024, OP.mult)
-        mset(R("so"), 0)
+        act(R("NMb"), R("NM"), scale=-4096.0)
 
     prep_side(0)
     nsent = 0
@@ -352,7 +354,8 @@ def rank_program(g, core, T, topo):
             deps("G", [reg], [])
             g.remote_dma(T[rname][:, reg[1]:reg[2]], reg[3], T.sem[sem], T.sem.sent, pid, rid, msk)
 
-        cp(R("Eu"), ind(R("Bi") if t == 0 else R("Bf"), LOPP))
+        for (a, b) in ((0, 6), (6, 8), (8, 16)):
+            cp(R("Eu", 16 * a, 16 * b), ind(R("Bi") if t == 0 else R("Bf"), R("lw", a, b)))
         prep_q()
         s0 = 128 if t == 0 else S0
         act(R("xe", 0, 16 * s0), ind(R("X"), R("Eu", 0, s0)))
@@ -365,6 +368,7 @@ def rank_program(g, core, T, topo):
             consts_s()
         else:
             act(R("Ef"), ind(R("Bf", 0, 1024), LOPP))
+            act(R("cro"), R("P5", 0, 256))
         for h in range(2):
             for k in range(16):
                 o = 2048 * h + 128 * k
@@ -391,12 +395,12 @@ def rank_program(g, core, T, topo):
                     nb[0] -= 1
                     put_b("oO", 0, "cro", 0, nb[0])
 
-        Z, NG = R("P1", 0, 256), R("P1", 256, 512)
-        own()
-        ts(R("Mk"), Z, MAGIC, OP.add, MAGIC, OP.subtract)
+        Hh = lambda n, h, o=0: R(n, o + 128 * h, o + 128 * h + 128)
         own()
         for h in range(2):
-            tt(R("aa", 128 * h, 128 * h + 128), R("Mk", 128 * h, 128 * h + 128), R("P2", 256 * h, 256 * h + 128), OP.subtract)
+            ts(Hh("Mk", h), Hh("P1", h), MAGIC, OP.add, MAGIC, OP.subtract)
+        for h in range(2):
+            tt(Hh("aa", h), Hh("Mk", h), R("P2", 256 * h, 256 * h + 128), OP.subtract)
         for h in range(2):
             act(R("pl", 128 * h, 128 * h + 128), R("P2", 256 * h + 128, 256 * h + 256))
         mm(R("P5", 0, 256), R("Im"), R("Mk"), True, False)
@@ -406,22 +410,26 @@ def rank_program(g, core, T, topo):
         mm(R("P3"), R("Ib"), R("cU"), True, False)
         mm(R("P3", 0, 256), R("Iq"), R("q"), False, False)
         mm(R("P3", 256, 512), R("Ihalf"), R("q"), False, False)
-        tt(NG, R("Mk"), Z, OP.is_le)
+        for h in range(2):
+            tt(Hh("P1", h, 256), Hh("Mk", h), Hh("P1", h), OP.is_le)
+        for h in range(2):
+            tt(Hh("P1", h, 256), Hh("aa", h), Hh("P1", h, 256), OP.mult)
         own()
-        tt(NG, R("aa"), NG, OP.mult)
-        own()
-        tt(R("key"), R("Mk"), NG, OP.add)
-        own()
-        scan(R("ks"), R("RST"), R("key"))
+        for h in range(2):
+            tt(Hh("key", h), Hh("Mk", h), Hh("P1", h, 256), OP.add)
+        for h in range(2):
+            scan(Hh("ks", h), Hh("RST", 0), Hh("key", h))
         act(R("hd", 0, 16), R("ks", 15, 256, 16), AF.Sign, bias=0.5)
         act(R("misT"), R("hd", 0, 16), scale=-0.5, bias=0.5)
-        own()
-        tt(R("oh"), ind(R("ks"), R("LK")), R("key"), OP.is_equal)
-        own()
-        tt(R("sl"), R("oh"), R("P5", 0, 256), OP.mult)
+        for h in range(2):
+            tt(Hh("oh", h), ind(Hh("ks", h), R("LK", 0, 8)), Hh("key", h), OP.is_equal)
+        for h in range(2):
+            tt(Hh("sl", h), Hh("oh", h), Hh("P5", h), OP.mult)
+        for h in range(2):
+            scan(Hh("ss", h), Hh("RST", 0), Hh("sl", h))
         tt(R("xp2", 0, 128), ind(R("hd", 0, 16), R("LE", 0, 8)), R("mb2", 0, 128), OP.mult)
-        mm(R("P4", 256, 272), R("Ih"), R("lane"), True, False)
-        t_to_w(R("P4", 256, 272), "xp2", 16, False, True)
+        mm(R("P1", 0, 16), R("Ih"), R("lane"), True, False)
+        t_to_w(R("P1", 0, 16), "xp2", 16, False, True)
         for j in range(2):
             for h in range(2):
                 mm(R("P6", 256 + 8 * j, 264 + 8 * j), R("one"), R("misT", 8 * h, 8 * h + 8), h == 0, h == 1)
@@ -429,12 +437,11 @@ def rank_program(g, core, T, topo):
         act(R("ymb", t, 48, 6, p1=1), R("A0", 0, 8, p1=1))
         if not last:
             act(R("A1"), R("A0"), scale=0.499, bias=MAGIC)
-        scan(R("ss"), R("RST"), R("sl"))
-        ts(R("hitW"), R("P4", 256, 272), 256.0, OP.is_lt)
         cp(R("Pi"), R("ss", 15, 256, 16))
-        cp(R("lsel"), R("P4", 256, 272))
+        own()
         ts(R("eT"), R("Pi"), 2047, OP.bitwise_and)
         ts(R("pT"), R("Pi"), 11, OP.arith_shift_right, 15, OP.bitwise_and)
+        own()
         tt(R("xp"), ind(R("eT"), R("LE", 0, 8)), R("mb"), OP.mult)
         mm(R("P7", 0, 16), R("Ih"), R("d2k"), True, False)
         t_to_w(R("P7", 0, 16), "xp", 16, False, True)
@@ -447,29 +454,35 @@ def rank_program(g, core, T, topo):
             mm(R("P0", 128 * h, 128 * h + 128), R("op2", 128 * h, 128 * h + 128), R("Ib"), True, True)
         mm(R("P7", 64, 80), R("Ih"), R("oneh"), True, False)
         t_to_w(R("P7", 64, 80), "xp", 16, False, True)
-        own()
+        ts(R("hitW"), R("P1", 0, 16), 256.0, OP.is_lt)
+        cp(R("lsel"), R("P1", 0, 16))
         tt(R("Y2", 0, 256), R("kc"), R("P4", 0, 256), OP.mult)
         act(R("m2s"), R("P0", 0, 256))
-        tt(R("t1"), R("P7", 64, 80), WC, OP.subtract)
+        for a in range(16):
+            mm(R("P5", 0, 16), Lsl("L1", (5 * t + a) % 16), R("Y2", a, 256, 16), a == 0, a == 15)
+        act(R("sc", 16 * t, 16 * t + 16), R("P5", 0, 16))
+        send(R("sc", 16 * t, 16 * t + 16), "rc", "ac%d" % t)
         ts(R("ly"), R("P7", 64, 80), -1.0, OP.add)
+        tt(R("t1"), R("P7", 64, 80), WC, OP.subtract)
         tt(R("Y2", 256, 512), R("ke"), R("P4", 0, 256), OP.mult)
-        rot("Y2", 0, t, R("sc", 256 * t, 256 * t + 256))
-        send(R("sc", 256 * t, 256 * t + 256), "rc", "ac%d" % t)
-        tt(R("t2"), R("t1"), R("hitW"), OP.mult)
         y_to_w(R("P7", 16, 32), "Y2", 256, 512, True)
+        mm(R("P1", 0, 256), R("Perm"), R("m2s"), True, True)
         act(R("yy"), ind(R("X"), R("ly")))
+        tt(R("t2"), R("t1"), R("hitW"), OP.mult)
+        own()
         ts(R("parT"), R("pT"), 1, OP.bitwise_and)
         tt(R("wp"), R("t2"), WC, OP.add)
         tt(R("hd", 16, 32), R("hd", 16, 32), R("parT"), OP.not_equal)
-        mm(R("P1", 0, 256), R("Perm"), R("m2s"), True, True)
         own()
         ts(R("w2"), R("P7", 16, 32), 1.0, OP.add)
         diff(R("w2"))
         diff(R("wp"), "P2")
         eq_s("P2")
         tt(R("xp2", 128, 256), ind(R("hd"), R("LE", 8, 16)), R("mb2", 128, 256), OP.mult)
-        tt(R("Y1", 256, 512), R("kc"), R("P1", 0, 256), OP.mult)
+        own()
         eq()
+        tt(R("Y1", 256, 512), R("kc"), R("P1", 0, 256), OP.mult)
+        own()
         losers(R("P7", 32, 48), R("w2"))
         mm(R("P3", 0, 256), R("Ib"), R("yy"), False, False)
         mm(R("P3", 256, 512), R("Ihalf"), R("yy"), False, True)
@@ -479,9 +492,8 @@ def rank_program(g, core, T, topo):
         t_to_w(R("P0", 256, 272), "xp2", 16, True, True, 128)
         tt(R("Y1", 0, 256), R("ke"), R("P1", 0, 256), OP.mult)
         own()
-        offs(R("so", 48 * t, 48 * t + 16), R("P7", 32, 48), DBC)
-        offs(R("so", 48 * t + 16, 48 * t + 48, 2), R("P7", 32, 48), DBC)
-        send(R("so", 48 * t, 48 * t + 48), "ro", "ao%d" % t)
+        offs(R("so", 16 * t, 16 * t + 16), R("P7", 32, 48), DBC)
+        send(R("so", 16 * t, 16 * t + 16), "ro", "ao%d" % t)
         nsent += 2 * neng
         nx = [16]
 
@@ -490,7 +502,7 @@ def rank_program(g, core, T, topo):
                 nx[0] -= 1
                 put_x(nx[0])
 
-        own()
+        own(3)
         offs(R("oX", 0, 32, 2), R("P4", 336, 352), DXC)
         own()
         cp(R("d2k"), R("P0", 256, 272))
@@ -499,7 +511,11 @@ def rank_program(g, core, T, topo):
             mm(R("P7", 96, 112), R("Iopp"), R("d2k"), True, False)
             mm(R("P7", 96, 112), R("Ih"), R("oneh"), False, False)
             y_to_w(R("P7", 96, 112), "Y1", 0, 256, False)
-            prep_side(t + 1)
+        wait("S", ("ac%d" % t, nin))
+        act(R("cb"), ind(R("rc", 16 * t, 16 * t + 16), R("LT")))
+        mm(R("P5", 256, 512), R("Ib"), R("NMb", (5 * t) % 16, (5 * t) % 16 + 256), True, False)
+        mm(R("P5", 256, 512), R("If"), R("cb"), False, True)
+        act(R("crr"), R("P5", 256, 512), AF.Relu)
         while nb[0]:
             own()
             shape()
@@ -509,8 +525,9 @@ def rank_program(g, core, T, topo):
             cp(R("lw"), R("P7", 96, 128))
             own_diff()
             eq_s()
-            rot("Y1", 256, t + 1, R("cro"))
+            prep_side(t + 1)
             losers(R("P4", 320, 336), WO, True, True)
+            rot("Y1", 256, t + 1, None)
         else:
             ts(R("Gh", 0, 8), R("G16"), 1.0 / 16, OP.mult)
             ts(R("Gh", 8, 16), R("G16"), 1.0 / 32, OP.mult)
@@ -527,14 +544,14 @@ def rank_program(g, core, T, topo):
         while nx[0] > 16 - XPRE:
             shape()
         wait("V", ("ao%d" % t, nin))
-        wait("V", ("ac%d" % t, nin))
-        old_columns("ro", 48 * t, t)
+        cp(R("oR", 0, 32, 2), R("ro", 16 * t, 16 * t + 16))
+        old_columns("ro", 16 * t, t)
         for b in range(15, -1, -1):
             if nx[0]:
                 shape()
-            elif b == 3 and not last:
-                own_offsets()
-            put_b("ro", 48 * t, "rc", 256 * t, b)
+            if b in (1, 2) and not last:
+                offs(R("oO", 0, 16) if b == 1 else R("oO", 16, 48, 2), R("P4", 320, 336), DBC, -2.0)
+            put_b("oR", -16, "crr", 0, b)
         if last:
             for b in range(8):
                 act(R("junk"), R("X", 256 * b, 256 * b + 256), acc=R("ysb", b, b + 1))

@@ -1,9 +1,9 @@
-from concourse.mybir import AluOpType as OP, ActivationFunctionType as AF
+from concourse.mybir import AluOpType as OP, ActivationFunctionType as AF, AxisListType
 
 ST = 6
 H = "float16"
 MAGIC = 12582912.0
-S0 = 68
+S0 = 66
 XPRE = 7
 
 F, B16, I32, U16 = "float32", "bfloat16", "int32", "uint16"
@@ -23,11 +23,11 @@ for _n, _c, _d in [
     ("Pi", 16, I32), ("eT", 16, I32), ("pT", 16, I32), ("parT", 16, I32), ("hd", 32, F), ("misT", 16, B16), ("A0", 16, F), ("A1", 16, F),
     ("dh", 32, H), ("xp", 128, H), ("xp2", 256, H), ("op2", 256, B16), ("m2s", 256, B16), ("Y2", 512, H), ("Y1", 512, H),
     ("lke", 16, U16), ("ly", 16, U16), ("lsel", 16, U16), ("lw", 32, U16),
-    ("W1", 32, H), ("w2", 16, H), ("wp", 16, H), ("d2k", 16, H), ("hitW", 16, F), ("t1", 16, F), ("t2", 16, F),
+    ("W1", 32, H), ("w2", 16, U16), ("wp", 16, H), ("d2k", 16, H), ("hitW", 16, F), ("t1", 16, F), ("t2", 16, F),
     ("EQ", 256, H), ("EQb", 256, B16), ("ab", 256, F), ("L1b", 144, B16), ("I32n", 128, B16), ("oX", 32, U16), ("oO", 48, U16), ("cro", 256, F), ("Ag", 256, F), ("Um", 512, F), ("val", 256, B16),
-    ("o8", 768, F), ("ysb", 8, F), ("ymb", 48, F), ("junk", 256, B16),
-    ("sc", 16 * ST, F), ("rc", 16 * ST, F), ("so", 16 * ST, U16), ("ro", 16 * ST, U16),
-    ("cb", 256, F), ("crr", 256, F), ("oR", 32, U16), ("NMb", 272, B16),
+    ("o8", 768, F), ("ysb", 8, F), ("ymb", 48, F), ("junk", 768, B16),
+    ("sc", 16 * ST, F), ("rc", 16 * ST, F), ("so", 16 * ST, H), ("ro", 16 * ST, H),
+    ("crr", 256, F), ("oR", 32, U16), ("MM", 272, F),
     ("row", 272, F), ("row1", 128, F), ("xg", 128, F), ("xa", 272, F), ("xa1", 256, F), ("x7", 128, F),
     ("pi", 8, I32), ("pc", 16, F),
     ("Ib", 128, B16), ("Ih", 128, H), ("If", 128, F), ("Im", 128, F), ("I32b", 128, B16), ("I16b", 128, B16), ("I16s", 128, B16),
@@ -289,11 +289,16 @@ def rank_program(g, core, T, topo):
     y_to_w(R("P4", 256, 304), "Y8", 0, 768, True, "L8", 8)
     for h in range(2):
         mm(R("P7", 8 * h, 8 * h + 8), R("Y8", 512 + 128 * h, 640 + 128 * h, p1=8), R("Ih", 0, 8, p1=8), True, True)
+    ts(R("IN"), R("P6", 0, 128), 1.0 / 16, OP.mult)
+    cp(R("L1"), R("L1b"))
+    for a in range(1, 5):
+        ts(R("Dm", 128 * a, 128 * a + 128), R("IN"), R("s12", a, a + 1), OP.mult, R("s12", 16 + a, 17 + a), OP.min)
     cp(R("lw"), R("P4", 256, 288))
     ts(R("hd", 16, 32), R("P7", 0, 16), 1.0 / 2048, OP.mult)
+    for a in range(5, 8):
+        ts(R("Dm", 128 * a, 128 * a + 128), R("IN"), R("s12", a, a + 1), OP.mult, R("s12", 16 + a, 17 + a), OP.min)
 
     def consts_a():
-        ts(R("IN"), R("P6", 0, 128), 1.0 / 16, OP.mult)
         ts(R("W1"), R("P4", 256, 288), 1.0, OP.add)
         cp(R("d2k"), R("P4", 288, 304))
         cp(R("Kc", 0, 512), R("Ki"))
@@ -303,9 +308,10 @@ def rank_program(g, core, T, topo):
         for j in range(1, 4):
             dma("Y", "dr1", 48, T.Kc[:, 512 * j:512 * j + 512], T.Kc[:, 0:512], [R("Kc", 0, 512)], [R("Kc", 512 * j, 512 * j + 512)])
         ts(R("mb"), R("x7"), GCOL, OP.is_equal)
+        cp(R("Bf", 0, 1024), R("Bi"))
 
-    def consts_d():
-        for a in range(1, 16):
+    def consts_d(lo=8, hi=16):
+        for a in range(lo, hi):
             ts(R("Dm", 128 * a, 128 * a + 128), R("IN"), R("s12", a, a + 1), OP.mult, R("s12", 16 + a, 17 + a), OP.min)
 
     def consts_s():
@@ -327,18 +333,16 @@ def rank_program(g, core, T, topo):
         act(R("mb2", 128, 256), R("mb"), scale=2048.0)
 
     def consts_b():
-        cp(R("Bf", 0, 1024), R("Bi"))
         ts(R("NM"), R("xa"), ACOL, OP.not_equal)
         ts(R("LK"), R("row", 0, 16), 16.0, OP.mult, 15.0, OP.add)
         ts(R("L2"), R("row", 0, 240), L2C, OP.is_equal)
         ts(R("LE", 0, 8), R("row", 0, 8), HC, OP.add)
         ts(R("LE", 8, 16), R("row", 16, 24), HC, OP.add)
-        cp(R("L1"), R("L1b"))
         ts(R("oneh"), R("row", 0, 16), 0.0, OP.mult, 1.0, OP.add)
         ts(R("Perm"), R("row1"), PCOL, OP.is_equal)
         ts(R("lane"), R("row", 0, 16), 16.0, OP.mult, LANEC, OP.add)
         ts(R("Iopp"), R("Ih"), -1.0 / 1024, OP.mult)
-        act(R("NMb"), R("NM"), scale=-4096.0)
+        act(R("MM"), R("NM"), scale=-1.0, bias=1.0)
 
     prep_side(0)
     nsent = 0
@@ -396,7 +400,6 @@ def rank_program(g, core, T, topo):
                     put_b("oO", 0, "cro", 0, nb[0])
 
         Hh = lambda n, h, o=0: R(n, o + 128 * h, o + 128 * h + 128)
-        own()
         for h in range(2):
             ts(Hh("Mk", h), Hh("P1", h), MAGIC, OP.add, MAGIC, OP.subtract)
         for h in range(2):
@@ -447,54 +450,53 @@ def rank_program(g, core, T, topo):
         t_to_w(R("P7", 0, 16), "xp", 16, False, True)
         tt(R("op2"), ind(R("pT"), R("LT")), R("xa1"), OP.is_equal)
         cp(R("lke"), R("P7", 0, 16))
+        for h in range(2):
+            mm(R("P0", 128 * h, 128 * h + 128), R("op2", 128 * h, 128 * h + 128), R("Ib"), True, True)
+        act(R("m2s"), R("P0", 0, 256))
         act(R("ke"), ind(R("KV"), R("lke")))
         for h in range(2):
             mm(R("P4", 128 * h, 128 * h + 128), R("op2", 128 * h, 128 * h + 128), R("Ib"), True, True)
-        for h in range(2):
-            mm(R("P0", 128 * h, 128 * h + 128), R("op2", 128 * h, 128 * h + 128), R("Ib"), True, True)
-        mm(R("P7", 64, 80), R("Ih"), R("oneh"), True, False)
-        t_to_w(R("P7", 64, 80), "xp", 16, False, True)
+        mm(R("P6", 272, 288), R("Ih"), R("oneh"), True, False)
+        t_to_w(R("P6", 272, 288), "xp", 16, False, True)
         ts(R("hitW"), R("P1", 0, 16), 256.0, OP.is_lt)
         cp(R("lsel"), R("P1", 0, 16))
-        tt(R("Y2", 0, 256), R("kc"), R("P4", 0, 256), OP.mult)
-        act(R("m2s"), R("P0", 0, 256))
-        for a in range(16):
-            mm(R("P5", 0, 16), Lsl("L1", (5 * t + a) % 16), R("Y2", a, 256, 16), a == 0, a == 15)
-        act(R("sc", 16 * t, 16 * t + 16), R("P5", 0, 16))
-        send(R("sc", 16 * t, 16 * t + 16), "rc", "ac%d" % t)
-        ts(R("ly"), R("P7", 64, 80), -1.0, OP.add)
-        tt(R("t1"), R("P7", 64, 80), WC, OP.subtract)
-        tt(R("Y2", 256, 512), R("ke"), R("P4", 0, 256), OP.mult)
-        y_to_w(R("P7", 16, 32), "Y2", 256, 512, True)
-        mm(R("P1", 0, 256), R("Perm"), R("m2s"), True, True)
-        act(R("yy"), ind(R("X"), R("ly")))
-        tt(R("t2"), R("t1"), R("hitW"), OP.mult)
         own()
         ts(R("parT"), R("pT"), 1, OP.bitwise_and)
-        tt(R("wp"), R("t2"), WC, OP.add)
+        own()
+        tt(R("Y2", 256, 512), ind(R("KV"), R("lke")), R("m2s"), OP.mult)
+        y_to_w(R("P7", 16, 32), "Y2", 256, 512, True)
+        own()
+        tt(R("Y2", 0, 256), R("kc"), R("P4", 0, 256), OP.mult)
+        for a in range(16):
+            mm(R("P5", 0, 16), Lsl("L1", (5 * t + a) % 16), R("Y2", a, 256, 16), a == 0, a == 15)
+        mm(R("P1", 0, 256), R("Perm"), R("m2s"), True, True)
+        ts(R("ly"), R("P6", 272, 288), -1.0, OP.add)
+        tt(R("t1"), R("P6", 272, 288), WC, OP.subtract)
+        act(R("yy"), ind(R("X"), R("ly")))
+        own()
+        ts(R("so", 16 * t, 16 * t + 16), R("P7", 16, 32), 1.0, OP.add)
+        send(R("so", 16 * t, 16 * t + 16), "ro", "ao%d" % t)
+        act(R("sc", 16 * t, 16 * t + 16), R("P5", 0, 16))
+        send(R("sc", 16 * t, 16 * t + 16), "rc", "ac%d" % t)
+        nsent += 2 * neng
+        tt(R("t2"), R("t1"), R("hitW"), OP.mult)
         tt(R("hd", 16, 32), R("hd", 16, 32), R("parT"), OP.not_equal)
         own()
-        ts(R("w2"), R("P7", 16, 32), 1.0, OP.add)
-        diff(R("w2"))
+        tt(R("wp"), R("t2"), WC, OP.add)
         diff(R("wp"), "P2")
         eq_s("P2")
         tt(R("xp2", 128, 256), ind(R("hd"), R("LE", 8, 16)), R("mb2", 128, 256), OP.mult)
         own()
-        eq()
-        tt(R("Y1", 256, 512), R("kc"), R("P1", 0, 256), OP.mult)
-        own()
-        losers(R("P7", 32, 48), R("w2"))
         mm(R("P3", 0, 256), R("Ib"), R("yy"), False, False)
         mm(R("P3", 256, 512), R("Ihalf"), R("yy"), False, True)
         act(R("Um"), R("P3"), bias=MAGIC)
         act(R("val"), ind(R("Um"), R("lsel")), AF.Abs, bias=-MAGIC)
-        losers(R("P4", 336, 352), R("wp"), False, True)
         t_to_w(R("P0", 256, 272), "xp2", 16, True, True, 128)
+        tt(R("Y1", 256, 512), R("kc"), R("P1", 0, 256), OP.mult)
+        own()
         tt(R("Y1", 0, 256), R("ke"), R("P1", 0, 256), OP.mult)
         own()
-        offs(R("so", 16 * t, 16 * t + 16), R("P7", 32, 48), DBC)
-        send(R("so", 16 * t, 16 * t + 16), "ro", "ao%d" % t)
-        nsent += 2 * neng
+        losers(R("P4", 336, 352), R("wp"), False, True)
         nx = [16]
 
         def shape():
@@ -502,33 +504,43 @@ def rank_program(g, core, T, topo):
                 nx[0] -= 1
                 put_x(nx[0])
 
-        own(3)
-        offs(R("oX", 0, 32, 2), R("P4", 336, 352), DXC)
-        own()
         cp(R("d2k"), R("P0", 256, 272))
+
         if not last:
             y_to_w(R("P7", 112, 128), "Y1", 256, 512, True)
             mm(R("P7", 96, 112), R("Iopp"), R("d2k"), True, False)
             mm(R("P7", 96, 112), R("Ih"), R("oneh"), False, False)
             y_to_w(R("P7", 96, 112), "Y1", 0, 256, False)
-        wait("S", ("ac%d" % t, nin))
-        act(R("cb"), ind(R("rc", 16 * t, 16 * t + 16), R("LT")))
-        mm(R("P5", 256, 512), R("Ib"), R("NMb", (5 * t) % 16, (5 * t) % 16 + 256), True, False)
-        mm(R("P5", 256, 512), R("If"), R("cb"), False, True)
-        act(R("crr"), R("P5", 256, 512), AF.Relu)
-        while nb[0]:
-            own()
-            shape()
+        own(nb[0] - 1)
+        offs(R("oX", 0, 32, 2), R("P4", 336, 352), DXC)
+        own()
+        RO = R("ro", 16 * t, 16 * t + 16)
+        wait("P", ("ao%d" % t, nin))
+        for a in range(1, 16):
+            bank = "P6" if a < 9 else "P0"
+            mm(R(bank, 16 * a, 16 * a + 16), R("Dm", 128 * a, 128 * a + 128), RO, True, True)
+        shape()
+        wait("V", ("ao%d" % t, nin))
+        ts(R("w2"), RO, -1.0, OP.add)
+        shape()
+        old_columns("w2", 0, t)
+        ts(R("EQ", 16, 144), R("P6", 16, 144), 0.0, OP.is_equal, 4096.0, OP.mult)
+        ts(R("EQ", 144, 256), R("P0", 144, 256), 0.0, OP.is_equal, 4096.0, OP.mult)
+        losers(R("P4", 352, 368), RO)
+        shape()
+        wait("V", ("ac%d" % t, nin))
+        tt(R("crr"), ind(R("rc", 16 * t, 16 * t + 16), R("LT")), R("MM", (5 * t) % 16, (5 * t) % 16 + 256), OP.mult)
+        shape()
+        offs(R("oR", 0, 32, 2), R("P4", 352, 368), DBC)
         if not last:
             ts(R("W1"), R("P7", 96, 128), 1.0, OP.add)
-            shape()
-            cp(R("lw"), R("P7", 96, 128))
             own_diff()
             eq_s()
-            prep_side(t + 1)
             losers(R("P4", 320, 336), WO, True, True)
+            prep_side(t + 1)
             rot("Y1", 256, t + 1, None)
-        else:
+
+        def final_lanes():
             ts(R("Gh", 0, 8), R("G16"), 1.0 / 16, OP.mult)
             ts(R("Gh", 8, 16), R("G16"), 1.0 / 32, OP.mult)
             cp(R("dh", 0, 16), R("hd", 16, 32))
@@ -539,31 +551,33 @@ def rank_program(g, core, T, topo):
                 mm(R("P5", 256 + 128 * h, 384 + 128 * h, p1=8), R("dh", 16 + 8 * h, 24 + 8 * h), R("Ih"), False, h == 1)
             for h in range(2):
                 mm(R("P6", 256 + 128 * h, 384 + 128 * h, p1=8), R("dh", 8 * h, 8 * h + 8), R("Ih"), True, True)
+            for b in range(5, 8):
+                act(R("junk", 256 * (b - 5), 256 * (b - 4)), R("X", 256 * b, 256 * b + 256), acc=R("ysb", b, b + 1))
             act(R("o8", 0, 512, p1=8), R("P5", p1=8))
             act(R("o8", 512, 768, p1=8), R("P6", 256, 512, p1=8))
-        while nx[0] > 16 - XPRE:
-            shape()
-        wait("V", ("ao%d" % t, nin))
-        cp(R("oR", 0, 32, 2), R("ro", 16 * t, 16 * t + 16))
-        old_columns("ro", 16 * t, t)
         for b in range(15, -1, -1):
-            if nx[0]:
+            if b == 14 and not last:
+                cp(R("lw"), R("P7", 96, 128))
+            if nx[0] and b != 15:
                 shape()
+            if b == 2 and last:
+                final_lanes()
             if b in (1, 2) and not last:
                 offs(R("oO", 0, 16) if b == 1 else R("oO", 16, 48, 2), R("P4", 320, 336), DBC, -2.0)
             put_b("oR", -16, "crr", 0, b)
         if last:
-            for b in range(8):
-                act(R("junk"), R("X", 256 * b, 256 * b + 256), acc=R("ysb", b, b + 1))
+            for b in range(5):
+                o, i = R("ysb", b, b + 1), R("X", 256 * b, 256 * b + 256)
+                emit("V", [i], [o], lambda: g.vector.tensor_reduce(o[3], i[3], AxisListType.X, OP.add))
 
     tot = 16 * 7
-    dma("Y", "dout", tot, T.yc[:], T.o8[0:8, 0:256], [R("o8")], [])
-    dma("Y", "dout", tot, T.yv[:], T.o8[0:8, 256:512], [R("o8")], [])
-    dma("Y", "dout", tot, T.yd[:], T.o8[0:8, 512:768], [R("o8")], [])
     dma("Y", "dout", tot, T.ym[:], T.ymb[0:1, 0:48], [R("ymb")], [])
     dma("Y", "dout", tot, T.yb[0:64, :], T.Bf[0:64, 0:1024], [R("Bf")], [])
+    dma("Y", "dout", tot, T.yb[64:128, :], T.Bf[64:128, 0:1024], [R("Bf")], [])
+    dma("S", "dout", tot, T.yc[:], T.o8[0:8, 0:256], [R("o8")], [])
+    dma("S", "dout", tot, T.yv[:], T.o8[0:8, 256:512], [R("o8")], [])
+    dma("S", "dout", tot, T.yd[:], T.o8[0:8, 512:768], [R("o8")], [])
     dma("S", "dout", tot, T.ys[:], T.ysb[:], [R("ysb")], [])
-    dma("S", "dout", tot, T.yb[64:128, :], T.Bf[64:128, 0:1024], [R("Bf")], [])
     g.wait_ge(T.sem.sent, nsent)
     for e in ("V", "S", "P", "G"):
         wait("G", ("s" + e, cnt[e]))

@@ -3,8 +3,21 @@ from concourse.mybir import AluOpType as OP, ActivationFunctionType as AF, AxisL
 ST = 6
 H = "float16"
 MAGIC = 12582912.0
+MAGIC2 = MAGIC * 2048
+OFF = 25.0
 S0 = 66
-XPRE = 7
+S00 = 60
+GD = 8
+S1 = 114
+PART = 64
+LATE = 3
+YS = 5
+LATE0 = 6
+XPER = (1, 1, 1, 1, 1, 1, 1, 1)
+LWB = 4
+DX = 9
+XPRE = 2
+EARLY = (9, 11, 13, 15)
 
 F, B16, I32, U16 = "float32", "bfloat16", "int32", "uint16"
 SCRATCH = {}
@@ -15,27 +28,27 @@ def _sb(name, cols, dtype):
 
 
 for _n, _c, _d in [
-    ("X", 2064, B16), ("Bi", 1024, I32), ("Bf", 1040, F), ("Ki", 512, I32), ("Kw", 512, I32), ("Kc", 2048, F), ("KV", 4096, F),
-    ("l8", 768, I32), ("v8", 256, F), ("Y8", 768, H),
-    ("Eu", 256, U16), ("Ef", 256, F), ("xe", 4096, B16), ("tt", 4096, F), ("q", 256, B16), ("yy", 256, B16),
-    ("kc", 256, F), ("ke", 256, F), ("sx", 256, B16), ("ax", 512, B16),
-    ("Mk", 256, F), ("aa", 256, F), ("pl", 256, F), ("key", 256, F), ("ks", 256, F), ("oh", 256, F), ("sl", 256, F), ("ss", 256, F),
-    ("Pi", 16, I32), ("eT", 16, I32), ("pT", 16, I32), ("parT", 16, I32), ("hd", 32, F), ("misT", 16, B16), ("A0", 16, F), ("A1", 16, F),
-    ("dh", 32, H), ("xp", 128, H), ("xp2", 256, H), ("op2", 256, B16), ("m2s", 256, B16), ("Y2", 512, H), ("Y1", 512, H),
-    ("lke", 16, U16), ("ly", 16, U16), ("lsel", 16, U16), ("lw", 32, U16),
-    ("W1", 32, H), ("w2", 16, U16), ("wp", 16, H), ("d2k", 16, H), ("hitW", 16, F), ("t1", 16, F), ("t2", 16, F),
-    ("EQ", 256, H), ("EQb", 256, B16), ("ab", 256, F), ("L1b", 144, B16), ("I32n", 128, B16), ("oX", 32, U16), ("oO", 48, U16), ("cro", 256, F), ("Ag", 256, F), ("Um", 512, F), ("val", 256, B16),
-    ("o8", 768, F), ("ysb", 8, F), ("ymb", 48, F), ("junk", 768, B16),
+    ("X", 2064, B16), ("Bi", 1024, I32), ("Bf", 1056, F), ("Bc", 2048, H), ("wf", 16, F), ("rep", 128, H), ("LR", 8, U16), ("Ki", 512, I32), ("Kw", 512, I32), ("Kc", 2048, F), ("KV", 2048, F),
+    ("l8", 768, I32), ("Y8", 768, H), ("vv", 16, H),
+    ("Eu", 256, U16), ("E16", 256, H), ("nAg", 256, H), ("newc", 256, F), ("xe", 4096, B16), ("tt", 4096, F), ("q", 256, B16), ("yy", 256, B16),
+    ("kc", 256, F), ("ke", 256, F), ("sx", 256, B16),
+    ("r1", 128, F), ("r2", 256, F), ("f2", 256, F), ("key", 256, F), ("ks", 256, F), ("oh", 256, F), ("sl", 256, F), ("ss", 264, F),
+    ("Pi", 16, I32), ("pT", 16, I32), ("parT", 16, I32), ("hd", 40, F), ("misT", 16, B16), ("ac", 8, F),
+    ("dh", 16, H), ("xp", 128, H), ("xs", 128, H), ("xd", 128, H), ("op2", 256, B16), ("m2s", 256, B16), ("Y2", 512, H), ("Y1", 512, H),
+    ("ly", 16, U16), ("lsel", 16, U16), ("lw", 48, U16),
+    ("W1", 32, H), ("w2", 16, U16), ("wp", 16, H), ("dW", 16, H), ("hitW", 16, F), ("t1", 16, F), ("t2", 16, F),
+    ("EQ", 384, H), ("EQs", 256, H), ("ab", 256, F), ("oX", 32, U16), ("oO", 32, U16), ("Ag", 256, F), ("Um", 512, F), ("val", 256, B16),
+    ("o8", 768, F), ("ysb", 8, F), ("ymb", 8, F),
     ("sc", 16 * ST, F), ("rc", 16 * ST, F), ("so", 16 * ST, H), ("ro", 16 * ST, H),
     ("crr", 256, F), ("oR", 32, U16), ("MM", 272, F),
-    ("row", 272, F), ("row1", 128, F), ("xg", 128, F), ("xa", 272, F), ("xa1", 256, F), ("x7", 128, F),
-    ("pi", 8, I32), ("pc", 16, F),
-    ("Ib", 128, B16), ("Ih", 128, H), ("If", 128, F), ("Im", 128, F), ("I32b", 128, B16), ("I16b", 128, B16), ("I16s", 128, B16),
-    ("Iq", 128, B16), ("Ihalf", 128, B16), ("Iopp", 128, H), ("Iown", 128, H), ("Perm", 128, B16),
-    ("Gq", 256, B16), ("G16", 8, F), ("Gx", 16, B16), ("Gh", 16, H), ("IN", 128, H), ("Dm", 2048, H), ("s12", 32, F),
-    ("L1", 144, H), ("L2", 240, H), ("L8", 144, H), ("NM", 272, F), ("RST", 256, F), ("cZ", 256, B16), ("cS", 512, B16), ("cU", 512, B16),
-    ("mb", 128, F), ("mb2", 256, F), ("lane", 16, H), ("one", 128, B16), ("oneh", 16, H),
-    ("LK", 16, U16), ("LT", 16, U16), ("LE", 16, U16),
+    ("row", 272, F), ("row1", 128, F), ("xg", 128, F), ("xa", 272, F), ("xa1", 128, F),
+    ("pi", 8, I32), ("pc", 24, F),
+    ("Ib", 128, B16), ("Ih", 128, H), ("nIh", 128, H), ("hIh", 128, H), ("pIh", 128, H), ("I2n", 128, H), ("LS", 8, U16), ("Isx", 128, B16),
+    ("Iq", 128, B16), ("Ihalf", 128, B16), ("Perm", 128, B16), ("BM", 128, H),
+    ("Gq", 256, B16), ("G8", 8, F), ("G32", 32, F), ("Gx", 16, B16), ("Gh", 16, H), ("IN", 128, H), ("Dm", 2048, H), ("Dg", 2048, H), ("s12", 32, F),
+    ("L1", 144, H), ("L2", 240, H), ("L8", 144, H), ("NM", 272, F), ("RST", 128, F), ("CT", 512, H), ("on16", 128, H), ("c24", 256, H), ("m8", 128, H), ("cU", 512, B16),
+    ("lane", 16, H), ("one", 16, B16),
+    ("LK", 8, U16), ("LT", 16, U16), ("LE", 16, U16),
 ]:
     _sb(_n, _c, _d)
 for _b in range(8):
@@ -130,13 +143,17 @@ def rank_program(g, core, T, topo):
         emit("V", [], [o], lambda: g.vector.memset(o[3], v))
 
     def act(o, i, fn=AF.Identity, bias=0.0, scale=1.0, acc=None):
+        w, r0, oa = outs(o)
         r, ia = sides(i)
-        rs = [bias] if isinstance(bias, tuple) else []
+        rs = [s for s in (bias, scale) if isinstance(s, tuple)]
         ba = bias[3] if isinstance(bias, tuple) else bias
-        if acc is None:
-            emit("S", r + rs, [o], lambda: g.scalar.activation(o[3], ia, fn, bias=ba, scale=scale))
+        sa = scale[3] if isinstance(scale, tuple) else scale
+        if fn == AF.Silu:
+            emit("S", r + r0, w, lambda: g.scalar.activation(oa, ia, fn))
+        elif acc is None:
+            emit("S", r + rs, w, lambda: g.scalar.activation(oa, ia, fn, bias=ba, scale=sa))
         else:
-            emit("S", r + rs, [o, acc], lambda: g.scalar.activation(o[3], ia, fn, bias=ba, scale=scale, accum_out=acc[3]))
+            emit("S", r + rs, w + [acc], lambda: g.scalar.activation(oa, ia, fn, bias=ba, scale=sa, accum_out=acc[3]))
 
     def mm(o, l, r, start, stop):
         emit("P", [l, r], [o], lambda: g.tensor.matmul(o[3], l[3], r[3], start, stop))
@@ -152,12 +169,15 @@ def rank_program(g, core, T, topo):
         Q[e].dma_start(out_ap, in_ap).then_inc(T.sem[sem], 16)
         note("D", (sem, total), reads, writes)
 
-    PCOL, ACOL, GCOL, PARC, HC, L1C, L2C, L8C, LANEC, DXC, DBC, FLIPC = [R("pc", j, j + 1) for j in range(12)]
-    LOPP, LCW, WO, WC = R("lw", 0, 16), R("lw", 16, 32), R("W1", 0, 16), R("W1", 16, 32)
+    PCOL, ACOL, GCOL, HC, B7, L1C, L2C, L8C, LANEC, DXC, DBC, MC, E0C, E1C = [R("pc", j, j + 1) for j in range(14)]
+    S0C, S1C, DB2, R2C = [R("pc", j, j + 1) for j in range(16, 20)]
+    C1, C2 = R("pc", 14, 15, p1=16), R("pc", 15, 16, p1=16)
+    LOPP, LCW, LOWN, WO, WC = R("lw", 0, 16), R("lw", 16, 32), R("lw", 32, 48), R("W1", 0, 16), R("W1", 16, 32)
+    PH = ("P1", "P2")
 
     dma("Y", "dl", 48, T.l8[0:8, 0:256], T.lv[:], [], [R("l8", 0, 256)])
-    dma("S", "dl", 48, T.l8[0:8, 256:512], T.lc[:], [], [R("l8", 256, 512)])
-    dma("Y", "dl", 48, T.l8[0:8, 512:768], T.ld[:], [], [R("l8", 512, 768)])
+    dma("S", "dl", 48, T.l8[0:8, 256:512], T.ld[:], [], [R("l8", 256, 512)])
+    dma("Y", "dl", 48, T.l8[0:8, 512:768], T.lc[:], [], [R("l8", 512, 768)])
     dma("S", "db", 16, T.Bi[:], T.bnd[:], [], [R("Bi")])
     dma("Y", "dx", 16, T.X[:, 0:2048], T.x[:], [], [R("X", 0, 2048)])
     dma("S", "dk", 16, T.Ki[:], T.kt[:], [], [R("Ki")])
@@ -167,105 +187,99 @@ def rank_program(g, core, T, topo):
     iota(R("row", 0, 144), [[1, 144]])
     iota(R("xg"), [[1, 8], [0, 16]])
     iota(R("xa"), [[0, 17], [1, 16]])
-    iota(R("row", 144, 272), [[1, 128]], 144)
-    iota(R("x7"), [[0, 16], [1, 8]])
-    iota(R("row1"), [[2, 64], [-1, 2]], 1)
-    iota(R("xa1"), [[0, 16], [2, 8], [-1, 2]], 1)
-    iota(R("one"), [[0, 128]], 1)
-    iota(R("cU"), [[0, 512]], 1)
+    mset(R("ab", 0, 32), OFF)
+    act(R("Bf", 1024, 1056), R("ab", 0, 32), AF.Silu)
+    mset(R("on16", p1=16), 1.0)
+    mset(R("c24", p1=16), (OFF - 1.0) / 16)
     ts(pi(1), pi(0), 15, OP.bitwise_and)
     ts(pi(2), pi(0), 4, OP.arith_shift_right)
-    ts(pi(3), pi(0), 1, OP.bitwise_and)
-    ts(pi(4), pi(0), 8, OP.bitwise_and)
+    ts(pi(3), pi(0), 8, OP.bitwise_and)
+    ts(pi(4), pi(0), 7, OP.bitwise_and)
     mset(R("X", 2048, 2064), 0.0)
     cp(R("pc", 0, 5), R("pi", 0, 5))
-    mset(R("Bf", 1024, 1040), 0.0)
+    mset(R("hd", 32, 40), 0.0)
     ts(L8C, PCOL, 16.0, OP.mult, 15.0, OP.add)
-    act(L1C, GCOL, scale=16.0, bias=15.0)
-    act(L2C, ACOL, bias=112.0)
-    act(LANEC, ACOL, bias=128.0)
-    act(DXC, ACOL, bias=2048.0)
-    act(DBC, ACOL, bias=1024.0)
-    act(FLIPC, PARC, scale=-2.0, bias=1.0)
-    ts(R("Ib"), R("row", 0, 128), PCOL, OP.is_equal)
+    ts(R("Ih"), R("row", 0, 128), PCOL, OP.is_equal)
     ts(R("L8", 0, 144), R("row", 0, 144), L8C, OP.is_equal)
-    cp(R("Ih"), R("Ib"))
-    cp(R("LT"), R("row", 0, 16))
-    ts(R("Gq", 0, 128), R("xg"), GCOL, OP.is_equal, 16.0, OP.mult)
-    ts(R("G16"), R("row", 0, 8), GCOL, OP.is_equal, 16.0, OP.mult)
-    ts(R("L1b"), R("row", 0, 144), L1C, OP.is_equal)
-    ts(R("s12", 0, 16), R("row", 0, 16), ACOL, OP.is_ge)
     ts(R("s12", 16, 32), R("row", 0, 16), ACOL, OP.is_equal)
-    act(R("I32n"), R("Ib"), scale=-32.0)
-    act(R("I16s"), R("Ib"), scale=-128.0)
-    act(R("cZ"), R("xa", 0, 256), scale=-1.0, bias=15.0)
-    for h in range(2):
-        act(R("cS", 256 * h, 256 * h + 128), R("xa", 0, 128), scale=-1.0, bias=31.0)
-        act(R("cS", 256 * h + 128, 256 * h + 256), R("xa", 0, 128), scale=-256.0, bias=3840.0)
-    act(R("Gq", 128, 256), R("Gq", 0, 128), scale=128.0)
-    act(R("Gx", 0, 8), R("G16"))
-    act(R("Gx", 8, 16), R("G16"), scale=128.0)
-    mm(R("P6", 0, 128), R("Ib"), R("Gq", 0, 128), True, False)
-    mm(R("P6", 0, 128), R("Ib"), R("I32n"), False, True)
+    ts(R("G8"), R("row", 0, 8), GCOL, OP.is_equal)
+    ts(R("BM"), R("xg"), GCOL, OP.is_equal)
+    ts(C1, R("pc", 0, 1, p1=16), 8.0, OP.is_equal, -2048.0, OP.mult)
+    ts(C2, R("pc", 0, 1, p1=16), 8.0, OP.is_equal, -1.0 / 4096, OP.mult)
+    ts(R("hIh"), R("Ih"), -0.5, OP.mult)
+    ts(R("pIh"), R("Ih"), 0.5, OP.mult)
+    ts(R("I2n"), R("Ih"), -2.0, OP.mult)
+    cp(R("LT"), R("row", 0, 16))
+    ts(L1C, GCOL, 16.0, OP.mult, 15.0, OP.add)
+    ts(R("s12", 0, 16), R("row", 0, 16), ACOL, OP.is_ge)
+    ts(R("CT", 384, 512, p1=16), R("on16", p1=16), 2040.0, OP.mult, C2, OP.mult)
+
+    for r in range(GD, 16):
+        o = R("Dg", 128 * r, 128 * r + 128)
+        emit("G", [R("Ih")], [o], lambda: g.affine_select(o[3], T.Ih[:, :], [[0, 8], [1, 16]], OP.is_equal, 0.0, -r, 0))
+    iota(R("row", 144, 272), [[1, 128]], 144)
+    iota(R("xa1"), [[0, 8], [2, 8], [-1, 2]], 1)
+    iota(R("row1"), [[2, 64], [-1, 2]], 1)
+    for a in range(16):
+        o = R("Bc", 128 * a, 128 * a + 128)
+        emit("G", [R("BM")], [o], lambda: g.affine_select(o[3], T.BM[:, :], [[-16, 8], [0, 16]], OP.is_equal, 0.0, -a, 1))
 
     def Lsl(name, a, p1=128):
         return R(name, 15 - a, 143 - a, p1=p1)
 
-    def y_to_w(out, ybuf, lo, hi, start, L="L1", p1=128):
+    def y_to_w(out, ybuf, lo, hi, start, stop=True, L="L1", p1=128):
         for a in range(16):
-            mm(out, Lsl(L, a, p1), R(ybuf, lo + a, hi, 16, p1=p1), start and a == 0, a == 15)
+            mm(out, Lsl(L, a, p1), R(ybuf, lo + a, hi, 16, p1=p1), start and a == 0, stop and a == 15)
 
-    def rot(ybuf, lo, t, dst, L="L1", p1=128):
+    def rot(ybuf, lo, t, L="L1", p1=128):
+        mm(R("P5", 0, 256), R("on16", p1=16), R("c24", p1=16), True, False)
         for a in range(16):
-            mm(R("P5", a, 256, 16), Lsl(L, (5 * t + a) % 16, p1), R(ybuf, lo + a, lo + 256, 16, p1=p1), True, True)
-        if dst is not None:
-            act(dst, R("P5", 0, 256))
+            mm(R("P5", a, 256, 16), Lsl(L, (5 * t + a) % 16, p1), R(ybuf, lo + a, lo + 256, 16, p1=p1), False, False)
 
-    def t_to_w(out, xbuf, n, start, stop, lo=0):
+    def old_rows(t):
+        mm(R("P5", 0, 256), R("nIh"), R("nAg"), False, False)
+        for a in range(16):
+            r = (5 * t + a) % 16
+            mm(R("P5", a, 256, 16), R("Dg", 128 * r, 128 * r + 128), R("nAg", a, 256, 16), False, a == 15)
+
+    def t_to_w(out, xbuf, start, stop=True):
         for gg in range(8):
-            mm(out, R("L2", 112 - 16 * gg, 240 - 16 * gg), R(xbuf, lo + n * gg, lo + n * gg + n), start and gg == 0, stop and gg == 7)
+            mm(out, R("L2", 112 - 16 * gg, 240 - 16 * gg), R(xbuf, 16 * gg, 16 * gg + 16), start and gg == 0, stop and gg == 7)
 
-    def diff(w, bank="P6"):
-        for a in range(1, 16):
+    def diff(w, bank="P6", lo=1, hi=16):
+        for a in range(lo, hi):
             mm(R(bank, 16 * a, 16 * a + 16), R("Dm", 128 * a, 128 * a + 128), w, True, True)
-
-    def eq():
-        ts(R("EQ", 16, 256), R("P6", 16, 256), 0.0, OP.is_equal, 4096.0, OP.mult)
 
     def eq_s(bank="P6"):
         act(R("ab", 16, 256), R(bank, 16, 256), AF.Abs)
-        act(R("EQb", 16, 256), R("ab", 16, 256), AF.Relu, scale=-4096.0, bias=4096.0)
+        act(R("EQs", 16, 256), R("ab", 16, 256), AF.Relu, scale=-4096.0, bias=4096.0)
 
-    def losers(out, w, own=False, sc=False):
+    def losers(out, w, buf, sign=None, stop=True):
         mm(out, R("Ih"), w, True, False)
-        if own:
-            mm(out, R("Iown"), R("d2k"), False, False)
+        if sign:
+            mm(out, R("Ih"), R(sign), False, False)
         for a in range(1, 16):
-            mm(out, Lsl("L1b" if sc else "L1", a), R("EQb" if sc else "EQ", 16 * a, 16 * a + 16), False, a == 15)
+            mm(out, Lsl("L1", a), R(buf, 16 * a, 16 * a + 16), False, stop and a == 15)
 
-    def offs(o, src, dummy, sub=-1.0):
-        ts(o, src, sub, OP.add, dummy, OP.min)
+    def offs(o, src, dummy):
+        ts(o, src, -1.0, OP.add, dummy, OP.min)
 
-    def old_columns(off, o, t):
-        s = (5 * t) % 16
-        tt(R("Ag"), ind(R("Bf"), R(off, o, o + 16)), R("NM", s, s + 256), OP.mult)
+    def put_r(b):
+        tt(ind(R("Bf"), R("oR", 2 * b, 2 * b + 2)), R("Ag", 32 * b, 32 * b + 32), R("crr", 32 * b, 32 * b + 32), OP.add)
 
-    def put_b(off, o, crot, c, b):
-        tt(ind(R("Bf"), R(off, o + 16 + 2 * b, o + 17 + 2 * b)), R("Ag", 16 * b, 16 * b + 16), R(crot, c + 16 * b, c + 16 * b + 16), OP.add)
+    def put_o(b):
+        act(ind(R("Bf"), R("oO", 2 * b, 2 * b + 1)), R("newc", 16 * b, 16 * b + 16), AF.Silu)
 
     def put_x(b):
         cp(ind(R("X"), R("oX", 2 * b, 2 * b + 1)), R("val", 16 * b, 16 * b + 16))
 
-    def prep_side(t):
+    def side():
         act(R("sx"), ind(R("hd", 16, 32), R("LT")), scale=1.0 / 256, bias=-1.0 / 512)
-        mm(R("P1", 0, 256), R("Ib"), R("cZ"), True, False)
-        mm(R("P1", 0, 256), R("I16s"), R("sx"), False, False)
-        if t > 0:
-            act(R("ax", 0, 256), ind(R("A0"), R("LT")))
-            act(R("ax", 256, 512), ind(R("A1"), R("LT")), bias=-MAGIC)
-            mm(R("P1", 0, 256), R("I32b"), R("ax", 0, 256), False, False)
-            mm(R("P1", 0, 256), R("I16b"), R("ax", 256, 512), False, False)
-        mm(R("P2"), R("Ib"), R("cS"), True, False)
+
+    def open_sums():
+        for h in range(2):
+            mm(R(PH[h]), R("on16", p1=16), R("CT", p1=16), True, False)
+            mm(R(PH[h], 0, 128), R("Isx"), R("sx", 128 * h, 128 * h + 128), False, False)
 
     def prep_q():
         act(R("q"), ind(R("X"), LCW))
@@ -273,78 +287,108 @@ def rank_program(g, core, T, topo):
         for h in range(2):
             mm(R("P0", 128 * h, 128 * h + 128), R("sx", 128 * h, 128 * h + 128), R("Ib"), False, h == 1)
         for h in range(2):
-            mm(R("P2", 256 * h, 256 * h + 256), R("q", 128 * h, 128 * h + 128), R("Gq"), False, False)
+            mm(R(PH[h], 256, 512), R("q", 128 * h, 128 * h + 128), R("Gq"), False, False)
 
-    def own_diff():
-        diff(WO)
+    def next_lists():
+        act(R("W1"), R("P7", 96, 128))
+        mm(R("P7", 128, 144), R("Ih"), WO, True, False)
+        mm(R("P7", 128, 144), R("Ih"), R("dW"), False, True)
 
-    def own_offsets():
-        offs(R("oO", 0, 16), R("P4", 320, 336), DBC, -2.0)
-        offs(R("oO", 16, 48, 2), R("P4", 320, 336), DBC, -2.0)
-
-    ts(R("v8", p1=8), R("l8", 0, 256, p1=8), 2.0, OP.mult, 1.0, OP.add)
-    cp(R("Y8", 256, 512, p1=8), R("l8", 256, 512, p1=8))
-    tt(R("Y8", 0, 256, p1=8), R("v8", p1=8), R("l8", 512, 768, p1=8), OP.subtract)
-    ts(R("Y8", 512, 768, p1=8), R("l8", 512, 768, p1=8), 2048.0, OP.mult)
-    y_to_w(R("P4", 256, 304), "Y8", 0, 768, True, "L8", 8)
+    cp(R("Y8", 0, 512, p1=8), R("l8", 0, 512, p1=8))
+    act(R("Y8", 512, 768, p1=8), R("l8", 512, 768, p1=8), bias=1.0)
+    y_to_w(R("P7", 80, 128), "Y8", 0, 768, True, True, "L8", 8)
     for h in range(2):
-        mm(R("P7", 8 * h, 8 * h + 8), R("Y8", 512 + 128 * h, 640 + 128 * h, p1=8), R("Ih", 0, 8, p1=8), True, True)
-    ts(R("IN"), R("P6", 0, 128), 1.0 / 16, OP.mult)
-    cp(R("L1"), R("L1b"))
-    for a in range(1, 5):
-        ts(R("Dm", 128 * a, 128 * a + 128), R("IN"), R("s12", a, a + 1), OP.mult, R("s12", 16 + a, 17 + a), OP.min)
-    cp(R("lw"), R("P4", 256, 288))
-    ts(R("hd", 16, 32), R("P7", 0, 16), 1.0 / 2048, OP.mult)
-    for a in range(5, 8):
-        ts(R("Dm", 128 * a, 128 * a + 128), R("IN"), R("s12", a, a + 1), OP.mult, R("s12", 16 + a, 17 + a), OP.min)
+        mm(R("P6", 304 + 8 * h, 312 + 8 * h), R("Y8", 256 + 128 * h, 384 + 128 * h, p1=8), R("Ih", 0, 8, p1=8), True, True)
+    act(R("Ib"), R("Ih"))
+    act(R("Isx"), R("Ih"), scale=-262144.0)
+    act(R("Gq", 0, 128), R("BM"), scale=-1.0 / 256)
+    act(R("Gq", 128, 256), R("BM"), scale=1.0 / 4096)
+    for j, s in enumerate((32768.0, 1.0 / 256, 1.0 / 128, -1.0 / 2048)):
+        act(R("G32", 8 * j, 8 * j + 8), R("G8"), scale=s)
+    act(R("Gx", 0, 8), R("G8"), scale=-1.0 / 256)
+    act(R("Gx", 8, 16), R("G8"), scale=1.0 / 4096)
+    act(R("nIh"), R("Ih"), scale=-1.0)
+    for r in range(GD):
+        act(R("Dg", 128 * r, 128 * r + 128), R("Ih"), scale=R("s12", 16 + r, 17 + r))
+    rot("Y8", 512, 0, "L8", 8)
 
-    def consts_a():
-        ts(R("W1"), R("P4", 256, 288), 1.0, OP.add)
-        cp(R("d2k"), R("P4", 288, 304))
-        cp(R("Kc", 0, 512), R("Ki"))
-        ts(R("Kw"), R("Ki"), 511, OP.bitwise_and)
-        ts(R("Iown"), R("Ih"), 1.0 / 1024, OP.mult)
-        ts(R("KV", 0, 512), R("Kw"), 2.0, OP.mult, PARC, OP.add)
-        for j in range(1, 4):
-            dma("Y", "dr1", 48, T.Kc[:, 512 * j:512 * j + 512], T.Kc[:, 0:512], [R("Kc", 0, 512)], [R("Kc", 512 * j, 512 * j + 512)])
-        ts(R("mb"), R("x7"), GCOL, OP.is_equal)
-        cp(R("Bf", 0, 1024), R("Bi"))
-
-    def consts_d(lo=8, hi=16):
+    def consts_d(lo, hi):
         for a in range(lo, hi):
             ts(R("Dm", 128 * a, 128 * a + 128), R("IN"), R("s12", a, a + 1), OP.mult, R("s12", 16 + a, 17 + a), OP.min)
 
-    def consts_s():
-        act(R("KV", 2048, 2560), R("KV", 0, 512), bias=FLIPC)
-        for s in (0, 2048):
+    tt(R("IN"), R("BM"), R("I2n"), OP.add)
+    xa16 = R("xa", 0, 128, p1=16)
+    ts(R("CT", 0, 128, p1=16), xa16, -15.015625, OP.add, C1, OP.mult)
+    ts(R("CT", 128, 256, p1=16), xa16, -15.0, OP.add, C2, OP.mult)
+    ts(R("CT", 256, 384, p1=16), xa16, 2.0, OP.add, C2, OP.mult)
+    consts_d(1, 4)
+    ts(R("vv"), R("P7", 80, 96), 2.0, OP.mult, 1.5, OP.add)
+    ts(R("dW"), R("P7", 96, 112), 2.0, OP.mult, -1.0, OP.add)
+    cp(R("hd", 16, 32), R("P6", 304, 320))
+    for (lo, I) in ((96, "hIh"), (128, "pIh")):
+        mm(R("P7", lo, lo + 16), R("Ih"), R("vv"), True, False)
+        mm(R("P7", lo, lo + 16), R(I), R("dW"), False, True)
+    side()
+    consts_d(4, 10)
+    ts(R("lw"), R("P7", 96, 144), -1.0, OP.add)
+    act(R("W1"), R("P7", 96, 128))
+    open_sums()
+
+    def tables(own):
+        act(R("KV", 0, 512), R("Kw"), scale=2.0, bias=1.5)
+        own(1)
+        act(R("Kc", 0, 512), R("Ki"), bias=1.0)
+        own(1)
+        for s, sem in (("KV", "dr2"), ("Kc", "dr1")):
             for j in range(1, 4):
-                dma("Y", "dr2", 96, T.KV[:, s + 512 * j:s + 512 * j + 512], T.KV[:, s:s + 512],
-                    [R("KV", s, s + 512)], [R("KV", s + 512 * j, s + 512 * j + 512)])
-        act(R("RST"), R("xa", 0, 256), scale=1.0e8, bias=-5.0e7)
-        act(R("Im"), R("Ib"), scale=-256.0)
-        act(R("Iq"), R("Ib"), scale=-0.25)
-        act(R("Ihalf"), R("Ib"), scale=0.5)
-        act(R("cU", 0, 256), R("cU", 0, 256), scale=0.375)
-        act(R("cU", 256, 512), R("cU", 256, 512), scale=-0.25)
-        act(R("I32b"), R("Ib"), scale=1.0 / 32)
-        act(R("I16b"), R("Ib"), scale=-1.0 / 16)
-        act(R("If"), R("Ib"))
-        act(R("mb2", 0, 128), R("mb"), scale=-128.0)
-        act(R("mb2", 128, 256), R("mb"), scale=2048.0)
+                dma("Y", sem, 48, T[s][:, 512 * j:512 * j + 512], T[s][:, 0:512], [R(s, 0, 512)], [R(s, 512 * j, 512 * j + 512)])
 
-    def consts_b():
-        ts(R("NM"), R("xa"), ACOL, OP.not_equal)
-        ts(R("LK"), R("row", 0, 16), 16.0, OP.mult, 15.0, OP.add)
+    def consts_choice(own):
+        own(1)
+        act(R("RST"), R("xa", 0, 128), scale=1.0e8, bias=-5.0e7)
+        act(L2C, ACOL, bias=112.0)
+        own(1)
+        act(LANEC, ACOL, bias=128.0)
+        act(S0C, HC, scale=16.0, bias=-241.0)
+        act(E0C, HC, bias=-32.0)
+        own(1)
+        ts(MC, B7, GCOL, OP.is_equal)
+        ts(R("LK"), R("row", 0, 8), 16.0, OP.mult, 15.0, OP.add)
+        mset(R("ss", 256, 264), 0.0)
+        mset(R("one"), 1.0)
+        act(E0C, E0C, scale=MC, bias=32.0)
+        act(S0C, S0C, scale=MC, bias=256.0)
+        act(S1C, MC, scale=16.0)
+        own(1)
+        act(E1C, MC, scale=16.0, bias=E0C)
+        act(R("lane"), R("row", 0, 16), scale=16.0, bias=LANEC)
+        own(1)
+
+    def consts_lists():
         ts(R("L2"), R("row", 0, 240), L2C, OP.is_equal)
-        ts(R("LE", 0, 8), R("row", 0, 8), HC, OP.add)
-        ts(R("LE", 8, 16), R("row", 16, 24), HC, OP.add)
-        ts(R("oneh"), R("row", 0, 16), 0.0, OP.mult, 1.0, OP.add)
-        ts(R("Perm"), R("row1"), PCOL, OP.is_equal)
-        ts(R("lane"), R("row", 0, 16), 16.0, OP.mult, LANEC, OP.add)
-        ts(R("Iopp"), R("Ih"), -1.0 / 1024, OP.mult)
-        act(R("MM"), R("NM"), scale=-1.0, bias=1.0)
+        ts(R("LE", 0, 8), R("row", 0, 8), MC, OP.mult, E0C, OP.add)
+        ts(R("LE", 8, 16), R("row", 0, 8), MC, OP.mult, E1C, OP.add)
+        ts(R("LS"), R("row", 0, 8), S1C, OP.mult, S0C, OP.add)
 
-    prep_side(0)
+    def consts_late():
+        ts(R("Iq"), R("Ib"), -0.25, OP.mult)
+        ts(R("Ihalf"), R("Ib"), 0.5, OP.mult)
+        mset(R("cU", 0, 256), 0.375)
+        mset(R("cU", 256, 512), -0.25)
+        ts(R("Perm"), R("row1"), PCOL, OP.is_equal)
+        ts(R("NM"), R("xa"), ACOL, OP.not_equal)
+        ts(R("MM"), R("xa"), ACOL, OP.is_equal)
+        ts(R("m8", p1=8), R("xg", p1=8), R("pc", 0, 1, p1=8), OP.is_equal, 64.0, OP.mult)
+        ts(DXC, ACOL, 2048.0, OP.add)
+        ts(DB2, ACOL, 1040.0, OP.add)
+        act(R2C, B7, scale=2.0)
+        ts(R("LR"), R("row", 0, 8), 0.0, OP.mult, R2C, OP.add)
+
+    def open_values():
+        mm(R("P3"), R("Ib"), R("cU"), True, False)
+        mm(R("P3", 0, 256), R("Iq"), R("q"), False, False)
+        mm(R("P3", 256, 512), R("Ihalf"), R("q"), False, False)
+
     nsent = 0
     for t in range(ST):
         last = t == ST - 1
@@ -358,225 +402,262 @@ def rank_program(g, core, T, topo):
             deps("G", [reg], [])
             g.remote_dma(T[rname][:, reg[1]:reg[2]], reg[3], T.sem[sem], T.sem.sent, pid, rid, msk)
 
-        for (a, b) in ((0, 6), (6, 8), (8, 16)):
-            cp(R("Eu", 16 * a, 16 * b), ind(R("Bi") if t == 0 else R("Bf"), R("lw", a, b)))
-        prep_q()
-        s0 = 128 if t == 0 else S0
+        BT, boff = (R("Bi"), 0.0) if t == 0 else (R("Bf"), OFF)
+        ts(R("Eu", 0, 128), ind(BT, R("lw", 0, 8)), 0.25 - boff, OP.add)
+        s0, s1 = (S00, 128) if t == 0 else (S0, S1)
+        if t == 0:
+            prep_q()
+        act(R("nAg"), ind(BT, LOWN), scale=-1.0, bias=boff - 1.0)
         act(R("xe", 0, 16 * s0), ind(R("X"), R("Eu", 0, s0)))
+        ts(R("Eu", 128, 256), ind(BT, R("lw", 8, 16)), 0.25 - boff, OP.add)
         if t == 0:
-            consts_a()
-        else:
-            cp(R("xe", 16 * s0, 2048), ind(R("X"), R("Eu", s0, 128)))
-        act(R("xe", 2048, 4096), ind(R("X"), R("Eu", 128, 256)))
+            consts_d(10, 16)
+            ts(R("L1"), R("row", 0, 144), L1C, OP.is_equal)
+            diff(WO)
+        cp(R("xe", 16 * s0, 2048), ind(R("X"), R("Eu", s0, 128)))
+        old_rows(t)
+        act(R("xe", 2048, 2048 + 16 * s1), ind(R("X"), R("Eu", 128, 128 + s1)))
+        act(R("E16"), ind(BT, LOPP), bias=1.0 - boff)
         if t == 0:
-            consts_s()
-        else:
-            act(R("Ef"), ind(R("Bf", 0, 1024), LOPP))
-            act(R("cro"), R("P5", 0, 256))
-        for h in range(2):
-            for k in range(16):
-                o = 2048 * h + 128 * k
-                tt(R("tt", o, o + 128), R("xe", 2048 * h + k, 2048 * h + 2048, 16), R("P0", 128 * h, 128 * h + 128), OP.min)
-                mm(R("P2", 256 * h + k, 256 * h + 256, 16), R("xe", 2048 * h + k, 2048 * h + 2048, 16), R("Gx"), False, h == 1 and k == 15)
-                mm(R("P1", 128 * h + k, 128 * h + 128, 16), R("tt", o, o + 128), R("G16"), False, h == 1 and k == 15)
-            if t == 0 and h == 0:
-                consts_d()
-                rot("Y8", 256, 0, R("cro"), "L8", 8)
-                own_diff()
-                eq_s()
-        if t == 0:
-            losers(R("P4", 320, 336), WO, True, True)
-            consts_b()
-            cp(R("Ef"), R("Eu"))
-            own_offsets()
-        act(R("kc"), ind(R("Kc"), LCW))
-        old_columns("oO", 0, t)
+            ts(R("EQs", 16, 256), R("P6", 16, 256), 0.0, OP.is_equal, 4096.0, OP.mult)
+            ts(DBC, ACOL, 1024.0, OP.add)
+            act(R("Bf", 0, 1024), R("Bi"), bias=OFF)
+        act(R("newc"), R("P5", 0, 256))
+
+        kind = lambda h, j, lo, hi: R(PH[h], 128 * j + lo, 128 * j + hi)
+        sb = lambda n, h, lo, hi: R(n, 128 * h + lo, 128 * h + hi)
+        stage = [
+            lambda h, lo, hi: ts(sb("r2", h, lo, hi), kind(h, 0, lo, hi), MAGIC2, OP.add, MAGIC2, OP.subtract),
+            lambda h, lo, hi: tt(sb("f2", h, lo, hi), sb("r2", h, lo, hi), kind(h, 0, lo, hi), OP.subtract),
+            lambda h, lo, hi: tt(sb("r2", h, lo, hi), sb("f2", h, lo, hi), kind(h, 1, lo, hi), OP.min),
+            lambda h, lo, hi: tt(sb("key", h, lo, hi), sb("r2", h, lo, hi), kind(h, 2, lo, hi), OP.max),
+            lambda h, lo, hi: scan(sb("ks", h, lo, hi), R("RST", lo, hi), sb("key", h, lo, hi)),
+            lambda h, lo, hi: tt(sb("oh", h, lo, hi), ind(sb("ks", h, lo, hi), R("LK", 0, (hi - lo) // 16)), sb("key", h, lo, hi), OP.is_equal),
+            lambda h, lo, hi: tt(sb("sl", h, lo, hi), sb("oh", h, lo, hi), kind(h, 3, lo, hi), OP.mult),
+            lambda h, lo, hi: scan(sb("ss", h, lo, hi), R("RST", lo, hi), sb("sl", h, lo, hi)),
+        ]
+
+        def sum_x(h, k):
+            mm(R(PH[h], 256 + k, 512, 16), R("xe", 2048 * h + k, 2048 * h + 2048, 16), R("Gx"), False, False)
+
+        def rows(h, k):
+            o = 2048 * h + 128 * k
+            tt(R("tt", o, o + 128), R("xe", 2048 * h + k, 2048 * h + 2048, 16), R("P0", 128 * h, 128 * h + 128), OP.min)
+            if h == 1:
+                sum_x(h, k)
+            mm(R(PH[h], k, 512, 16), R("tt", o, o + 128), R("G32"), False, False)
+            if h == 1 and k in (1, 15):
+                hh = k // 15
+                mm(R(PH[hh], 384, 512), R("E16", 128 * hh, 128 * hh + 128), R("Ih"), False, True)
+            if h == 1 and k == 1:
+                own(2)
+                act(R("r1"), R("P1", 0, 128), bias=MAGIC2)
+                own(1)
+                act(R("r2", 0, 128), R("r1"), bias=-MAGIC2)
+
         nb = [16]
 
         def own(n=1):
-            for _ in range(n):
-                if nb[0]:
-                    nb[0] -= 1
-                    put_b("oO", 0, "cro", 0, nb[0])
+            for _ in range(min(n, nb[0])):
+                nb[0] -= 1
+                put_o(nb[0])
 
-        Hh = lambda n, h, o=0: R(n, o + 128 * h, o + 128 * h + 128)
+        for k in range(16):
+            sum_x(0, k)
+        if t == 0:
+            losers(R("P4", 320, 336), WO, "EQs", "dW")
+        for k in range(16):
+            rows(0, k)
+        if t == 0:
+            ts(R("Kw"), R("Ki"), 511, OP.bitwise_and)
+        else:
+            cp(R("xe", 2048 + 16 * s1, 4096), ind(R("X"), R("Eu", 128 + s1, 256)))
+        for k in range(16):
+            if k == 0:
+                offs(R("oO", 0, 32, 2), R("P4", 320, 336), DBC)
+            rows(1, k)
+            if k == 1 and t == 0:
+                consts_choice(own)
+                tables(own)
+            if k in EARLY:
+                stage[1 + EARLY.index(k)](0, 0, 128)
+        if t == 0:
+            consts_lists()
+            own(nb[0] - LATE0)
+        else:
+            own(1)
+            act(R("kc"), ind(R("Kc"), LCW))
+            own(nb[0] - LATE)
+            open_values()
+        mm(R("P6", 256, 272), R("Ih"), R("lane"), True, False)
+
+        rest = list(range(1 + len(EARLY), 8))
+        for j in range(8):
+            if rest:
+                stage[rest.pop(0)](0, 0, 128)
+            for lo in range(0, 128, PART):
+                stage[j](1, lo, lo + PART)
+            if j == 4:
+                act(R("hd", 0, 16), R("ks", 15, 256, 16), AF.Sign, bias=0.75 / 4096)
+                act(R("xs"), ind(R("hd"), R("LE", 0, 8)), scale=-128.0)
+                act(R("misT"), R("hd", 0, 16), scale=-0.5, bias=0.5)
+                own(2)
+        t_to_w(R("P6", 256, 272), "xs", False)
+        PA = R("P4", 304, 305, p1=8)
         for h in range(2):
-            ts(Hh("Mk", h), Hh("P1", h), MAGIC, OP.add, MAGIC, OP.subtract)
-        for h in range(2):
-            tt(Hh("aa", h), Hh("Mk", h), R("P2", 256 * h, 256 * h + 128), OP.subtract)
-        for h in range(2):
-            act(R("pl", 128 * h, 128 * h + 128), R("P2", 256 * h + 128, 256 * h + 256))
-        mm(R("P5", 0, 256), R("Im"), R("Mk"), True, False)
-        for h in range(2):
-            mm(R("P5", 128 * h, 128 * h + 128), R("Ef", 128 * h, 128 * h + 128), R("If"), False, False)
-        mm(R("P5", 0, 256), R("If"), R("pl"), False, True)
-        mm(R("P3"), R("Ib"), R("cU"), True, False)
-        mm(R("P3", 0, 256), R("Iq"), R("q"), False, False)
-        mm(R("P3", 256, 512), R("Ihalf"), R("q"), False, False)
-        for h in range(2):
-            tt(Hh("P1", h, 256), Hh("Mk", h), Hh("P1", h), OP.is_le)
-        for h in range(2):
-            tt(Hh("P1", h, 256), Hh("aa", h), Hh("P1", h, 256), OP.mult)
-        own()
-        for h in range(2):
-            tt(Hh("key", h), Hh("Mk", h), Hh("P1", h, 256), OP.add)
-        for h in range(2):
-            scan(Hh("ks", h), Hh("RST", 0), Hh("key", h))
-        act(R("hd", 0, 16), R("ks", 15, 256, 16), AF.Sign, bias=0.5)
-        act(R("misT"), R("hd", 0, 16), scale=-0.5, bias=0.5)
-        for h in range(2):
-            tt(Hh("oh", h), ind(Hh("ks", h), R("LK", 0, 8)), Hh("key", h), OP.is_equal)
-        for h in range(2):
-            tt(Hh("sl", h), Hh("oh", h), Hh("P5", h), OP.mult)
-        for h in range(2):
-            scan(Hh("ss", h), Hh("RST", 0), Hh("sl", h))
-        tt(R("xp2", 0, 128), ind(R("hd", 0, 16), R("LE", 0, 8)), R("mb2", 0, 128), OP.mult)
-        mm(R("P1", 0, 16), R("Ih"), R("lane"), True, False)
-        t_to_w(R("P1", 0, 16), "xp2", 16, False, True)
-        for j in range(2):
-            for h in range(2):
-                mm(R("P6", 256 + 8 * j, 264 + 8 * j), R("one"), R("misT", 8 * h, 8 * h + 8), h == 0, h == 1)
-        act(R("A0"), R("P6", 256, 272))
-        act(R("ymb", t, 48, 6, p1=1), R("A0", 0, 8, p1=1))
-        if not last:
-            act(R("A1"), R("A0"), scale=0.499, bias=MAGIC)
-        cp(R("Pi"), R("ss", 15, 256, 16))
-        own()
-        ts(R("eT"), R("Pi"), 2047, OP.bitwise_and)
-        ts(R("pT"), R("Pi"), 11, OP.arith_shift_right, 15, OP.bitwise_and)
-        own()
-        tt(R("xp"), ind(R("eT"), R("LE", 0, 8)), R("mb"), OP.mult)
-        mm(R("P7", 0, 16), R("Ih"), R("d2k"), True, False)
-        t_to_w(R("P7", 0, 16), "xp", 16, False, True)
-        tt(R("op2"), ind(R("pT"), R("LT")), R("xa1"), OP.is_equal)
-        cp(R("lke"), R("P7", 0, 16))
-        for h in range(2):
-            mm(R("P0", 128 * h, 128 * h + 128), R("op2", 128 * h, 128 * h + 128), R("Ib"), True, True)
-        act(R("m2s"), R("P0", 0, 256))
-        act(R("ke"), ind(R("KV"), R("lke")))
-        for h in range(2):
-            mm(R("P4", 128 * h, 128 * h + 128), R("op2", 128 * h, 128 * h + 128), R("Ib"), True, True)
-        mm(R("P6", 272, 288), R("Ih"), R("oneh"), True, False)
-        t_to_w(R("P6", 272, 288), "xp", 16, False, True)
-        ts(R("hitW"), R("P1", 0, 16), 256.0, OP.is_lt)
-        cp(R("lsel"), R("P1", 0, 16))
-        own()
-        ts(R("parT"), R("pT"), 1, OP.bitwise_and)
-        own()
-        tt(R("Y2", 256, 512), ind(R("KV"), R("lke")), R("m2s"), OP.mult)
-        y_to_w(R("P7", 16, 32), "Y2", 256, 512, True)
-        own()
-        tt(R("Y2", 0, 256), R("kc"), R("P4", 0, 256), OP.mult)
-        for a in range(16):
-            mm(R("P5", 0, 16), Lsl("L1", (5 * t + a) % 16), R("Y2", a, 256, 16), a == 0, a == 15)
-        mm(R("P1", 0, 256), R("Perm"), R("m2s"), True, True)
-        ts(R("ly"), R("P6", 272, 288), -1.0, OP.add)
-        tt(R("t1"), R("P6", 272, 288), WC, OP.subtract)
-        act(R("yy"), ind(R("X"), R("ly")))
-        own()
-        ts(R("so", 16 * t, 16 * t + 16), R("P7", 16, 32), 1.0, OP.add)
-        send(R("so", 16 * t, 16 * t + 16), "ro", "ao%d" % t)
-        act(R("sc", 16 * t, 16 * t + 16), R("P5", 0, 16))
-        send(R("sc", 16 * t, 16 * t + 16), "rc", "ac%d" % t)
-        nsent += 2 * neng
-        tt(R("t2"), R("t1"), R("hitW"), OP.mult)
+            mm(PA, R("misT", 8 * h, 8 * h + 8), R("one", 0, 1), h == 0, h == 1)
+        act(R("hitW"), R("P6", 256, 272), AF.Sign, scale=-1.0, bias=255.5)
+        act(R("ymb", t, t + 1, p1=8), PA)
+        act(R("hitW"), R("hitW"), AF.Relu)
+        ts(R("Pi"), R("ss", 15, 256, 16), 4096.0, OP.mult, 2040.125, OP.add)
+        ts(R("xp"), ind(R("ss"), R("LS")), MAGIC, OP.add, MAGIC, OP.subtract)
+        t_to_w(R("P7", 0, 16), "xp", True)
+        ts(R("parT"), R("Pi"), 1, OP.bitwise_and)
+        ts(R("pT"), R("Pi"), 15, OP.bitwise_and)
         tt(R("hd", 16, 32), R("hd", 16, 32), R("parT"), OP.not_equal)
-        own()
+        act(R("xd"), ind(R("hd"), R("LE", 8, 16)))
+        tt(R("op2", 0, 128), ind(R("pT"), R("LT", 0, 8)), R("xa1", 0, 128), OP.is_equal)
+        ts(R("ly"), R("P7", 0, 16), -1.0, OP.add)
+        act(R("ke"), ind(R("KV"), R("ly")))
+        own(1)
+        tt(R("t1"), R("P7", 0, 16), WC, OP.subtract)
+        tt(R("op2", 128, 256), ind(R("pT"), R("LT", 8, 16)), R("xa1", 0, 128), OP.is_equal)
+        for bank in ("P0", "P4"):
+            for h in range(2):
+                mm(R(bank, 128 * h, 128 * h + 128), R("op2", 128 * h, 128 * h + 128), R("Ib"), True, True)
+            if bank == "P0":
+                t_to_w(R("P6", 288, 304), "xd", True)
+        act(R("dW"), R("P6", 288, 304), scale=2.0, bias=-1.0)
+        if t == 0:
+            act(R("kc"), ind(R("Kc"), LCW))
+        act(R("yy"), ind(R("X"), R("ly")))
+        tt(R("t2"), R("t1"), R("hitW"), OP.mult)
         tt(R("wp"), R("t2"), WC, OP.add)
-        diff(R("wp"), "P2")
-        eq_s("P2")
-        tt(R("xp2", 128, 256), ind(R("hd"), R("LE", 8, 16)), R("mb2", 128, 256), OP.mult)
-        own()
+        tt(R("Y2", 256, 512), R("ke"), R("P0", 0, 256), OP.mult)
+        diff(R("wp"), "P2", 1, DX)
+        y_to_w(R("P7", 16, 32), "Y2", 256, 512, True, False)
+        mm(R("P7", 16, 32), R("hIh"), R("dW"), False, True)
+        tt(R("Y2", 0, 256), R("kc"), R("P0", 0, 256), OP.mult)
+        cp(R("lsel"), R("P6", 256, 272))
+        own(1)
+        act(R("m2s"), R("P4", 0, 256))
+        own(16)
+        if last:
+            ts(R("Bf", 0, 512), R("Bf", 0, 512), MAGIC - OFF, OP.add, MAGIC, OP.subtract)
+        cp(R("so", 16 * t, 16 * t + 16), R("P7", 16, 32))
+        send(R("so", 16 * t, 16 * t + 16), "ro", "ao%d" % t)
+        if last:
+            ts(R("Bf", 512, 1024), R("Bf", 512, 1024), MAGIC - OFF, OP.add, MAGIC, OP.subtract)
+        if t == 0:
+            consts_late()
+            open_values()
+        diff(R("wp"), "P2", DX, 16)
         mm(R("P3", 0, 256), R("Ib"), R("yy"), False, False)
         mm(R("P3", 256, 512), R("Ihalf"), R("yy"), False, True)
+        mm(R("P1", 0, 256), R("Perm"), R("m2s"), True, True)
+        for a in range(16):
+            mm(R("P5", 256, 272), Lsl("L1", (5 * t + a) % 16), R("Y2", a, 256, 16), a == 0, a == 15)
         act(R("Um"), R("P3"), bias=MAGIC)
-        act(R("val"), ind(R("Um"), R("lsel")), AF.Abs, bias=-MAGIC)
-        t_to_w(R("P0", 256, 272), "xp2", 16, True, True, 128)
-        tt(R("Y1", 256, 512), R("kc"), R("P1", 0, 256), OP.mult)
-        own()
+        ts(R("EQ", 16, 256), R("P2", 16, 256), 0.0, OP.is_equal, 4096.0, OP.mult)
+        losers(R("P2", 256, 272), R("wp"), "EQ")
         tt(R("Y1", 0, 256), R("ke"), R("P1", 0, 256), OP.mult)
-        own()
-        losers(R("P4", 336, 352), R("wp"), False, True)
+        ts(R("sc", 16 * t, 16 * t + 16), R("P5", 256, 272), -1.0 if last else OFF - 1.0, OP.add)
+        send(R("sc", 16 * t, 16 * t + 16), "rc", "ac%d" % t)
+        nsent += 2 * neng
+        act(R("val"), ind(R("Um"), R("lsel")), AF.Abs, bias=-MAGIC)
+        tt(R("Y1", 256, 512), R("kc"), R("P1", 0, 256), OP.mult)
+        if not last:
+            y_to_w(R("P7", 96, 112), "Y1", 0, 256, True, False)
+            mm(R("P7", 96, 112), R("hIh"), R("dW"), False, True)
+        offs(R("oX", 0, 32, 2), R("P2", 256, 272), DXC)
         nx = [16]
 
-        def shape():
-            if nx[0]:
+        def shape(n=1):
+            for _ in range(min(n, nx[0])):
                 nx[0] -= 1
                 put_x(nx[0])
 
-        cp(R("d2k"), R("P0", 256, 272))
-
-        if not last:
-            y_to_w(R("P7", 112, 128), "Y1", 256, 512, True)
-            mm(R("P7", 96, 112), R("Iopp"), R("d2k"), True, False)
-            mm(R("P7", 96, 112), R("Ih"), R("oneh"), False, False)
-            y_to_w(R("P7", 96, 112), "Y1", 0, 256, False)
-        own(nb[0] - 1)
-        offs(R("oX", 0, 32, 2), R("P4", 336, 352), DXC)
-        own()
         RO = R("ro", 16 * t, 16 * t + 16)
         wait("P", ("ao%d" % t, nin))
         for a in range(1, 16):
             bank = "P6" if a < 9 else "P0"
             mm(R(bank, 16 * a, 16 * a + 16), R("Dm", 128 * a, 128 * a + 128), RO, True, True)
-        shape()
+        shape(XPRE)
         wait("V", ("ao%d" % t, nin))
+        cp(R("wf"), RO)
         ts(R("w2"), RO, -1.0, OP.add)
         shape()
-        old_columns("w2", 0, t)
+        cp(R("rep"), ind(R("wf"), R("LR")))
+        shape()
+        mm(R("P1", 256, 384), R("nIh"), R("rep"), True, False)
+        for a in range(16):
+            mm(R("P1", 256 + 8 * a, 264 + 8 * a), R("Bc", 128 * a, 128 * a + 128), R("ro", 16 * t + 1, 16 * t + 16, 2), False, a == 15)
+        s = (5 * t) % 16
         ts(R("EQ", 16, 144), R("P6", 16, 144), 0.0, OP.is_equal, 4096.0, OP.mult)
         ts(R("EQ", 144, 256), R("P0", 144, 256), 0.0, OP.is_equal, 4096.0, OP.mult)
-        losers(R("P4", 352, 368), RO)
+        shape()
+        losers(R("P4", 352, 368), RO, "EQ", stop=False)
+        tt(R("Ag"), ind(R("Bf"), R("w2")), R("NM", s, s + 256), OP.mult)
+        shape()
+        ts(R("EQ", 256, 384), R("P1", 256, 384), 0.0, OP.is_equal, 4096.0, OP.mult)
+        for a in range(16):
+            mm(R("P4", 353, 368, 2), Lsl("L1", a), R("EQ", 256 + 8 * a, 264 + 8 * a), False, a == 15)
         shape()
         wait("V", ("ac%d" % t, nin))
-        tt(R("crr"), ind(R("rc", 16 * t, 16 * t + 16), R("LT")), R("MM", (5 * t) % 16, (5 * t) % 16 + 256), OP.mult)
+        tt(R("crr"), ind(R("rc", 16 * t, 16 * t + 16), R("LT")), R("MM", s, s + 256), OP.mult)
+        shape(2)
+        offs(R("oR", 0, 16, 2), R("P4", 352, 368, 2), DBC)
+        hist["oR"], even = [], hist["oR"]
+        offs(R("oR", 1, 16, 2), R("P4", 353, 368, 2), DB2)
+        hist["oR"] += even
         shape()
-        offs(R("oR", 0, 32, 2), R("P4", 352, 368), DBC)
         if not last:
-            ts(R("W1"), R("P7", 96, 128), 1.0, OP.add)
-            own_diff()
+            y_to_w(R("P7", 112, 128), "Y1", 256, 512, True)
+            A1, A2, A3 = [R("ac", j, j + 1, p1=8) for j in range(3)]
+            act(A1, R("ymb", t, t + 1, p1=8), scale=0.499, bias=MAGIC)
+            act(A2, A1, scale=-2.0, bias=2 * MAGIC)
+            act(A3, A2, bias=R("ymb", t, t + 1, p1=8))
+            act(R("CT", 0, 128, p1=8), R("m8", p1=8), scale=A3)
+            side()
+            next_lists()
+            diff(WO)
+            open_sums()
             eq_s()
-            losers(R("P4", 320, 336), WO, True, True)
-            prep_side(t + 1)
-            rot("Y1", 256, t + 1, None)
-
-        def final_lanes():
-            ts(R("Gh", 0, 8), R("G16"), 1.0 / 16, OP.mult)
-            ts(R("Gh", 8, 16), R("G16"), 1.0 / 32, OP.mult)
-            cp(R("dh", 0, 16), R("hd", 16, 32))
-            ts(R("dh", 16, 32), R("hd", 16, 32), -0.5, OP.mult)
+            rot("Y1", 256, t + 1)
+            losers(R("P4", 320, 336), WO, "EQs", "dW")
+        else:
+            act(R("Gh", 0, 8), R("G8"))
+            act(R("Gh", 8, 16), R("G8"), scale=0.5)
+            act(R("dh"), R("hd", 16, 32))
             mm(R("P5", 0, 256, p1=8), R("Gh", 0, 8), R("Y1", 256, 512), True, True)
-            mm(R("P5", 256, 512, p1=8), R("Gh", 8, 16), R("Y1", 0, 256), True, False)
+            mm(R("P5", 256, 512, p1=8), R("Gh", 8, 16), R("Y1", 0, 256), True, True)
             for h in range(2):
-                mm(R("P5", 256 + 128 * h, 384 + 128 * h, p1=8), R("dh", 16 + 8 * h, 24 + 8 * h), R("Ih"), False, h == 1)
-            for h in range(2):
-                mm(R("P6", 256 + 128 * h, 384 + 128 * h, p1=8), R("dh", 8 * h, 8 * h + 8), R("Ih"), True, True)
-            for b in range(5, 8):
-                act(R("junk", 256 * (b - 5), 256 * (b - 4)), R("X", 256 * b, 256 * b + 256), acc=R("ysb", b, b + 1))
-            act(R("o8", 0, 512, p1=8), R("P5", p1=8))
-            act(R("o8", 512, 768, p1=8), R("P6", 256, 512, p1=8))
-        for b in range(15, -1, -1):
-            if b == 14 and not last:
-                cp(R("lw"), R("P7", 96, 128))
-            if nx[0] and b != 15:
-                shape()
-            if b == 2 and last:
-                final_lanes()
-            if b in (1, 2) and not last:
-                offs(R("oO", 0, 16) if b == 1 else R("oO", 16, 48, 2), R("P4", 320, 336), DBC, -2.0)
-            put_b("oR", -16, "crr", 0, b)
-        if last:
-            for b in range(5):
-                o, i = R("ysb", b, b + 1), R("X", 256 * b, 256 * b + 256)
-                emit("V", [i], [o], lambda: g.vector.tensor_reduce(o[3], i[3], AxisListType.X, OP.add))
+                mm(R("P1", 128 * h, 128 * h + 128, p1=8), R("dh", 8 * h, 8 * h + 8), R("Ih"), True, True)
+            act(R("o8", 0, 256, p1=8), R("P5", 0, 256, p1=8), bias=-1.0)
+            act(R("o8", 256, 512, p1=8), R("P5", 256, 512, p1=8), bias=-0.75)
+            act(R("o8", 512, 768, p1=8), R("P1", 0, 256, p1=8))
+        for b in range(7, -1, -1):
+            if b == LWB and not last:
+                ts(R("lw"), R("P7", 96, 144), -1.0, OP.add)
+            put_r(b)
+            if nx[0]:
+                shape(16 if b == 0 else XPER[b])
+                if not nx[0] and not last:
+                    prep_q()
+                if not nx[0] and last:
+                    dma("S", "dout", 16 * 7, T.ym[:], T.ymb[0:8, 0:6], [R("ymb")], [])
+                    dma("S", "dout", 16 * 7, T.yc[:], T.o8[0:8, 0:256], [R("o8")], [])
+                    dma("S", "dout", 16 * 7, T.yv[:], T.o8[0:8, 256:512], [R("o8")], [])
+                    dma("S", "dout", 16 * 7, T.yd[:], T.o8[0:8, 512:768], [R("o8")], [])
+                    for j in range(YS):
+                        act(R("xe", 256 * j, 256 * j + 256), R("X", 256 * j, 256 * j + 256), acc=R("ysb", j, j + 1))
 
     tot = 16 * 7
-    dma("Y", "dout", tot, T.ym[:], T.ymb[0:1, 0:48], [R("ymb")], [])
     dma("Y", "dout", tot, T.yb[0:64, :], T.Bf[0:64, 0:1024], [R("Bf")], [])
     dma("Y", "dout", tot, T.yb[64:128, :], T.Bf[64:128, 0:1024], [R("Bf")], [])
-    dma("S", "dout", tot, T.yc[:], T.o8[0:8, 0:256], [R("o8")], [])
-    dma("S", "dout", tot, T.yv[:], T.o8[0:8, 256:512], [R("o8")], [])
-    dma("S", "dout", tot, T.yd[:], T.o8[0:8, 512:768], [R("o8")], [])
+    for b in range(YS, 8):
+        o, i = R("ysb", b, b + 1), R("X", 256 * b, 256 * b + 256)
+        emit("V", [i], [o], lambda: g.vector.tensor_reduce(o[3], i[3], AxisListType.X, OP.add))
     dma("S", "dout", tot, T.ys[:], T.ysb[:], [R("ysb")], [])
     g.wait_ge(T.sem.sent, nsent)
     for e in ("V", "S", "P", "G"):

@@ -10,14 +10,19 @@ S00 = 60
 GD = 8
 S1 = 114
 PART = 64
-LATE = 3
+LATE = 2
 YS = 5
-LATE0 = 6
-XPER = (1, 1, 1, 1, 1, 1, 1, 1)
-LWB = 4
-DX = 9
-XPRE = 2
+LATE0 = 11
+MID0 = 6
+LWB = 3
+XPRE = 1
 EARLY = (9, 11, 13, 15)
+
+CYCLE, COLUMN = 1.04, 0.52
+GATHER, SCATTER = 1.3, 3.2
+WAKE = 180.0
+FLIGHT = 2200.0
+PASSES = 4
 
 F, B16, I32, U16 = "float32", "bfloat16", "int32", "uint16"
 SCRATCH = {}
@@ -28,25 +33,25 @@ def _sb(name, cols, dtype):
 
 
 for _n, _c, _d in [
-    ("X", 2064, B16), ("Bi", 1024, I32), ("Bf", 1056, F), ("Bc", 2048, H), ("wf", 16, F), ("rep", 128, H), ("LR", 8, U16), ("Ki", 512, I32), ("Kw", 512, I32), ("Kc", 2048, F), ("KV", 2048, F),
+    ("X", 2080, B16), ("Bi", 1024, I32), ("Bf", 1056, F), ("Bc", 2048, H), ("wf", 16, F), ("rep", 128, H), ("LR", 8, U16), ("Ki", 512, I32), ("Kw", 512, I32), ("Kc", 2048, F), ("KV", 2048, F),
     ("l8", 768, I32), ("Y8", 768, H), ("vv", 16, H),
     ("Eu", 256, U16), ("E16", 256, H), ("nAg", 256, H), ("newc", 256, F), ("xe", 4096, B16), ("tt", 4096, F), ("q", 256, B16), ("yy", 256, B16),
     ("kc", 256, F), ("ke", 256, F), ("sx", 256, B16),
-    ("r1", 128, F), ("r2", 256, F), ("f2", 256, F), ("key", 256, F), ("ks", 256, F), ("oh", 256, F), ("sl", 256, F), ("ss", 264, F),
+    ("r1", 128, F), ("r2", 256, F), ("f2", 256, F), ("key", 256, F), ("ks", 256, F), ("oh", 256, F), ("sl", 256, F), ("ss", 272, F),
     ("Pi", 16, I32), ("pT", 16, I32), ("parT", 16, I32), ("hd", 40, F), ("misT", 16, B16), ("ac", 8, F),
     ("dh", 16, H), ("xp", 128, H), ("xs", 128, H), ("xd", 128, H), ("op2", 256, B16), ("m2s", 256, B16), ("Y2", 512, H), ("Y1", 512, H),
     ("ly", 16, U16), ("lsel", 16, U16), ("lw", 48, U16),
     ("W1", 32, H), ("w2", 16, U16), ("wp", 16, H), ("dW", 16, H), ("hitW", 16, F), ("t1", 16, F), ("t2", 16, F),
-    ("EQ", 384, H), ("EQs", 256, H), ("ab", 256, F), ("oX", 32, U16), ("oO", 32, U16), ("Ag", 256, F), ("Um", 512, F), ("val", 256, B16),
+    ("EQ", 512, H), ("EQs", 256, H), ("ab", 256, F), ("oX", 32, U16), ("oO", 32, U16), ("Ag", 256, F), ("Um", 512, F), ("val", 256, B16),
     ("o8", 768, F), ("ysb", 8, F), ("ymb", 8, F),
     ("sc", 16 * ST, F), ("rc", 16 * ST, F), ("so", 16 * ST, H), ("ro", 16 * ST, H),
     ("crr", 256, F), ("oR", 32, U16), ("MM", 272, F),
     ("row", 272, F), ("row1", 128, F), ("xg", 128, F), ("xa", 272, F), ("xa1", 128, F),
     ("pi", 8, I32), ("pc", 24, F),
-    ("Ib", 128, B16), ("Ih", 128, H), ("nIh", 128, H), ("hIh", 128, H), ("pIh", 128, H), ("I2n", 128, H), ("LS", 8, U16), ("Isx", 128, B16),
+    ("Ib", 128, B16), ("Ih", 128, H), ("nIh", 128, H), ("hIh", 128, H), ("pIh", 128, H), ("I2n", 128, H), ("LS", 4, U16), ("I4k", 128, H), ("Isx", 128, B16),
     ("Iq", 128, B16), ("Ihalf", 128, B16), ("Perm", 128, B16), ("BM", 128, H),
     ("Gq", 256, B16), ("G8", 8, F), ("G32", 32, F), ("Gx", 16, B16), ("Gh", 16, H), ("IN", 128, H), ("Dm", 2048, H), ("Dg", 2048, H), ("s12", 32, F),
-    ("L1", 144, H), ("L2", 240, H), ("L8", 144, H), ("NM", 272, F), ("RST", 128, F), ("CT", 512, H), ("on16", 128, H), ("c24", 256, H), ("m8", 128, H), ("cU", 512, B16),
+    ("L1", 144, H), ("L2", 240, H), ("L8", 144, H), ("NM", 272, F), ("RST", 128, F), ("CT", 512, H), ("on16", 128, H), ("m8", 128, H), ("cU", 512, B16), ("EQx", 512, H),
     ("lane", 16, H), ("one", 16, B16),
     ("LK", 8, U16), ("LT", 16, U16), ("LE", 16, U16),
 ]:
@@ -71,7 +76,13 @@ def rank_program(g, core, T, topo):
     def R(name, lo=0, hi=None, step=1, p1=128):
         if hi is None:
             hi = SCRATCH[name][1][1]
-        return (name, lo, hi, T[name][0:p1, lo:hi:step] if step != 1 else T[name][0:p1, lo:hi])
+        return (name, lo, hi, T[name][0:p1, lo:hi:step] if step != 1 else T[name][0:p1, lo:hi], step)
+
+    def meet(r, s):
+        return r[1] < s[2] and s[1] < r[2] and not (r[4] == s[4] > 1 and (r[1] - s[1]) % r[4])
+
+    def covers(r, s):
+        return r[1] <= s[1] and s[2] <= r[2] and (r[4] == 1 or (r[4] == s[4] and (r[1] - s[1]) % r[4] == 0))
 
     def wait(e, tok):
         if seen[e].get(tok[0], 0) < tok[1]:
@@ -83,8 +94,8 @@ def rank_program(g, core, T, topo):
         for regs, w in ((reads, False), (writes, True)):
             for r in regs:
                 ps = SCRATCH[r[0]][0] == "psum"
-                for (lo, hi, e2, tok, w2) in hist.get(r[0], []):
-                    clash = lo < r[2] and r[1] < hi and (w or w2)
+                for (r2, e2, tok, w2) in hist.get(r[0], []):
+                    clash = meet(r, r2) and (w or w2)
                     if e2 != e:
                         clash = clash or ps
                     elif e == "P":
@@ -98,14 +109,87 @@ def rank_program(g, core, T, topo):
         for regs, w in ((reads, False), (writes, True)):
             for r in regs:
                 old = hist.get(r[0], [])
-                keep = [x for x in old if not (r[1] <= x[0] and x[1] <= r[2] and x[2] == e and x[3][0] == tok[0] and (w or not x[4]))]
-                hist[r[0]] = keep + [(r[1], r[2], e, tok, w)]
+                keep = [x for x in old if not (covers(r, x[0]) and x[1] == e and x[2][0] == tok[0] and (w or not x[3]))]
+                hist[r[0]] = keep + [(r, e, tok, w)]
 
-    def emit(e, reads, writes, call):
-        deps(e, reads, writes)
-        cnt[e] += 1
-        call().then_inc(T.sem["s" + e], 1)
-        note(e, ("s" + e, cnt[e]), reads, writes)
+    calls = []
+
+    def emit(e, reads, writes, call, time):
+        def issue():
+            deps(e, reads, writes)
+            cnt[e] += 1
+            call().then_inc(T.sem["s" + e], 1)
+            note(e, ("s" + e, cnt[e]), reads, writes)
+        calls.append((e, reads, writes, time, time + WAKE, issue, None))
+
+    def size(r):
+        return len(range(r[1], r[2], r[4]))
+
+    def wide(r):
+        return SCRATCH[r[0]][2] in (F, I32)
+
+    def span(e, o, ins, each):
+        for x, c in ((ins[0] if ins else o, GATHER), (o, SCATTER)):
+            if len(x) == 2:
+                return (50.0 if e == "V" else 65.0) + 16 * size(x[0][1]) * c
+        return CYCLE * max(64, size(o) * each)
+
+    def order():
+        n = len(calls)
+        before, after, past, group = [{} for _ in calls], [[] for _ in calls], {}, {}
+        for i, (e, reads, writes, _, _, _, sem) in enumerate(calls):
+            for regs, w in ((reads, False), (writes, True)):
+                for r in regs:
+                    ps = SCRATCH[r[0]][0] == "psum"
+                    for (r2, j, w2) in past.get(r[0], []):
+                        e2 = calls[j][0]
+                        if e == e2 == "P":
+                            if ps:
+                                before[i][j] = calls[j][3]
+                        elif (ps and e != e2) or (meet(r, r2) and (w or w2)):
+                            for k in group.get(calls[j][6], [j]):
+                                if k != i:
+                                    before[i][k] = calls[k][4]
+            for regs, w in ((reads, False), (writes, True)):
+                for r in regs:
+                    keep = [x for x in past.get(r[0], []) if not (x[1] in before[i] and covers(r, x[0]) and (w or not x[2]))]
+                    past[r[0]] = keep + [(r, i, w)]
+            if sem:
+                group.setdefault(sem, []).append(i)
+            for j in before[i]:
+                after[j].append(i)
+
+        def place(turn, earliest):
+            busy, at = {e: [] for e in Q}, [0.0] * n
+            for i in turn:
+                line, t, time = busy[calls[i][0]], earliest(i, at), calls[i][3]
+                k = len(line)
+                while k and line[k - 1][1] > t:
+                    k -= 1
+                while k < len(line) and line[k][0] < t + time:
+                    t = max(t, line[k][1])
+                    k += 1
+                line.insert(k, (t, t + time))
+                at[i] = t
+            return at
+
+        def forward(i, at):
+            return max([0.0] + [at[j] + d for j, d in before[i].items()])
+
+        def backward(i, at):
+            time = calls[i][3]
+            return max([calls[i][4] - time] + [at[k] + calls[k][3] + before[k][i] - time for k in after[i]])
+
+        back = place(list(range(n - 1, -1, -1)), backward)
+        turn, best = sorted(range(n), key=lambda i: (-back[i] - calls[i][3], i)), None
+        for _ in range(PASSES):
+            at = place(turn, forward)
+            end = max(at[i] + calls[i][4] for i in range(n))
+            if best is None or end < best[0]:
+                best = (end, at)
+            back = place(sorted(range(n), key=lambda i: (-at[i] - calls[i][3], -i)), backward)
+            turn = sorted(range(n), key=lambda i: (-back[i] - calls[i][3], i))
+        return sorted(range(n), key=lambda i: (best[1][i], i))
 
     def ind(win, off):
         return ([win, off], win[3].indirect(off[3]))
@@ -119,28 +203,33 @@ def rank_program(g, core, T, topo):
     def cp(o, i):
         w, r0, oa = outs(o)
         r, ia = sides(i)
-        emit("V", r + r0, w, lambda: g.vector.tensor_copy(oa, ia))
+        emit("V", r + r0, w, lambda: g.vector.tensor_copy(oa, ia), span("V", o, [i], 1.0 if wide(w[0]) or wide(r[0]) else 0.5))
 
     def tt(o, a, b, op):
         w, r0, oa = outs(o)
         r, ia = sides(a)
-        emit("V", r + r0 + [b], w, lambda: g.vector.tensor_tensor(oa, ia, b[3], op))
+        both = SCRATCH[r[0][0]][0] == SCRATCH[b[0]][0]
+        emit("V", r + r0 + [b], w, lambda: g.vector.tensor_tensor(oa, ia, b[3], op), span("V", o, [a], 2.0 if both else 1.0))
 
     def ts(o, a, s1, op0, s2=None, op1=None):
         r, ia = sides(a)
         rs = [s for s in (s1, s2) if isinstance(s, tuple)]
         a1 = s1[3] if isinstance(s1, tuple) else s1
         a2 = s2[3] if isinstance(s2, tuple) else s2
+        time = span("V", o, [a], 1.0 if wide(o) or wide(r[0]) else 0.5)
         if op1 is None:
-            emit("V", r + rs, [o], lambda: g.vector.tensor_scalar(o[3], ia, a1, None, op0))
+            emit("V", r + rs, [o], lambda: g.vector.tensor_scalar(o[3], ia, a1, None, op0), time)
         else:
-            emit("V", r + rs, [o], lambda: g.vector.tensor_scalar(o[3], ia, a1, a2, op0, op1))
+            emit("V", r + rs, [o], lambda: g.vector.tensor_scalar(o[3], ia, a1, a2, op0, op1), time)
 
     def scan(o, d0, d1):
-        emit("V", [d0, d1], [o], lambda: g.vector.tensor_tensor_scan(o[3], d0[3], d1[3], 0.0, OP.min, OP.max))
+        emit("V", [d0, d1], [o], lambda: g.vector.tensor_tensor_scan(o[3], d0[3], d1[3], 0.0, OP.min, OP.max), span("V", o, [d1], 1.0))
 
     def mset(o, v):
-        emit("V", [], [o], lambda: g.vector.memset(o[3], v))
+        emit("V", [], [o], lambda: g.vector.memset(o[3], v), span("V", o, [], 1.0 if wide(o) else 0.5))
+
+    def row_sum(o, i):
+        emit("V", [i], [o], lambda: g.vector.tensor_reduce(o[3], i[3], AxisListType.X, OP.add), span("V", i, [i], 1.0))
 
     def act(o, i, fn=AF.Identity, bias=0.0, scale=1.0, acc=None):
         w, r0, oa = outs(o)
@@ -148,29 +237,47 @@ def rank_program(g, core, T, topo):
         rs = [s for s in (bias, scale) if isinstance(s, tuple)]
         ba = bias[3] if isinstance(bias, tuple) else bias
         sa = scale[3] if isinstance(scale, tuple) else scale
+        time = span("S", o, [i], 1.0)
         if fn == AF.Silu:
-            emit("S", r + r0, w, lambda: g.scalar.activation(oa, ia, fn))
+            emit("S", r + r0, w, lambda: g.scalar.activation(oa, ia, fn), time if len(o) == 2 else time + 1300.0)
         elif acc is None:
-            emit("S", r + rs, w, lambda: g.scalar.activation(oa, ia, fn, bias=ba, scale=sa))
+            emit("S", r + rs, w, lambda: g.scalar.activation(oa, ia, fn, bias=ba, scale=sa), time)
         else:
-            emit("S", r + rs, w + [acc], lambda: g.scalar.activation(oa, ia, fn, bias=ba, scale=sa, accum_out=acc[3]))
+            emit("S", r + rs, w + [acc], lambda: g.scalar.activation(oa, ia, fn, bias=ba, scale=sa, accum_out=acc[3]), time)
 
     def mm(o, l, r, start, stop):
-        emit("P", [l, r], [o], lambda: g.tensor.matmul(o[3], l[3], r[3], start, stop))
+        emit("P", [l, r], [o], lambda: g.tensor.matmul(o[3], l[3], r[3], start, stop),
+             COLUMN * max(min(64, size(l)), size(r)) * (4 if wide(l) else 1))
 
     def iota(o, pat, base=0, cm=0):
+        time = 160.0 + 2 * CYCLE * size(o)
         if SCRATCH[o[0]][2] != I32:
-            emit("G", [], [o], lambda: g.iota(o[3], pat, base, cm, allow_small_or_imprecise_dtypes=True))
+            emit("G", [], [o], lambda: g.iota(o[3], pat, base, cm, allow_small_or_imprecise_dtypes=True), time)
         else:
-            emit("G", [], [o], lambda: g.iota(o[3], pat, base, cm))
+            emit("G", [], [o], lambda: g.iota(o[3], pat, base, cm), time)
 
-    def dma(e, sem, total, out_ap, in_ap, reads, writes):
-        deps(e, reads, writes)
-        Q[e].dma_start(out_ap, in_ap).then_inc(T.sem[sem], 16)
-        note("D", (sem, total), reads, writes)
+    def select(o, i, pat, base, cm):
+        emit("G", [i], [o], lambda: g.affine_select(o[3], i[3], pat, OP.is_equal, 0.0, base, cm), 210.0 + 2 * CYCLE * size(o))
+
+    def dma(e, sem, total, out_ap, in_ap, reads, writes, time=2000.0):
+        def issue():
+            deps(e, reads, writes)
+            Q[e].dma_start(out_ap, in_ap).then_inc(T.sem[sem], 16)
+            note("D", (sem, total), reads, writes)
+        calls.append((e, reads, writes, 50.0, time, issue, sem))
+
+    def send(reg, rname, sem, dst, src):
+        land = R(rname, reg[1], reg[2])
+        rid, pid = topo.addr(dst, core)
+
+        def issue():
+            deps("G", [reg], [])
+            g.remote_dma(land[3], reg[3], T.sem[sem], T.sem.sent, pid, rid, topo.mask(core, dst))
+            note("R", (sem, len(topo.engines(src, core))), [], [land])
+        calls.append(("G", [reg], [land], 300.0, FLIGHT, issue, None))
 
     PCOL, ACOL, GCOL, HC, B7, L1C, L2C, L8C, LANEC, DXC, DBC, MC, E0C, E1C = [R("pc", j, j + 1) for j in range(14)]
-    S0C, S1C, DB2, R2C = [R("pc", j, j + 1) for j in range(16, 20)]
+    S0C, S1C, DB2, DX2 = [R("pc", j, j + 1) for j in range(16, 20)]
     C1, C2 = R("pc", 14, 15, p1=16), R("pc", 15, 16, p1=16)
     LOPP, LCW, LOWN, WO, WC = R("lw", 0, 16), R("lw", 16, 32), R("lw", 32, 48), R("W1", 0, 16), R("W1", 16, 32)
     PH = ("P1", "P2")
@@ -178,9 +285,9 @@ def rank_program(g, core, T, topo):
     dma("Y", "dl", 48, T.l8[0:8, 0:256], T.lv[:], [], [R("l8", 0, 256)])
     dma("S", "dl", 48, T.l8[0:8, 256:512], T.ld[:], [], [R("l8", 256, 512)])
     dma("Y", "dl", 48, T.l8[0:8, 512:768], T.lc[:], [], [R("l8", 512, 768)])
-    dma("S", "db", 16, T.Bi[:], T.bnd[:], [], [R("Bi")])
-    dma("Y", "dx", 16, T.X[:, 0:2048], T.x[:], [], [R("X", 0, 2048)])
-    dma("S", "dk", 16, T.Ki[:], T.kt[:], [], [R("Ki")])
+    dma("S", "db", 16, T.Bi[:], T.bnd[:], [], [R("Bi")], 4500.0)
+    dma("Y", "dx", 16, T.X[:, 0:2048], T.x[:], [], [R("X", 0, 2048)], 4500.0)
+    dma("S", "dk", 16, T.Ki[:], T.kt[:], [], [R("Ki")], 4500.0)
 
     pi = lambda j: R("pi", j, j + 1)
     iota(pi(0), [[0, 1]], 0, 1)
@@ -190,14 +297,13 @@ def rank_program(g, core, T, topo):
     mset(R("ab", 0, 32), OFF)
     act(R("Bf", 1024, 1056), R("ab", 0, 32), AF.Silu)
     mset(R("on16", p1=16), 1.0)
-    mset(R("c24", p1=16), (OFF - 1.0) / 16)
     ts(pi(1), pi(0), 15, OP.bitwise_and)
     ts(pi(2), pi(0), 4, OP.arith_shift_right)
     ts(pi(3), pi(0), 8, OP.bitwise_and)
     ts(pi(4), pi(0), 7, OP.bitwise_and)
-    mset(R("X", 2048, 2064), 0.0)
+    mset(R("X", 2048, 2080), 0.0)
     cp(R("pc", 0, 5), R("pi", 0, 5))
-    mset(R("hd", 32, 40), 0.0)
+    mset(R("hd"), 0.0)
     ts(L8C, PCOL, 16.0, OP.mult, 15.0, OP.add)
     ts(R("Ih"), R("row", 0, 128), PCOL, OP.is_equal)
     ts(R("L8", 0, 144), R("row", 0, 144), L8C, OP.is_equal)
@@ -215,14 +321,12 @@ def rank_program(g, core, T, topo):
     ts(R("CT", 384, 512, p1=16), R("on16", p1=16), 2040.0, OP.mult, C2, OP.mult)
 
     for r in range(GD, 16):
-        o = R("Dg", 128 * r, 128 * r + 128)
-        emit("G", [R("Ih")], [o], lambda: g.affine_select(o[3], T.Ih[:, :], [[0, 8], [1, 16]], OP.is_equal, 0.0, -r, 0))
+        select(R("Dg", 128 * r, 128 * r + 128), R("Ih"), [[0, 8], [1, 16]], -r, 0)
     iota(R("row", 144, 272), [[1, 128]], 144)
     iota(R("xa1"), [[0, 8], [2, 8], [-1, 2]], 1)
     iota(R("row1"), [[2, 64], [-1, 2]], 1)
     for a in range(16):
-        o = R("Bc", 128 * a, 128 * a + 128)
-        emit("G", [R("BM")], [o], lambda: g.affine_select(o[3], T.BM[:, :], [[-16, 8], [0, 16]], OP.is_equal, 0.0, -a, 1))
+        select(R("Bc", 128 * a, 128 * a + 128), R("BM"), [[-16, 8], [0, 16]], -a, 1)
 
     def Lsl(name, a, p1=128):
         return R(name, 15 - a, 143 - a, p1=p1)
@@ -232,9 +336,8 @@ def rank_program(g, core, T, topo):
             mm(out, Lsl(L, a, p1), R(ybuf, lo + a, hi, 16, p1=p1), start and a == 0, stop and a == 15)
 
     def rot(ybuf, lo, t, L="L1", p1=128):
-        mm(R("P5", 0, 256), R("on16", p1=16), R("c24", p1=16), True, False)
         for a in range(16):
-            mm(R("P5", a, 256, 16), Lsl(L, (5 * t + a) % 16, p1), R(ybuf, lo + a, lo + 256, 16, p1=p1), False, False)
+            mm(R("P5", a, 256, 16), Lsl(L, (5 * t + a) % 16, p1), R(ybuf, lo + a, lo + 256, 16, p1=p1), a == 0, False)
 
     def old_rows(t):
         mm(R("P5", 0, 256), R("nIh"), R("nAg"), False, False)
@@ -271,7 +374,22 @@ def rank_program(g, core, T, topo):
         act(ind(R("Bf"), R("oO", 2 * b, 2 * b + 1)), R("newc", 16 * b, 16 * b + 16), AF.Silu)
 
     def put_x(b):
-        cp(ind(R("X"), R("oX", 2 * b, 2 * b + 1)), R("val", 16 * b, 16 * b + 16))
+        cp(ind(R("X"), R("oX", 2 * b, 2 * b + 2)), R("val", 32 * b, 32 * b + 32))
+
+    def rivals(w, eq, across, low, high, out, lists, spare):
+        act(R("wf"), w)
+        act(R("rep"), ind(R("wf"), R("LR")))
+        for a in range(16):
+            mm(R(across[0], across[1] + a, across[1] + 128, 16), R("Bc", 128 * a, 128 * a + 128), R(w[0], w[1], w[2], 2), True, True)
+        for a in range(1, 16):
+            mm(R(low if a < 9 else high, 16 * a, 16 * a + 16), R("Dm", 128 * a, 128 * a + 128), w, True, True)
+        tt(R(eq, 256, 384), R("rep"), R(across[0], across[1], across[1] + 128), OP.is_equal)
+        ts(R(eq, 16, 144), R(low, 16, 144), 0.0, OP.is_equal, 4096.0, OP.mult)
+        scan(R(eq, 384, 512), R("RST"), R(eq, 256, 384))
+        ts(R(eq, 144, 256), R(high, 144, 256), 0.0, OP.is_equal, 4096.0, OP.mult)
+        losers(R(out[0], out[1], out[1] + 16), w, eq, stop=False)
+        mm(R(out[0], out[1] + 1, out[1] + 16, 2), R("I4k"), R(eq, 399, 512, 16), False, True)
+        return [lambda j=j: offs(R(lists, j, 16, 2), R(out[0], out[1] + j, out[1] + 16, 2), spare[j]) for j in range(2)]
 
     def side():
         act(R("sx"), ind(R("hd", 16, 32), R("LT")), scale=1.0 / 256, bias=-1.0 / 512)
@@ -334,14 +452,10 @@ def rank_program(g, core, T, topo):
     act(R("W1"), R("P7", 96, 128))
     open_sums()
 
-    def tables(own):
-        act(R("KV", 0, 512), R("Kw"), scale=2.0, bias=1.5)
-        own(1)
-        act(R("Kc", 0, 512), R("Ki"), bias=1.0)
-        own(1)
-        for s, sem in (("KV", "dr2"), ("Kc", "dr1")):
-            for j in range(1, 4):
-                dma("Y", sem, 48, T[s][:, 512 * j:512 * j + 512], T[s][:, 0:512], [R(s, 0, 512)], [R(s, 512 * j, 512 * j + 512)])
+    def table(s, src, scale, bias, sem):
+        act(R(s, 0, 512), R(src), scale=scale, bias=bias)
+        for j in range(1, 4):
+            dma("Y", sem, 48, T[s][:, 512 * j:512 * j + 512], T[s][:, 0:512], [R(s, 0, 512)], [R(s, 512 * j, 512 * j + 512)])
 
     def consts_choice(own):
         own(1)
@@ -349,40 +463,42 @@ def rank_program(g, core, T, topo):
         act(L2C, ACOL, bias=112.0)
         own(1)
         act(LANEC, ACOL, bias=128.0)
-        act(S0C, HC, scale=16.0, bias=-241.0)
+        act(S0C, HC, scale=2.0, bias=-113.0)
         act(E0C, HC, bias=-32.0)
         own(1)
         ts(MC, B7, GCOL, OP.is_equal)
         ts(R("LK"), R("row", 0, 8), 16.0, OP.mult, 15.0, OP.add)
-        mset(R("ss", 256, 264), 0.0)
+        mset(R("ss", 128, 136), 0.0)
+        mset(R("ss", 264, 272), 0.0)
         mset(R("one"), 1.0)
         act(E0C, E0C, scale=MC, bias=32.0)
-        act(S0C, S0C, scale=MC, bias=256.0)
-        act(S1C, MC, scale=16.0)
+        act(S0C, S0C, scale=MC, bias=128.0)
+        act(S1C, MC, scale=32.0)
         own(1)
         act(E1C, MC, scale=16.0, bias=E0C)
         act(R("lane"), R("row", 0, 16), scale=16.0, bias=LANEC)
+        act(R("Iq"), R("Ib"), scale=-0.25)
+        act(R("Ihalf"), R("Ib"), scale=0.5)
         own(1)
 
     def consts_lists():
         ts(R("L2"), R("row", 0, 240), L2C, OP.is_equal)
         ts(R("LE", 0, 8), R("row", 0, 8), MC, OP.mult, E0C, OP.add)
-        ts(R("LE", 8, 16), R("row", 0, 8), MC, OP.mult, E1C, OP.add)
-        ts(R("LS"), R("row", 0, 8), S1C, OP.mult, S0C, OP.add)
-
-    def consts_late():
-        ts(R("Iq"), R("Ib"), -0.25, OP.mult)
-        ts(R("Ihalf"), R("Ib"), 0.5, OP.mult)
         mset(R("cU", 0, 256), 0.375)
         mset(R("cU", 256, 512), -0.25)
+        ts(R("LE", 8, 16), R("row", 0, 8), MC, OP.mult, E1C, OP.add)
+        ts(R("LS"), R("row", 0, 4), S1C, OP.mult, S0C, OP.add)
+
+    def consts_late():
         ts(R("Perm"), R("row1"), PCOL, OP.is_equal)
         ts(R("NM"), R("xa"), ACOL, OP.not_equal)
         ts(R("MM"), R("xa"), ACOL, OP.is_equal)
         ts(R("m8", p1=8), R("xg", p1=8), R("pc", 0, 1, p1=8), OP.is_equal, 64.0, OP.mult)
         ts(DXC, ACOL, 2048.0, OP.add)
+        ts(DX2, ACOL, 2064.0, OP.add)
         ts(DB2, ACOL, 1040.0, OP.add)
-        act(R2C, B7, scale=2.0)
-        ts(R("LR"), R("row", 0, 8), 0.0, OP.mult, R2C, OP.add)
+        act(R("I4k"), R("Ih"), scale=4096.0)
+        ts(R("LR"), R("row", 0, 8), 2.0, OP.mult, 1.0, OP.add)
 
     def open_values():
         mm(R("P3"), R("Ib"), R("cU"), True, False)
@@ -393,14 +509,8 @@ def rank_program(g, core, T, topo):
     for t in range(ST):
         last = t == ST - 1
         dst = T.cores[(rank + 1 + t % (N - 1)) % N]
-        rid, pid = topo.addr(dst, core)
-        msk = topo.mask(core, dst)
+        src = T.cores[(rank - 1 - t % (N - 1)) % N]
         neng = len(topo.engines(core, dst))
-        nin = len(topo.engines(T.cores[(rank - 1 - t % (N - 1)) % N], core))
-
-        def send(reg, rname, sem):
-            deps("G", [reg], [])
-            g.remote_dma(T[rname][:, reg[1]:reg[2]], reg[3], T.sem[sem], T.sem.sent, pid, rid, msk)
 
         BT, boff = (R("Bi"), 0.0) if t == 0 else (R("Bf"), OFF)
         ts(R("Eu", 0, 128), ind(BT, R("lw", 0, 8)), 0.25 - boff, OP.add)
@@ -421,8 +531,8 @@ def rank_program(g, core, T, topo):
         if t == 0:
             ts(R("EQs", 16, 256), R("P6", 16, 256), 0.0, OP.is_equal, 4096.0, OP.mult)
             ts(DBC, ACOL, 1024.0, OP.add)
-            act(R("Bf", 0, 1024), R("Bi"), bias=OFF)
-        act(R("newc"), R("P5", 0, 256))
+        else:
+            act(R("newc"), R("P5", 0, 256), bias=OFF - 1.0)
 
         kind = lambda h, j, lo, hi: R(PH[h], 128 * j + lo, 128 * j + hi)
         sb = lambda n, h, lo, hi: R(n, 128 * h + lo, 128 * h + hi)
@@ -434,7 +544,7 @@ def rank_program(g, core, T, topo):
             lambda h, lo, hi: scan(sb("ks", h, lo, hi), R("RST", lo, hi), sb("key", h, lo, hi)),
             lambda h, lo, hi: tt(sb("oh", h, lo, hi), ind(sb("ks", h, lo, hi), R("LK", 0, (hi - lo) // 16)), sb("key", h, lo, hi), OP.is_equal),
             lambda h, lo, hi: tt(sb("sl", h, lo, hi), sb("oh", h, lo, hi), kind(h, 3, lo, hi), OP.mult),
-            lambda h, lo, hi: scan(sb("ss", h, lo, hi), R("RST", lo, hi), sb("sl", h, lo, hi)),
+            lambda h, lo, hi: scan(R("ss", 136 * h + lo, 136 * h + hi), R("RST", lo, hi), sb("sl", h, lo, hi)),
         ]
 
         def sum_x(h, k):
@@ -450,9 +560,12 @@ def rank_program(g, core, T, topo):
                 hh = k // 15
                 mm(R(PH[hh], 384, 512), R("E16", 128 * hh, 128 * hh + 128), R("Ih"), False, True)
             if h == 1 and k == 1:
-                own(2)
+                own(2 if t else 0)
                 act(R("r1"), R("P1", 0, 128), bias=MAGIC2)
-                own(1)
+                if t:
+                    own(1)
+                else:
+                    act(R("newc"), R("P5", 0, 256), bias=OFF - 1.0)
                 act(R("r2", 0, 128), R("r1"), bias=-MAGIC2)
 
         nb = [16]
@@ -468,8 +581,10 @@ def rank_program(g, core, T, topo):
             losers(R("P4", 320, 336), WO, "EQs", "dW")
         for k in range(16):
             rows(0, k)
+            if t == 0 and k == 11:
+                ts(R("Kw"), R("Ki"), 511, OP.bitwise_and)
         if t == 0:
-            ts(R("Kw"), R("Ki"), 511, OP.bitwise_and)
+            table("KV", "Kw", 2.0, 1.5, "dr2")
         else:
             cp(R("xe", 2048 + 16 * s1, 4096), ind(R("X"), R("Eu", 128 + s1, 256)))
         for k in range(16):
@@ -477,8 +592,9 @@ def rank_program(g, core, T, topo):
                 offs(R("oO", 0, 32, 2), R("P4", 320, 336), DBC)
             rows(1, k)
             if k == 1 and t == 0:
-                consts_choice(own)
-                tables(own)
+                table("Kc", "Ki", 1.0, 1.0, "dr1")
+                consts_choice(lambda n: None)
+                act(R("Bf", 0, 1024), R("Bi"), bias=OFF)
             if k in EARLY:
                 stage[1 + EARLY.index(k)](0, 0, 128)
         if t == 0:
@@ -488,130 +604,125 @@ def rank_program(g, core, T, topo):
             own(1)
             act(R("kc"), ind(R("Kc"), LCW))
             own(nb[0] - LATE)
-            open_values()
+        open_values()
         mm(R("P6", 256, 272), R("Ih"), R("lane"), True, False)
 
-        rest = list(range(1 + len(EARLY), 8))
+        def chosen(h):
+            ts(R("xp", 64 * h, 64 * h + 64), ind(R("ss", 136 * h, 136 * h + 136), R("LS")), MAGIC, OP.add, MAGIC, OP.subtract)
+            for gg in range(8):
+                mm(R("P7", 8 * h, 8 * h + 8), R("L2", 112 - 16 * gg, 240 - 16 * gg), R("xp", 64 * h + 8 * gg, 64 * h + 8 * gg + 8), gg == 0, gg == 7)
+
+        def payload(h):
+            ts(R("Pi", 8 * h, 8 * h + 8), R("ss", 136 * h + 15, 136 * h + 128, 16), 4096.0, OP.mult, 2040.125, OP.add)
+
+        def low_bits(h):
+            ts(R("pT", 8 * h, 8 * h + 8), R("Pi", 8 * h, 8 * h + 8), 15, OP.bitwise_and)
+
+        def e_list(h):
+            ts(R("ly", 8 * h, 8 * h + 8), R("P7", 8 * h, 8 * h + 8), -1.0, OP.add)
+            act(R("ke", 128 * h, 128 * h + 128), ind(R("KV"), R("ly", 8 * h, 8 * h + 8)))
+
+        MK = (R("P4", 0, 128), R("P0", 128, 256))
+
+        def mask(h):
+            o = R("op2", 128 * h, 128 * h + 128)
+            tt(o, ind(R("pT", 8 * h, 8 * h + 8), R("LT", 0, 8)), R("xa1"), OP.is_equal)
+            mm(MK[h], o, R("Ib"), True, True)
+
+        def pick(h, lo, k):
+            tt(R("Y2", lo + 128 * h, lo + 128 * h + 128), R(k, 128 * h, 128 * h + 128), MK[h], OP.mult)
+
+        rest = [lambda j=j: stage[j](0, 0, 128) for j in range(1 + len(EARLY), 8)]
+        rest += [lambda: chosen(0), lambda: payload(0), lambda: None, lambda: e_list(0), lambda: low_bits(0)]
         for j in range(8):
             if rest:
-                stage[rest.pop(0)](0, 0, 128)
+                rest.pop(0)()
             for lo in range(0, 128, PART):
                 stage[j](1, lo, lo + PART)
             if j == 4:
                 act(R("hd", 0, 16), R("ks", 15, 256, 16), AF.Sign, bias=0.75 / 4096)
                 act(R("xs"), ind(R("hd"), R("LE", 0, 8)), scale=-128.0)
                 act(R("misT"), R("hd", 0, 16), scale=-0.5, bias=0.5)
-                own(2)
-        t_to_w(R("P6", 256, 272), "xs", False)
+                t_to_w(R("P6", 256, 272), "xs", False)
+        for f in rest:
+            f()
+        act(R("yy", 0, 128), ind(R("X"), R("ly", 0, 8)))
+        if t == 0:
+            act(R("kc"), ind(R("Kc"), LCW))
         PA = R("P4", 304, 305, p1=8)
         for h in range(2):
             mm(PA, R("misT", 8 * h, 8 * h + 8), R("one", 0, 1), h == 0, h == 1)
         act(R("hitW"), R("P6", 256, 272), AF.Sign, scale=-1.0, bias=255.5)
         act(R("ymb", t, t + 1, p1=8), PA)
         act(R("hitW"), R("hitW"), AF.Relu)
-        ts(R("Pi"), R("ss", 15, 256, 16), 4096.0, OP.mult, 2040.125, OP.add)
-        ts(R("xp"), ind(R("ss"), R("LS")), MAGIC, OP.add, MAGIC, OP.subtract)
-        t_to_w(R("P7", 0, 16), "xp", True)
+        cp(R("lsel"), R("P6", 256, 272))
+        chosen(1)
+        payload(1)
+        mask(0)
         ts(R("parT"), R("Pi"), 1, OP.bitwise_and)
-        ts(R("pT"), R("Pi"), 15, OP.bitwise_and)
+        low_bits(1)
         tt(R("hd", 16, 32), R("hd", 16, 32), R("parT"), OP.not_equal)
+        e_list(1)
         act(R("xd"), ind(R("hd"), R("LE", 8, 16)))
-        tt(R("op2", 0, 128), ind(R("pT"), R("LT", 0, 8)), R("xa1", 0, 128), OP.is_equal)
-        ts(R("ly"), R("P7", 0, 16), -1.0, OP.add)
-        act(R("ke"), ind(R("KV"), R("ly")))
-        own(1)
+        mask(1)
         tt(R("t1"), R("P7", 0, 16), WC, OP.subtract)
-        tt(R("op2", 128, 256), ind(R("pT"), R("LT", 8, 16)), R("xa1", 0, 128), OP.is_equal)
-        for bank in ("P0", "P4"):
-            for h in range(2):
-                mm(R(bank, 128 * h, 128 * h + 128), R("op2", 128 * h, 128 * h + 128), R("Ib"), True, True)
-            if bank == "P0":
-                t_to_w(R("P6", 288, 304), "xd", True)
-        act(R("dW"), R("P6", 288, 304), scale=2.0, bias=-1.0)
-        if t == 0:
-            act(R("kc"), ind(R("Kc"), LCW))
-        act(R("yy"), ind(R("X"), R("ly")))
+        pick(0, 256, "ke")
         tt(R("t2"), R("t1"), R("hitW"), OP.mult)
-        tt(R("wp"), R("t2"), WC, OP.add)
-        tt(R("Y2", 256, 512), R("ke"), R("P0", 0, 256), OP.mult)
-        diff(R("wp"), "P2", 1, DX)
+        pick(0, 0, "kc")
+        mm(R("P4", 128, 256), R("op2", 128, 256), R("Ib"), True, True)
+        t_to_w(R("P6", 288, 304), "xd", True)
+        act(R("yy", 128, 256), ind(R("X"), R("ly", 8, 16)))
+        act(R("dW"), R("P6", 288, 304), scale=2.0, bias=-1.0)
+        act(R("m2s"), R("P4", 0, 256))
+        pick(1, 256, "ke")
         y_to_w(R("P7", 16, 32), "Y2", 256, 512, True, False)
         mm(R("P7", 16, 32), R("hIh"), R("dW"), False, True)
-        tt(R("Y2", 0, 256), R("kc"), R("P0", 0, 256), OP.mult)
-        cp(R("lsel"), R("P6", 256, 272))
-        own(1)
-        act(R("m2s"), R("P4", 0, 256))
-        own(16)
+        pick(1, 0, "kc")
+        tt(R("wp"), R("t2"), WC, OP.add)
+        own(16 if t else MID0)
         if last:
             ts(R("Bf", 0, 512), R("Bf", 0, 512), MAGIC - OFF, OP.add, MAGIC, OP.subtract)
         cp(R("so", 16 * t, 16 * t + 16), R("P7", 16, 32))
-        send(R("so", 16 * t, 16 * t + 16), "ro", "ao%d" % t)
+        send(R("so", 16 * t, 16 * t + 16), "ro", "ao%d" % t, dst, src)
         if last:
             ts(R("Bf", 512, 1024), R("Bf", 512, 1024), MAGIC - OFF, OP.add, MAGIC, OP.subtract)
-        if t == 0:
-            consts_late()
-            open_values()
-        diff(R("wp"), "P2", DX, 16)
-        mm(R("P3", 0, 256), R("Ib"), R("yy"), False, False)
-        mm(R("P3", 256, 512), R("Ihalf"), R("yy"), False, True)
-        mm(R("P1", 0, 256), R("Perm"), R("m2s"), True, True)
-        for a in range(16):
-            mm(R("P5", 256, 272), Lsl("L1", (5 * t + a) % 16), R("Y2", a, 256, 16), a == 0, a == 15)
-        act(R("Um"), R("P3"), bias=MAGIC)
-        ts(R("EQ", 16, 256), R("P2", 16, 256), 0.0, OP.is_equal, 4096.0, OP.mult)
-        losers(R("P2", 256, 272), R("wp"), "EQ")
-        tt(R("Y1", 0, 256), R("ke"), R("P1", 0, 256), OP.mult)
-        ts(R("sc", 16 * t, 16 * t + 16), R("P5", 256, 272), -1.0 if last else OFF - 1.0, OP.add)
-        send(R("sc", 16 * t, 16 * t + 16), "rc", "ac%d" % t)
-        nsent += 2 * neng
-        act(R("val"), ind(R("Um"), R("lsel")), AF.Abs, bias=-MAGIC)
-        tt(R("Y1", 256, 512), R("kc"), R("P1", 0, 256), OP.mult)
-        if not last:
-            y_to_w(R("P7", 96, 112), "Y1", 0, 256, True, False)
-            mm(R("P7", 96, 112), R("hIh"), R("dW"), False, True)
-        offs(R("oX", 0, 32, 2), R("P2", 256, 272), DXC)
-        nx = [16]
+        nx = [8]
 
         def shape(n=1):
             for _ in range(min(n, nx[0])):
                 nx[0] -= 1
                 put_x(nx[0])
 
-        RO = R("ro", 16 * t, 16 * t + 16)
-        wait("P", ("ao%d" % t, nin))
-        for a in range(1, 16):
-            bank = "P6" if a < 9 else "P0"
-            mm(R(bank, 16 * a, 16 * a + 16), R("Dm", 128 * a, 128 * a + 128), RO, True, True)
-        shape(XPRE)
-        wait("V", ("ao%d" % t, nin))
-        cp(R("wf"), RO)
+        if t == 0:
+            consts_late()
+        for a in range(16):
+            mm(R("P5", 256, 272), Lsl("L1", (5 * t + a) % 16), R("Y2", a, 256, 16), a == 0, a == 15)
+        mm(R("P1", 0, 256), R("Perm"), R("m2s"), True, True)
+        ts(R("sc", 16 * t, 16 * t + 16), R("P5", 256, 272), -1.0 if last else OFF - 1.0, OP.add)
+        send(R("sc", 16 * t, 16 * t + 16), "rc", "ac%d" % t, dst, src)
+        nsent += 2 * neng
+        mm(R("P3", 0, 256), R("Ib"), R("yy"), False, False)
+        mm(R("P3", 256, 512), R("Ihalf"), R("yy"), False, True)
+        tt(R("Y1", 0, 256), R("ke"), R("P1", 0, 256), OP.mult)
+        lists = rivals(R("wp"), "EQx", ("P0", 256), "P2", "P2", ("P2", 400), "oX", (DXC, DX2))
+        act(R("Um"), R("P3"), bias=MAGIC)
+        tt(R("Y1", 256, 512), R("kc"), R("P1", 0, 256), OP.mult)
+        own(1)
+        act(R("val"), ind(R("Um"), R("lsel")), AF.Abs, bias=-MAGIC)
+        own(16)
+        for f in lists:
+            f()
+        RO, s = R("ro", 16 * t, 16 * t + 16), (5 * t) % 16
         ts(R("w2"), RO, -1.0, OP.add)
-        shape()
-        cp(R("rep"), ind(R("wf"), R("LR")))
-        shape()
-        mm(R("P1", 256, 384), R("nIh"), R("rep"), True, False)
-        for a in range(16):
-            mm(R("P1", 256 + 8 * a, 264 + 8 * a), R("Bc", 128 * a, 128 * a + 128), R("ro", 16 * t + 1, 16 * t + 16, 2), False, a == 15)
-        s = (5 * t) % 16
-        ts(R("EQ", 16, 144), R("P6", 16, 144), 0.0, OP.is_equal, 4096.0, OP.mult)
-        ts(R("EQ", 144, 256), R("P0", 144, 256), 0.0, OP.is_equal, 4096.0, OP.mult)
-        shape()
-        losers(R("P4", 352, 368), RO, "EQ", stop=False)
         tt(R("Ag"), ind(R("Bf"), R("w2")), R("NM", s, s + 256), OP.mult)
-        shape()
-        ts(R("EQ", 256, 384), R("P1", 256, 384), 0.0, OP.is_equal, 4096.0, OP.mult)
-        for a in range(16):
-            mm(R("P4", 353, 368, 2), Lsl("L1", a), R("EQ", 256 + 8 * a, 264 + 8 * a), False, a == 15)
-        shape()
-        wait("V", ("ac%d" % t, nin))
+        lists = rivals(RO, "EQ", ("P5", 272), "P6", "P0", ("P4", 352), "oR", (DBC, DB2))
         tt(R("crr"), ind(R("rc", 16 * t, 16 * t + 16), R("LT")), R("MM", s, s + 256), OP.mult)
-        shape(2)
-        offs(R("oR", 0, 16, 2), R("P4", 352, 368, 2), DBC)
-        hist["oR"], even = [], hist["oR"]
-        offs(R("oR", 1, 16, 2), R("P4", 353, 368, 2), DB2)
-        hist["oR"] += even
-        shape()
+        shape(XPRE)
+        for f in lists:
+            f()
         if not last:
+            y_to_w(R("P7", 96, 112), "Y1", 0, 256, True, False)
+            mm(R("P7", 96, 112), R("hIh"), R("dW"), False, True)
             y_to_w(R("P7", 112, 128), "Y1", 256, 512, True)
             A1, A2, A3 = [R("ac", j, j + 1, p1=8) for j in range(3)]
             act(A1, R("ymb", t, t + 1, p1=8), scale=0.499, bias=MAGIC)
@@ -636,15 +747,17 @@ def rank_program(g, core, T, topo):
             act(R("o8", 0, 256, p1=8), R("P5", 0, 256, p1=8), bias=-1.0)
             act(R("o8", 256, 512, p1=8), R("P5", 256, 512, p1=8), bias=-0.75)
             act(R("o8", 512, 768, p1=8), R("P1", 0, 256, p1=8))
+        done = []
         for b in range(7, -1, -1):
             if b == LWB and not last:
                 ts(R("lw"), R("P7", 96, 144), -1.0, OP.add)
             put_r(b)
-            if nx[0]:
-                shape(16 if b == 0 else XPER[b])
-                if not nx[0] and not last:
+            shape(16 if b == 0 else 1)
+            if not nx[0] and b <= LWB and not done:
+                done.append(b)
+                if not last:
                     prep_q()
-                if not nx[0] and last:
+                else:
                     dma("S", "dout", 16 * 7, T.ym[:], T.ymb[0:8, 0:6], [R("ymb")], [])
                     dma("S", "dout", 16 * 7, T.yc[:], T.o8[0:8, 0:256], [R("o8")], [])
                     dma("S", "dout", 16 * 7, T.yv[:], T.o8[0:8, 256:512], [R("o8")], [])
@@ -653,12 +766,13 @@ def rank_program(g, core, T, topo):
                         act(R("xe", 256 * j, 256 * j + 256), R("X", 256 * j, 256 * j + 256), acc=R("ysb", j, j + 1))
 
     tot = 16 * 7
-    dma("Y", "dout", tot, T.yb[0:64, :], T.Bf[0:64, 0:1024], [R("Bf")], [])
-    dma("Y", "dout", tot, T.yb[64:128, :], T.Bf[64:128, 0:1024], [R("Bf")], [])
+    dma("Y", "dout", tot, T.yb[0:64, :], T.Bf[0:64, 0:1024], [R("Bf")], [], 3500.0)
+    dma("Y", "dout", tot, T.yb[64:128, :], T.Bf[64:128, 0:1024], [R("Bf")], [], 3500.0)
     for b in range(YS, 8):
-        o, i = R("ysb", b, b + 1), R("X", 256 * b, 256 * b + 256)
-        emit("V", [i], [o], lambda: g.vector.tensor_reduce(o[3], i[3], AxisListType.X, OP.add))
+        row_sum(R("ysb", b, b + 1), R("X", 256 * b, 256 * b + 256))
     dma("S", "dout", tot, T.ys[:], T.ysb[:], [R("ysb")], [])
+    for i in order():
+        calls[i][5]()
     g.wait_ge(T.sem.sent, nsent)
     for e in ("V", "S", "P", "G"):
         wait("G", ("s" + e, cnt[e]))

@@ -7,25 +7,45 @@ MAGIC2 = MAGIC * 2048
 OFF = 25.0
 S0 = 66
 S00 = 60
-GD = 8
+GD = 10
+GB = 8
 S1 = 114
 PART = 64
-LATE = 2
-YS = 5
-LATE0 = 11
-MID0 = 6
-LWB = 3
-XPRE = 1
-EARLY = (9, 11, 13, 15)
+YS = 4
+RS = (0, 1)
+RED = ()
+J = 0
+RA = 1
+XH = 0
+QV = 0
+EQV = 1
+TWO = 1
+E16S = 0
+RB = 0
 
-CYCLE, COLUMN = 1.04, 0.52
-GATHER, SCATTER = 1.3, 3.2
-WAKE = 180.0
-FLIGHT = 2200.0
-PASSES = 4
+CYCLE = 1.0
+COLUMN = 0.43
+CALL = 0.0
+START = 50.0
+GATHER = 1.3
+SCATTER = 3.2
+WAKE = 175.0
+SAME = 220.0
+GSLOW = 1.35
+LOAD = 2600.0
+COPY = 900.0
+FLIGHT = 1400.0
+FIRST = 1800.0
+STEP = 20780.0
+QUICK = 9
+SLOW = 120.0
+DUE = {'start': 5620, 'for choice': 7150, 'bounds': 8110, 'tables': 13950, 'own new': 14360, 'side': 17740, 'for rivals': 19890, 'misses': 21400}
+TURNS = {'G': 'start*2 for_sums*2'}
+PASSES = 2
 
 F, B16, I32, U16 = "float32", "bfloat16", "int32", "uint16"
 SCRATCH = {}
+ORDER = []
 
 
 def _sb(name, cols, dtype):
@@ -33,34 +53,34 @@ def _sb(name, cols, dtype):
 
 
 for _n, _c, _d in [
-    ("X", 2080, B16), ("Bi", 1024, I32), ("Bf", 1056, F), ("Bc", 2048, H), ("wf", 16, F), ("rep", 128, H), ("LR", 8, U16), ("Ki", 512, I32), ("Kw", 512, I32), ("Kc", 2048, F), ("KV", 2048, F),
+    ("X", 2080, B16), ("Bi", 1024, I32), ("Bf", 1088, F), ("Bc", 2048, H), ("wf", 16, F), ("rep", 128, H), ("LR", 8, U16), ("Kc", 2048, I32), ("KV", 2048, I32), ("RSr", 320, B16),
     ("l8", 768, I32), ("Y8", 768, H), ("vv", 16, H),
     ("Eu", 256, U16), ("E16", 256, H), ("nAg", 256, H), ("newc", 256, F), ("xe", 4096, B16), ("tt", 4096, F), ("q", 256, B16), ("yy", 256, B16),
     ("kc", 256, F), ("ke", 256, F), ("sx", 256, B16),
     ("r1", 128, F), ("r2", 256, F), ("f2", 256, F), ("key", 256, F), ("ks", 256, F), ("oh", 256, F), ("sl", 256, F), ("ss", 272, F),
-    ("Pi", 16, I32), ("pT", 16, I32), ("parT", 16, I32), ("hd", 40, F), ("misT", 16, B16), ("ac", 8, F),
-    ("dh", 16, H), ("xp", 128, H), ("xs", 128, H), ("xd", 128, H), ("op2", 256, B16), ("m2s", 256, B16), ("Y2", 512, H), ("Y1", 512, H),
+    ("Pi", 16, I32), ("pT", 32, I32), ("hd", 64, B16), ("ah", 2, B16), ("ac", 8, F),
+    ("xp", 128, H), ("xs", 128, H), ("xd", 128, H), ("op2", 256, B16), ("m2s", 256, B16), ("Y2", 512, H), ("Y1", 512, H),
     ("ly", 16, U16), ("lsel", 16, U16), ("lw", 48, U16),
     ("W1", 32, H), ("w2", 16, U16), ("wp", 16, H), ("dW", 16, H), ("hitW", 16, F), ("t1", 16, F), ("t2", 16, F),
-    ("EQ", 512, H), ("EQs", 256, H), ("ab", 256, F), ("oX", 32, U16), ("oO", 32, U16), ("Ag", 256, F), ("Um", 512, F), ("val", 256, B16),
+    ("EQs", 256, H), ("ab", 256, F), ("oX", 32, U16), ("oO", 32, U16), ("Ag", 256, F), ("Um", 512, F), ("val", 256, B16),
     ("o8", 768, F), ("ysb", 8, F), ("ymb", 8, F),
-    ("sc", 16 * ST, F), ("rc", 16 * ST, F), ("so", 16 * ST, H), ("ro", 16 * ST, H),
-    ("crr", 256, F), ("oR", 32, U16), ("MM", 272, F),
-    ("row", 272, F), ("row1", 128, F), ("xg", 128, F), ("xa", 272, F), ("xa1", 128, F),
-    ("pi", 8, I32), ("pc", 24, F),
-    ("Ib", 128, B16), ("Ih", 128, H), ("nIh", 128, H), ("hIh", 128, H), ("pIh", 128, H), ("I2n", 128, H), ("LS", 4, U16), ("I4k", 128, H), ("Isx", 128, B16),
+    ("so", 32 * ST, F), ("ro", 32 * ST, F), ("rx", 768, H), ("rd", 1280, F), ("RM", 952, H), ("nIb", 128, B16),
+    ("crr", 256, F), ("oR", 32, U16), ("MM", 144 + 128 * J, F),
+    ("row", 272, F), ("row1", 128, F), ("xg", 128, F), ("xa", 144 + 128 * J, F), ("xa1", 128 + 128 * J, F),
+    ("pi", 8, I32), ("pc", 32, F),
+    ("Ib", 128, B16), ("Ih", 128, H), ("nIh", 128, H), ("hIh", 128, H), ("pIh", 128, H), ("I2n", 128, H), ("LS", 4 + 4 * J, U16), ("I4k", 128, H), ("Isx", 128, B16),
     ("Iq", 128, B16), ("Ihalf", 128, B16), ("Perm", 128, B16), ("BM", 128, H),
     ("Gq", 256, B16), ("G8", 8, F), ("G32", 32, F), ("Gx", 16, B16), ("Gh", 16, H), ("IN", 128, H), ("Dm", 2048, H), ("Dg", 2048, H), ("s12", 32, F),
-    ("L1", 144, H), ("L2", 240, H), ("L8", 144, H), ("NM", 272, F), ("RST", 128, F), ("CT", 512, H), ("on16", 128, H), ("m8", 128, H), ("cU", 512, B16), ("EQx", 512, H),
+    ("L1", 144, H), ("L2", 240, H), ("L8", 144, H), ("NM", 144 + 128 * J, F), ("RST", 128, F), ("LN", 2, U16), ("zi", 32, F), ("CT", 512, H), ("on16", 128, H), ("m8", 128, H), ("cU", 256, B16), ("EQx", 512, H),
     ("lane", 16, H), ("one", 16, B16),
-    ("LK", 8, U16), ("LT", 16, U16), ("LE", 16, U16),
+    ("LK", 8, U16), ("LT", 16, U16), ("LE", 8, U16),
 ]:
     _sb(_n, _c, _d)
 for _b in range(8):
     SCRATCH["P%d" % _b] = ("psum", [128, 512], F)
 
 SEMAPHORES = (["sV", "sS", "sP", "sG", "sent", "dl", "dx", "db", "dk", "dr1", "dr2", "dout"]
-              + ["ac%d" % _t for _t in range(ST)] + ["ao%d" % _t for _t in range(ST)])
+              + ["a%d" % _t for _t in range(2 * ST)])
 
 
 def rank_program(g, core, T, topo):
@@ -114,12 +134,18 @@ def rank_program(g, core, T, topo):
 
     calls = []
 
+    marks, now = [], [0]
+
+    def part(name, later=0.0):
+        marks.append((len(calls), now[0], name, later))
+
     def emit(e, reads, writes, call, time):
         def issue():
             deps(e, reads, writes)
             cnt[e] += 1
             call().then_inc(T.sem["s" + e], 1)
             note(e, ("s" + e, cnt[e]), reads, writes)
+        time = time * GSLOW if e == "G" else time + CALL if e in "VS" else time
         calls.append((e, reads, writes, time, time + WAKE, issue, None))
 
     def size(r):
@@ -149,7 +175,7 @@ def rank_program(g, core, T, topo):
                         elif (ps and e != e2) or (meet(r, r2) and (w or w2)):
                             for k in group.get(calls[j][6], [j]):
                                 if k != i:
-                                    before[i][k] = calls[k][4]
+                                    before[i][k] = calls[k][3] + SAME if e == e2 and e in "VS" and not calls[k][6] else calls[k][4]
             for regs, w in ((reads, False), (writes, True)):
                 for r in regs:
                     keep = [x for x in past.get(r[0], []) if not (x[1] in before[i] and covers(r, x[0]) and (w or not x[2]))]
@@ -158,6 +184,23 @@ def rank_program(g, core, T, topo):
                 group.setdefault(sem, []).append(i)
             for j in before[i]:
                 after[j].append(i)
+
+        left = {}
+        for (lo, t, name, _), hi in zip(marks, [m[0] for m in marks[1:]] + [n]):
+            for i in range(lo, hi):
+                left.setdefault((t, name.replace(" ", "_"), calls[i][0]), []).append(i)
+        for e, turns in TURNS.items():
+            j = None
+            for t in range(ST + 1):
+                for word in turns.split():
+                    name, _, k = word.partition("*")
+                    line = left.get((t - (name[0] == "-"), name.lstrip("-"), e), [])
+                    for _ in range(min(int(k or 1), len(line))):
+                        i = line.pop(0)
+                        if j is not None and j not in before[i]:
+                            before[i][j] = calls[j][3]
+                            after[j].append(i)
+                        j = i
 
         def place(turn, earliest):
             busy, at = {e: [] for e in Q}, [0.0] * n
@@ -180,8 +223,19 @@ def rank_program(g, core, T, topo):
             time = calls[i][3]
             return max([calls[i][4] - time] + [at[k] + calls[k][3] + before[k][i] - time for k in after[i]])
 
-        back = place(list(range(n - 1, -1, -1)), backward)
-        turn, best = sorted(range(n), key=lambda i: (-back[i] - calls[i][3], i)), None
+        due = [0.0] * n
+        for (lo, t, name, later), hi in zip(marks, [m[0] for m in marks[1:]] + [n]):
+            for i in range(lo, hi):
+                due[i] = STEP * t + DUE.get(name, -30000.0) + later
+        open_, ready = [len(b) for b in before], [i for i in range(n) if not before[i]]
+        for i in ready:
+            due[i] = max(due[i], forward(i, due))
+            for k in after[i]:
+                open_[k] -= 1
+                if not open_[k]:
+                    ready.append(k)
+        assert len(ready) == n
+        turn, best = sorted(range(n), key=lambda i: (due[i], i)), None
         for _ in range(PASSES):
             at = place(turn, forward)
             end = max(at[i] + calls[i][4] for i in range(n))
@@ -222,14 +276,18 @@ def rank_program(g, core, T, topo):
         else:
             emit("V", r + rs, [o], lambda: g.vector.tensor_scalar(o[3], ia, a1, a2, op0, op1), time)
 
-    def scan(o, d0, d1):
-        emit("V", [d0, d1], [o], lambda: g.vector.tensor_tensor_scan(o[3], d0[3], d1[3], 0.0, OP.min, OP.max), span("V", o, [d1], 1.0))
+    def scan(o, d0, d1, op0=OP.min, op1=OP.max):
+        each = 1.0 if wide(o) or wide(d0) or wide(d1) else 0.5
+        emit("V", [d0, d1], [o], lambda: g.vector.tensor_tensor_scan(o[3], d0[3], d1[3], 0.0, op0, op1), span("V", o, [d1], each))
 
     def mset(o, v):
         emit("V", [], [o], lambda: g.vector.memset(o[3], v), span("V", o, [], 1.0 if wide(o) else 0.5))
 
     def row_sum(o, i):
         emit("V", [i], [o], lambda: g.vector.tensor_reduce(o[3], i[3], AxisListType.X, OP.add), span("V", i, [i], 1.0))
+
+    def least(o, i):
+        emit("V", [i], [o], lambda: g.vector.tensor_reduce(o[3], i[3], AxisListType.X, OP.min, apply_absolute_value=True), span("V", i, [i], 1.0))
 
     def act(o, i, fn=AF.Identity, bias=0.0, scale=1.0, acc=None):
         w, r0, oa = outs(o)
@@ -259,12 +317,12 @@ def rank_program(g, core, T, topo):
     def select(o, i, pat, base, cm):
         emit("G", [i], [o], lambda: g.affine_select(o[3], i[3], pat, OP.is_equal, 0.0, base, cm), 210.0 + 2 * CYCLE * size(o))
 
-    def dma(e, sem, total, out_ap, in_ap, reads, writes, time=2000.0):
+    def dma(e, sem, total, out_ap, in_ap, reads, writes, time=COPY):
         def issue():
             deps(e, reads, writes)
             Q[e].dma_start(out_ap, in_ap).then_inc(T.sem[sem], 16)
             note("D", (sem, total), reads, writes)
-        calls.append((e, reads, writes, 50.0, time, issue, sem))
+        calls.append((e, reads, writes, START, time, issue, sem))
 
     def send(reg, rname, sem, dst, src):
         land = R(rname, reg[1], reg[2])
@@ -274,59 +332,75 @@ def rank_program(g, core, T, topo):
             deps("G", [reg], [])
             g.remote_dma(land[3], reg[3], T.sem[sem], T.sem.sent, pid, rid, topo.mask(core, dst))
             note("R", (sem, len(topo.engines(src, core))), [], [land])
-        calls.append(("G", [reg], [land], 300.0, FLIGHT, issue, None))
+        late = FIRST if now[0] == 0 and (J or reg[1] == 16 * HA) else 0.0
+        calls.append(("G", [reg], [land], 300.0 + late, FLIGHT + late, issue, None))
 
     PCOL, ACOL, GCOL, HC, B7, L1C, L2C, L8C, LANEC, DXC, DBC, MC, E0C, E1C = [R("pc", j, j + 1) for j in range(14)]
-    S0C, S1C, DB2, DX2 = [R("pc", j, j + 1) for j in range(16, 20)]
+    S0C, S1C, DX2 = [R("pc", j, j + 1) for j in range(16, 19)]
+    M1, M2, CC, MH = 0, 320, 648, 808
+
+    def run(b):
+        lo = 160 * (b // 4) + 8 * (b % 4) * (b % 4 + 1)
+        return lo, lo + 16 * (b % 4 + 1)
+
+    HA, HB = 1, 0
     C1, C2 = R("pc", 14, 15, p1=16), R("pc", 15, 16, p1=16)
     LOPP, LCW, LOWN, WO, WC = R("lw", 0, 16), R("lw", 16, 32), R("lw", 32, 48), R("W1", 0, 16), R("W1", 16, 32)
     PH = ("P1", "P2")
 
+    part("start")
     dma("Y", "dl", 48, T.l8[0:8, 0:256], T.lv[:], [], [R("l8", 0, 256)])
     dma("S", "dl", 48, T.l8[0:8, 256:512], T.ld[:], [], [R("l8", 256, 512)])
     dma("Y", "dl", 48, T.l8[0:8, 512:768], T.lc[:], [], [R("l8", 512, 768)])
-    dma("S", "db", 16, T.Bi[:], T.bnd[:], [], [R("Bi")], 4500.0)
-    dma("Y", "dx", 16, T.X[:, 0:2048], T.x[:], [], [R("X", 0, 2048)], 4500.0)
-    dma("S", "dk", 16, T.Ki[:], T.kt[:], [], [R("Ki")], 4500.0)
+    dma("S", "db", 16, T.Bi[:], T.bnd[:], [], [R("Bi")], LOAD)
+    dma("Y", "dx", 16, T.X[:, 0:2048], T.x[:], [], [R("X", 0, 2048)], LOAD)
+    dma("Y", "dk", 16, T.Kc[:, 0:512], T.kt[:], [R("Bi")], [R("Kc", 0, 512)], LOAD)
 
     pi = lambda j: R("pi", j, j + 1)
     iota(pi(0), [[0, 1]], 0, 1)
     iota(R("row", 0, 144), [[1, 144]])
+    mset(R("ab", 0, 64), OFF)
+    act(R("Bf", 1024, 1088), R("ab", 0, 64), AF.Silu)
+    cp(PCOL, pi(0))
+    ts(L8C, pi(0), 16.0, OP.mult, 15.0, OP.add)
+    mset(R("X", 2048, 2080), 0.0)
+    mset(R("hd"), 0.0)
+    ts(R("L8", 0, 144), R("row", 0, 144), L8C, OP.is_equal)
+    ts(R("Ih"), R("row", 0, 128), PCOL, OP.is_equal)
+    ts(R("hIh"), R("Ih"), -0.5, OP.mult)
+    ts(R("pIh"), R("Ih"), 0.5, OP.mult)
+    cp(R("LT"), R("row", 0, 16))
+    part("for sums")
     iota(R("xg"), [[1, 8], [0, 16]])
-    iota(R("xa"), [[0, 17], [1, 16]])
-    mset(R("ab", 0, 32), OFF)
-    act(R("Bf", 1024, 1056), R("ab", 0, 32), AF.Silu)
+    iota(R("xa"), [[0, 9 + 8 * J], [1, 16]])
     mset(R("on16", p1=16), 1.0)
     ts(pi(1), pi(0), 15, OP.bitwise_and)
     ts(pi(2), pi(0), 4, OP.arith_shift_right)
     ts(pi(3), pi(0), 8, OP.bitwise_and)
     ts(pi(4), pi(0), 7, OP.bitwise_and)
-    mset(R("X", 2048, 2080), 0.0)
-    cp(R("pc", 0, 5), R("pi", 0, 5))
-    mset(R("hd"), 0.0)
-    ts(L8C, PCOL, 16.0, OP.mult, 15.0, OP.add)
-    ts(R("Ih"), R("row", 0, 128), PCOL, OP.is_equal)
-    ts(R("L8", 0, 144), R("row", 0, 144), L8C, OP.is_equal)
-    ts(R("s12", 16, 32), R("row", 0, 16), ACOL, OP.is_equal)
+    cp(R("pc", 1, 5), R("pi", 1, 5))
     ts(R("G8"), R("row", 0, 8), GCOL, OP.is_equal)
     ts(R("BM"), R("xg"), GCOL, OP.is_equal)
     ts(C1, R("pc", 0, 1, p1=16), 8.0, OP.is_equal, -2048.0, OP.mult)
     ts(C2, R("pc", 0, 1, p1=16), 8.0, OP.is_equal, -1.0 / 4096, OP.mult)
-    ts(R("hIh"), R("Ih"), -0.5, OP.mult)
-    ts(R("pIh"), R("Ih"), 0.5, OP.mult)
+    ts(R("CT", 384, 512, p1=16), R("on16", p1=16), 2040.0, OP.mult, C2, OP.mult)
+    part("for own")
+    ts(R("s12", 16, 32), R("row", 0, 16), ACOL, OP.is_equal)
     ts(R("I2n"), R("Ih"), -2.0, OP.mult)
-    cp(R("LT"), R("row", 0, 16))
     ts(L1C, GCOL, 16.0, OP.mult, 15.0, OP.add)
     ts(R("s12", 0, 16), R("row", 0, 16), ACOL, OP.is_ge)
-    ts(R("CT", 384, 512, p1=16), R("on16", p1=16), 2040.0, OP.mult, C2, OP.mult)
-
     for r in range(GD, 16):
         select(R("Dg", 128 * r, 128 * r + 128), R("Ih"), [[0, 8], [1, 16]], -r, 0)
+    part("for choice")
     iota(R("row", 144, 272), [[1, 128]], 144)
-    iota(R("xa1"), [[0, 8], [2, 8], [-1, 2]], 1)
+    iota(R("xa1"), [[0, 8 + 8 * J], [2, 8], [-1, 2]], 1)
     iota(R("row1"), [[2, 64], [-1, 2]], 1)
+    part("for rivals")
     for a in range(16):
-        select(R("Bc", 128 * a, 128 * a + 128), R("BM"), [[-16, 8], [0, 16]], -a, 1)
+        if a < GB:
+            select(R("Bc", 128 * a, 128 * a + 128), R("BM"), [[-16, 8], [0, 16]], -a, 1)
+        else:
+            act(R("Bc", 128 * a, 128 * a + 128), R("BM"), scale=R("s12", 16 + a, 17 + a))
 
     def Lsl(name, a, p1=128):
         return R(name, 15 - a, 143 - a, p1=p1)
@@ -354,8 +428,11 @@ def rank_program(g, core, T, topo):
             mm(R(bank, 16 * a, 16 * a + 16), R("Dm", 128 * a, 128 * a + 128), w, True, True)
 
     def eq_s(bank="P6"):
-        act(R("ab", 16, 256), R(bank, 16, 256), AF.Abs)
-        act(R("EQs", 16, 256), R("ab", 16, 256), AF.Relu, scale=-4096.0, bias=4096.0)
+        if EQV:
+            ts(R("EQs", 16, 256), R(bank, 16, 256), 0.0, OP.is_equal, 4096.0, OP.mult)
+        else:
+            act(R("ab", 16, 256), R(bank, 16, 256), AF.Abs)
+            act(R("EQs", 16, 256), R("ab", 16, 256), AF.Relu, scale=-4096.0, bias=4096.0)
 
     def losers(out, w, buf, sign=None, stop=True):
         mm(out, R("Ih"), w, True, False)
@@ -367,8 +444,13 @@ def rank_program(g, core, T, topo):
     def offs(o, src, dummy):
         ts(o, src, -1.0, OP.add, dummy, OP.min)
 
-    def put_r(b):
-        tt(ind(R("Bf"), R("oR", 2 * b, 2 * b + 2)), R("Ag", 32 * b, 32 * b + 32), R("crr", 32 * b, 32 * b + 32), OP.add)
+    def put_r(b, exact):
+        o = 16 * (b // 2) + 4 * (b % 2)
+        o = ind(R("Bf"), R("oR", o, o + 4))
+        if exact:
+            tt(o, R("Ag", 64 * b, 64 * b + 64), R("crr", 64 * b, 64 * b + 64), OP.max)
+        else:
+            act(o, R("crr", 64 * b, 64 * b + 64), AF.Silu)
 
     def put_o(b):
         act(ind(R("Bf"), R("oO", 2 * b, 2 * b + 1)), R("newc", 16 * b, 16 * b + 16), AF.Silu)
@@ -376,23 +458,27 @@ def rank_program(g, core, T, topo):
     def put_x(b):
         cp(ind(R("X"), R("oX", 2 * b, 2 * b + 2)), R("val", 32 * b, 32 * b + 32))
 
-    def rivals(w, eq, across, low, high, out, lists, spare):
-        act(R("wf"), w)
-        act(R("rep"), ind(R("wf"), R("LR")))
+    def rivals(h, n, bank, across, out):
+        lo, e = 8 * h, 256 * h
+        w, wf, rep = R("wp", lo, lo + n), R("wf", lo, lo + n), R("rep", 8 * lo, 8 * (lo + n))
+        act(wf, w)
+        act(rep, ind(wf, R("LR", 0, n // 2)))
         for a in range(16):
-            mm(R(across[0], across[1] + a, across[1] + 128, 16), R("Bc", 128 * a, 128 * a + 128), R(w[0], w[1], w[2], 2), True, True)
+            mm(R(bank, across + a, across + 8 * n, 16), R("Bc", 128 * a, 128 * a + 128), R("wp", lo, lo + n, 2), True, True)
         for a in range(1, 16):
-            mm(R(low if a < 9 else high, 16 * a, 16 * a + 16), R("Dm", 128 * a, 128 * a + 128), w, True, True)
-        tt(R(eq, 256, 384), R("rep"), R(across[0], across[1], across[1] + 128), OP.is_equal)
-        ts(R(eq, 16, 144), R(low, 16, 144), 0.0, OP.is_equal, 4096.0, OP.mult)
-        scan(R(eq, 384, 512), R("RST"), R(eq, 256, 384))
-        ts(R(eq, 144, 256), R(high, 144, 256), 0.0, OP.is_equal, 4096.0, OP.mult)
-        losers(R(out[0], out[1], out[1] + 16), w, eq, stop=False)
-        mm(R(out[0], out[1] + 1, out[1] + 16, 2), R("I4k"), R(eq, 399, 512, 16), False, True)
-        return [lambda j=j: offs(R(lists, j, 16, 2), R(out[0], out[1] + j, out[1] + 16, 2), spare[j]) for j in range(2)]
+            mm(R(bank, n * a, n * a + n), R("Dm", 128 * a, 128 * a + 128), w, True, True)
+        tt(R("EQx", e + 16 * n, e + 24 * n), rep, R(bank, across, across + 8 * n), OP.is_equal)
+        ts(R("EQx", e + n, e + 16 * n), R(bank, n, 16 * n), 0.0, OP.is_equal, 4096.0, OP.mult)
+        scan(R("EQx", e + 24 * n, e + 32 * n), R("RST", 0, 8 * n), R("EQx", e + 16 * n, e + 24 * n))
+        mm(R(bank, out, out + n), R("Ih"), w, True, False)
+        for a in range(1, 16):
+            mm(R(bank, out, out + n), Lsl("L1", a), R("EQx", e + n * a, e + n * a + n), False, False)
+        mm(R(bank, out + 1, out + n, 2), R("I4k"), R("EQx", e + 24 * n + 15, e + 32 * n, 16), False, True)
+        for j, spare in enumerate((DXC, DX2)):
+            offs(R("oX", lo + j, lo + n, 2), R(bank, out + j, out + n, 2), spare)
 
-    def side():
-        act(R("sx"), ind(R("hd", 16, 32), R("LT")), scale=1.0 / 256, bias=-1.0 / 512)
+    def side(lo=0, hi=16):
+        act(R("sx", 16 * lo, 16 * hi), ind(R("hd", 32, 48), R("LT", lo, hi)), scale=1.0 / 256, bias=-1.0 / 512)
 
     def open_sums():
         for h in range(2):
@@ -400,11 +486,13 @@ def rank_program(g, core, T, topo):
             mm(R(PH[h], 0, 128), R("Isx"), R("sx", 128 * h, 128 * h + 128), False, False)
 
     def prep_q():
-        act(R("q"), ind(R("X"), LCW))
-        mm(R("P0", 0, 256), R("Ib"), R("q"), True, False)
-        for h in range(2):
-            mm(R("P0", 128 * h, 128 * h + 128), R("sx", 128 * h, 128 * h + 128), R("Ib"), False, h == 1)
-        for h in range(2):
+        (cp if QV else act)(R("q"), ind(R("X"), LCW))
+        for j in range(2 * TWO):
+            h = j // TWO
+            mm(R("P0", 128 * TWO * h + j % TWO, 128 * TWO * (h + 1), TWO), R("sx", 128 * h, 128 * h + 128), R("Ib"), j == 0, False)
+        for j in range(TWO):
+            mm(R("P0", j, 256 * TWO, TWO), R("Ib"), R("q"), False, j == TWO - 1)
+        for h in (HA, HB):
             mm(R(PH[h], 256, 512), R("q", 128 * h, 128 * h + 128), R("Gq"), False, False)
 
     def next_lists():
@@ -412,11 +500,20 @@ def rank_program(g, core, T, topo):
         mm(R("P7", 128, 144), R("Ih"), WO, True, False)
         mm(R("P7", 128, 144), R("Ih"), R("dW"), False, True)
 
+    part("start")
     cp(R("Y8", 0, 512, p1=8), R("l8", 0, 512, p1=8))
-    act(R("Y8", 512, 768, p1=8), R("l8", 512, 768, p1=8), bias=1.0)
+    ts(R("Y8", 512, 768, p1=8), R("l8", 512, 768, p1=8), 1.0, OP.add)
     y_to_w(R("P7", 80, 128), "Y8", 0, 768, True, True, "L8", 8)
     for h in range(2):
         mm(R("P6", 304 + 8 * h, 312 + 8 * h), R("Y8", 256 + 128 * h, 384 + 128 * h, p1=8), R("Ih", 0, 8, p1=8), True, True)
+    ts(R("vv"), R("P7", 80, 96), 2.0, OP.mult, 1.5, OP.add)
+    ts(R("dW"), R("P7", 96, 112), 2.0, OP.mult, -1.0, OP.add)
+    cp(R("hd", 32, 48), R("P6", 304, 320))
+    for (lo, I) in ((96, "hIh"), (128, "pIh")):
+        mm(R("P7", lo, lo + 16), R("Ih"), R("vv"), True, False)
+        mm(R("P7", lo, lo + 16), R(I), R("dW"), False, True)
+    ts(R("lw"), R("P7", 96, 144), -1.0, OP.add)
+    part("for sums")
     act(R("Ib"), R("Ih"))
     act(R("Isx"), R("Ih"), scale=-262144.0)
     act(R("Gq", 0, 128), R("BM"), scale=-1.0 / 256)
@@ -425,6 +522,12 @@ def rank_program(g, core, T, topo):
         act(R("G32", 8 * j, 8 * j + 8), R("G8"), scale=s)
     act(R("Gx", 0, 8), R("G8"), scale=-1.0 / 256)
     act(R("Gx", 8, 16), R("G8"), scale=1.0 / 4096)
+    xa16 = R("xa", 0, 128, p1=16)
+    ts(R("CT", 0, 128, p1=16), xa16, -15.015625, OP.add, C1, OP.mult)
+    ts(R("CT", 128, 256, p1=16), xa16, -15.0, OP.add, C2, OP.mult)
+    ts(R("CT", 256, 384, p1=16), xa16, 2.0, OP.add, C2, OP.mult)
+    part("for own")
+    act(R("W1"), R("P7", 96, 128))
     act(R("nIh"), R("Ih"), scale=-1.0)
     for r in range(GD):
         act(R("Dg", 128 * r, 128 * r + 128), R("Ih"), scale=R("s12", 16 + r, 17 + r))
@@ -435,59 +538,45 @@ def rank_program(g, core, T, topo):
             ts(R("Dm", 128 * a, 128 * a + 128), R("IN"), R("s12", a, a + 1), OP.mult, R("s12", 16 + a, 17 + a), OP.min)
 
     tt(R("IN"), R("BM"), R("I2n"), OP.add)
-    xa16 = R("xa", 0, 128, p1=16)
-    ts(R("CT", 0, 128, p1=16), xa16, -15.015625, OP.add, C1, OP.mult)
-    ts(R("CT", 128, 256, p1=16), xa16, -15.0, OP.add, C2, OP.mult)
-    ts(R("CT", 256, 384, p1=16), xa16, 2.0, OP.add, C2, OP.mult)
-    consts_d(1, 4)
-    ts(R("vv"), R("P7", 80, 96), 2.0, OP.mult, 1.5, OP.add)
-    ts(R("dW"), R("P7", 96, 112), 2.0, OP.mult, -1.0, OP.add)
-    cp(R("hd", 16, 32), R("P6", 304, 320))
-    for (lo, I) in ((96, "hIh"), (128, "pIh")):
-        mm(R("P7", lo, lo + 16), R("Ih"), R("vv"), True, False)
-        mm(R("P7", lo, lo + 16), R(I), R("dW"), False, True)
+    consts_d(1, 10)
+    part("for sums")
     side()
-    consts_d(4, 10)
-    ts(R("lw"), R("P7", 96, 144), -1.0, OP.add)
-    act(R("W1"), R("P7", 96, 128))
     open_sums()
 
-    def table(s, src, scale, bias, sem):
-        act(R(s, 0, 512), R(src), scale=scale, bias=bias)
+    def table(s, sem):
         for j in range(1, 4):
             dma("Y", sem, 48, T[s][:, 512 * j:512 * j + 512], T[s][:, 0:512], [R(s, 0, 512)], [R(s, 512 * j, 512 * j + 512)])
 
-    def consts_choice(own):
-        own(1)
-        act(R("RST"), R("xa", 0, 128), scale=1.0e8, bias=-5.0e7)
+    def consts_choice():
+        act(R("RST", 0, 128), R("xa", 0, 128), scale=1.0e8, bias=-5.0e7)
+        act(R("Gh", 0, 8), R("G8"))
+        act(R("nIb"), R("Ib"), scale=-1.0)
         act(L2C, ACOL, bias=112.0)
-        own(1)
-        act(LANEC, ACOL, bias=128.0)
-        act(S0C, HC, scale=2.0, bias=-113.0)
-        act(E0C, HC, bias=-32.0)
-        own(1)
+        act(LANEC, ACOL, bias=64.0)
+        act(S0C, HC, scale=16.0 if J else 2.0, bias=-241.0 if J else -113.0)
+        act(E0C, HC, bias=-16.0)
         ts(MC, B7, GCOL, OP.is_equal)
         ts(R("LK"), R("row", 0, 8), 16.0, OP.mult, 15.0, OP.add)
-        mset(R("ss", 128, 136), 0.0)
-        mset(R("ss", 264, 272), 0.0)
+        if J:
+            mset(R("ss", 256, 272), 0.0)
+        else:
+            mset(R("ss", 128, 136), 0.0)
+            mset(R("ss", 264, 272), 0.0)
         mset(R("one"), 1.0)
-        act(E0C, E0C, scale=MC, bias=32.0)
-        act(S0C, S0C, scale=MC, bias=128.0)
-        act(S1C, MC, scale=32.0)
-        own(1)
-        act(E1C, MC, scale=16.0, bias=E0C)
-        act(R("lane"), R("row", 0, 16), scale=16.0, bias=LANEC)
+        act(E0C, E0C, scale=MC, bias=16.0)
+        act(S0C, S0C, scale=MC, bias=256.0 if J else 128.0)
+        act(S1C, MC, scale=16.0 if J else 32.0)
+        for h in range(2):
+            act(R("lane", 8 * h, 8 * h + 8), R("row", 0, 8), scale=16.0, bias=LANEC)
         act(R("Iq"), R("Ib"), scale=-0.25)
         act(R("Ihalf"), R("Ib"), scale=0.5)
-        own(1)
 
     def consts_lists():
         ts(R("L2"), R("row", 0, 240), L2C, OP.is_equal)
         ts(R("LE", 0, 8), R("row", 0, 8), MC, OP.mult, E0C, OP.add)
-        mset(R("cU", 0, 256), 0.375)
-        mset(R("cU", 256, 512), -0.25)
-        ts(R("LE", 8, 16), R("row", 0, 8), MC, OP.mult, E1C, OP.add)
-        ts(R("LS"), R("row", 0, 4), S1C, OP.mult, S0C, OP.add)
+        mset(R("cU", 0, 128), 0.375)
+        mset(R("cU", 128, 256), -0.25)
+        ts(R("LS"), R("row", 0, 4 + 4 * J), S1C, OP.mult, S0C, OP.add)
 
     def consts_late():
         ts(R("Perm"), R("row1"), PCOL, OP.is_equal)
@@ -496,14 +585,47 @@ def rank_program(g, core, T, topo):
         ts(R("m8", p1=8), R("xg", p1=8), R("pc", 0, 1, p1=8), OP.is_equal, 64.0, OP.mult)
         ts(DXC, ACOL, 2048.0, OP.add)
         ts(DX2, ACOL, 2064.0, OP.add)
-        ts(DB2, ACOL, 1040.0, OP.add)
         act(R("I4k"), R("Ih"), scale=4096.0)
         ts(R("LR"), R("row", 0, 8), 2.0, OP.mult, 1.0, OP.add)
 
-    def open_values():
-        mm(R("P3"), R("Ib"), R("cU"), True, False)
-        mm(R("P3", 0, 256), R("Iq"), R("q"), False, False)
-        mm(R("P3", 256, 512), R("Ihalf"), R("q"), False, False)
+    def consts_received():
+        GE, SP = R("zi", 8, 24), R("zi", 24, 28)
+        mset(R("RM", M1, M1 + 320), 0.0)
+        act(R("zi", 0, 8), R("G8"), scale=-4096.0)
+        ts(GE, R("row", 0, 16), ACOL, OP.is_ge, 2048.0, OP.mult)
+        ts(SP, R("row", 0, 4), 16.0, OP.mult, ACOL, OP.add)
+        mset(R("zi", 23, 24), 1088.0)
+        for b in range(8):
+            lo, hi = run(b)
+            cp(R("RM", M1 + lo, M1 + hi - 1), R("I4k", 64 * (b // 4), 64 * (b // 4) + hi - lo - 1))
+            act(R("RM", M2 + lo, M2 + hi), R("xa", 0, hi - lo), scale=0.0, bias=R("zi", b, b + 1))
+        for u in range(4):
+            lo, hi = run(u)
+            act(R("RM", M2 + hi - 1, M2 + 320, 160), R("G8", u, 8, 4), scale=-1.0)
+            if u:
+                act(R("RM", CC + lo, CC + hi - 16), R("xa", 0, hi - lo - 16), scale=0.0, bias=R("zi", 24 + u, 25 + u))
+            ts(R("RM", CC + hi - 16, CC + hi), GE, R("zi", 24 + u, 25 + u), OP.max)
+        act(R("RM", MH, MH + 144), R("NM", 0, 144), scale=-4096.0, bias=OFF - 1.0)
+        mset(R("RSr"), 0.0)
+        for u in range(4):
+            mset(R("RSr", run(u)[0], 320, 160), 4096.0)
+        U, C4, Z = [R("zi", j, j + 1) for j in range(28, 31)]
+        ts(pi(5), pi(0), 3, OP.bitwise_and)
+        ts(pi(6), pi(0), 4, OP.bitwise_and)
+        cp(R("zi", 28, 30), R("pi", 5, 7))
+        act(Z, U, scale=8.0, bias=24.0)
+        act(C4, C4, scale=40.0, bias=15.0)
+        ts(R("LN", 0, 1), Z, U, OP.mult, C4, OP.add)
+
+    def values(h):
+        o, q, y = 256 * h, R("q", 128 * h, 128 * h + 128), R("yy", 128 * h, 128 * h + 128)
+        mm(R("P3", o, o + 256), R("Ib"), R("cU"), True, False)
+        mm(R("P3", o, o + 128), R("Iq"), q, False, False)
+        mm(R("P3", o + 128, o + 256), R("Ihalf"), q, False, False)
+        mm(R("P3", o, o + 128), R("Ib"), y, False, False)
+        mm(R("P3", o + 128, o + 256), R("Ihalf"), y, False, True)
+        act(R("Um", o, o + 256), R("P3", o, o + 256), bias=MAGIC)
+        act(R("val", 128 * h, 128 * h + 128), ind(R("Um", o, o + 256), R("lsel", 8 * h, 8 * h + 8)), AF.Abs, bias=-MAGIC)
 
     nsent = 0
     for t in range(ST):
@@ -513,26 +635,38 @@ def rank_program(g, core, T, topo):
         neng = len(topo.engines(core, dst))
 
         BT, boff = (R("Bi"), 0.0) if t == 0 else (R("Bf"), OFF)
-        ts(R("Eu", 0, 128), ind(BT, R("lw", 0, 8)), 0.25 - boff, OP.add)
+        a0, b0 = 128 * HA, 128 * HB
+        now[0] = t
+        part("bounds")
+        ts(R("Eu", a0, a0 + 128), ind(BT, R("lw", 8 * HA, 8 * HA + 8)), 0.25 - boff, OP.add)
         s0, s1 = (S00, 128) if t == 0 else (S0, S1)
         if t == 0:
             prep_q()
+        part("own old" if t else "first own")
         act(R("nAg"), ind(BT, LOWN), scale=-1.0, bias=boff - 1.0)
-        act(R("xe", 0, 16 * s0), ind(R("X"), R("Eu", 0, s0)))
-        ts(R("Eu", 128, 256), ind(BT, R("lw", 8, 16)), 0.25 - boff, OP.add)
+        part("rows a")
+        act(R("xe", 16 * a0, 16 * (a0 + s0)), ind(R("X"), R("Eu", a0, a0 + s0)))
+        part("bounds", 200)
+        ts(R("Eu", b0, b0 + 128), ind(BT, R("lw", 8 * HB, 8 * HB + 8)), 0.25 - boff, OP.add)
+        part("bounds", 430)
+        cp(R("xe", 16 * (a0 + s0), 16 * a0 + 2048), ind(R("X"), R("Eu", a0 + s0, a0 + 128)))
+        part("rows b")
+        act(R("xe", 16 * b0, 16 * (b0 + s1)), ind(R("X"), R("Eu", b0, b0 + s1)))
+        part("own old" if t else "first own")
         if t == 0:
             consts_d(10, 16)
             ts(R("L1"), R("row", 0, 144), L1C, OP.is_equal)
             diff(WO)
-        cp(R("xe", 16 * s0, 2048), ind(R("X"), R("Eu", s0, 128)))
-        old_rows(t)
-        act(R("xe", 2048, 2048 + 16 * s1), ind(R("X"), R("Eu", 128, 128 + s1)))
-        act(R("E16"), ind(BT, LOPP), bias=1.0 - boff)
-        if t == 0:
-            ts(R("EQs", 16, 256), R("P6", 16, 256), 0.0, OP.is_equal, 4096.0, OP.mult)
+            eq_s()
             ts(DBC, ACOL, 1024.0, OP.add)
+        old_rows(t)
+        part("number")
+        if E16S:
+            act(R("E16"), ind(BT, LOPP), bias=1.0 - boff)
         else:
-            act(R("newc"), R("P5", 0, 256), bias=OFF - 1.0)
+            ts(R("E16"), R("Eu"), 1.0, OP.add)
+        part("own new")
+        act(R("newc"), R("P5", 0, 256), bias=OFF - 1.0)
 
         kind = lambda h, j, lo, hi: R(PH[h], 128 * j + lo, 128 * j + hi)
         sb = lambda n, h, lo, hi: R(n, 128 * h + lo, 128 * h + hi)
@@ -544,73 +678,62 @@ def rank_program(g, core, T, topo):
             lambda h, lo, hi: scan(sb("ks", h, lo, hi), R("RST", lo, hi), sb("key", h, lo, hi)),
             lambda h, lo, hi: tt(sb("oh", h, lo, hi), ind(sb("ks", h, lo, hi), R("LK", 0, (hi - lo) // 16)), sb("key", h, lo, hi), OP.is_equal),
             lambda h, lo, hi: tt(sb("sl", h, lo, hi), sb("oh", h, lo, hi), kind(h, 3, lo, hi), OP.mult),
-            lambda h, lo, hi: scan(R("ss", 136 * h + lo, 136 * h + hi), R("RST", lo, hi), sb("sl", h, lo, hi)),
+            lambda h, lo, hi: scan(R("ss", (136 - 8 * J) * h + lo, (136 - 8 * J) * h + hi), R("RST", lo, hi), sb("sl", h, lo, hi)),
         ]
 
         def sum_x(h, k):
             mm(R(PH[h], 256 + k, 512, 16), R("xe", 2048 * h + k, 2048 * h + 2048, 16), R("Gx"), False, False)
 
         def rows(h, k):
-            o = 2048 * h + 128 * k
-            tt(R("tt", o, o + 128), R("xe", 2048 * h + k, 2048 * h + 2048, 16), R("P0", 128 * h, 128 * h + 128), OP.min)
-            if h == 1:
+            n, k = k, k // TWO + 16 // TWO * (k % TWO)
+            o, w = 2048 * h + 128 * (n - n % TWO), 128 * TWO
+            if n % TWO == 0:
+                tt(R("tt", o, o + w), R("xe", 2048 * h + k, 2048 * h + 2048, 16 // TWO), R("P0", w * h, w * h + w), OP.min)
+            if h == HB:
                 sum_x(h, k)
-            mm(R(PH[h], k, 512, 16), R("tt", o, o + 128), R("G32"), False, False)
-            if h == 1 and k in (1, 15):
-                hh = k // 15
+            mm(R(PH[h], k, 512, 16), R("tt", o + n % TWO, o + w, TWO), R("G32"), False, False)
+            if h == HB and n in (1, 15):
+                hh = HA if n == 1 else HB
                 mm(R(PH[hh], 384, 512), R("E16", 128 * hh, 128 * hh + 128), R("Ih"), False, True)
-            if h == 1 and k == 1:
-                own(2 if t else 0)
-                act(R("r1"), R("P1", 0, 128), bias=MAGIC2)
-                if t:
-                    own(1)
-                else:
-                    act(R("newc"), R("P5", 0, 256), bias=OFF - 1.0)
-                act(R("r2", 0, 128), R("r1"), bias=-MAGIC2)
 
-        nb = [16]
-
-        def own(n=1):
-            for _ in range(min(n, nb[0])):
-                nb[0] -= 1
-                put_o(nb[0])
-
+        part("min a")
         for k in range(16):
-            sum_x(0, k)
+            sum_x(HA, k)
+        for k in range(16):
+            part("min a", 133 * k)
+            rows(HA, k)
+        part("rest b")
+        if s1 < 128:
+            cp(R("xe", 16 * (b0 + s1), 16 * b0 + 2048), ind(R("X"), R("Eu", b0 + s1, b0 + 128)))
+        for k in range(16):
+            part("min b", 133 * k + SLOW * max(0, k - QUICK))
+            rows(HB, k)
+        part("tables")
         if t == 0:
             losers(R("P4", 320, 336), WO, "EQs", "dW")
-        for k in range(16):
-            rows(0, k)
-            if t == 0 and k == 11:
-                ts(R("Kw"), R("Ki"), 511, OP.bitwise_and)
-        if t == 0:
-            table("KV", "Kw", 2.0, 1.5, "dr2")
-        else:
-            cp(R("xe", 2048 + 16 * s1, 4096), ind(R("X"), R("Eu", 128 + s1, 256)))
-        for k in range(16):
-            if k == 0:
-                offs(R("oO", 0, 32, 2), R("P4", 320, 336), DBC)
-            rows(1, k)
-            if k == 1 and t == 0:
-                table("Kc", "Ki", 1.0, 1.0, "dr1")
-                consts_choice(lambda n: None)
-                act(R("Bf", 0, 1024), R("Bi"), bias=OFF)
-            if k in EARLY:
-                stage[1 + EARLY.index(k)](0, 0, 128)
-        if t == 0:
+            ts(R("KV", 0, 512), R("Kc", 0, 512), 511, OP.bitwise_and)
+            table("KV", "dr2")
+            table("Kc", "dr1")
+            consts_choice()
+            act(R("Bf", 0, 1024), R("Bi"), bias=OFF)
             consts_lists()
-            own(nb[0] - LATE0)
-        else:
-            own(1)
-            act(R("kc"), ind(R("Kc"), LCW))
-            own(nb[0] - LATE)
-        open_values()
+            consts_late()
+            consts_received()
+        part("own list")
+        offs(R("oO", 0, 32, 2), R("P4", 320, 336), DBC)
+        part("own put")
+        for b in range(15, -1, -1):
+            put_o(b)
+        part("kc")
+        act(R("kc"), ind(R("Kc"), LCW), bias=1.0)
+        part("open values")
         mm(R("P6", 256, 272), R("Ih"), R("lane"), True, False)
+        EW = {HA: R("P5", 352, 360), HB: R("P7", 0, 8)}
 
         def chosen(h):
             ts(R("xp", 64 * h, 64 * h + 64), ind(R("ss", 136 * h, 136 * h + 136), R("LS")), MAGIC, OP.add, MAGIC, OP.subtract)
             for gg in range(8):
-                mm(R("P7", 8 * h, 8 * h + 8), R("L2", 112 - 16 * gg, 240 - 16 * gg), R("xp", 64 * h + 8 * gg, 64 * h + 8 * gg + 8), gg == 0, gg == 7)
+                mm(EW[h], R("L2", 112 - 16 * gg, 240 - 16 * gg), R("xp", 64 * h + 8 * gg, 64 * h + 8 * gg + 8), gg == 0, gg == 7)
 
         def payload(h):
             ts(R("Pi", 8 * h, 8 * h + 8), R("ss", 136 * h + 15, 136 * h + 128, 16), 4096.0, OP.mult, 2040.125, OP.add)
@@ -619,10 +742,69 @@ def rank_program(g, core, T, topo):
             ts(R("pT", 8 * h, 8 * h + 8), R("Pi", 8 * h, 8 * h + 8), 15, OP.bitwise_and)
 
         def e_list(h):
-            ts(R("ly", 8 * h, 8 * h + 8), R("P7", 8 * h, 8 * h + 8), -1.0, OP.add)
-            act(R("ke", 128 * h, 128 * h + 128), ind(R("KV"), R("ly", 8 * h, 8 * h + 8)))
+            ts(R("ly", 8 * h, 8 * h + 8), EW[h], -1.0, OP.add)
+            act(R("ke", 128 * h, 128 * h + 128), ind(R("KV"), R("ly", 8 * h, 8 * h + 8)), scale=2.0, bias=1.5)
 
-        MK = (R("P4", 0, 128), R("P0", 128, 256))
+        MK = {HA: R("P4", a0, a0 + 128), HB: R("P0", b0, b0 + 128)}
+        OUT = {HA: ("P5", 336), HB: ("P7", 16)}
+        IN = {HA: "P5", HB: PH[HB]}
+        M1B = {HA: "P4", HB: "P0"}
+        s = (5 * t) % 16
+
+        def parity(h):
+            ts(R("pT", 16 + 8 * h, 24 + 8 * h), R("Pi", 8 * h, 8 * h + 8), 1, OP.bitwise_and)
+
+        def flip(h):
+            d = R("hd", 32 + 8 * h, 40 + 8 * h)
+            tt(d, d, R("pT", 16 + 8 * h, 24 + 8 * h), OP.not_equal)
+
+        def post(h):
+            bank, lo = OUT[h]
+            col, slot = R(bank, lo, lo + 8), R("so", 32 * t + 16 * h, 32 * t + 16 * h + 16)
+            mm(col, R("Ihalf"), R("one", 0, 8), True, False)
+            mm(col, R("nIb"), R("hd", 32 + 8 * h, 40 + 8 * h), False, False)
+            mm(R(bank, lo + 8, lo + 16), R("Y2", 128 * h, 128 * h + 128), R("Gh", 0, 8), False, False)
+            mm(col, R("Y2", 256 + 128 * h, 384 + 128 * h), R("Gh", 0, 8), False, True)
+            act(slot, R(bank, lo, lo + 16))
+            send(slot, "ro", "a%d" % (2 * t + h), dst, src)
+
+        def received(h):
+            lo, bank = 32 * t + 16 * h, IN[h]
+            col = ind(R("ro", lo, lo + 8), R("LT", 0, 8))
+            own_, al, cc = [R("rx", 384 * h + 128 * j, 384 * h + 128 * j + 128) for j in range(3)]
+            rows_ = R(bank, 384, 512)
+            tt(own_, col, R("MM", 0, 128), OP.mult)
+            act(R("rx", 384 * h + 128, 384 * h + 384), ind(R("ro", lo, lo + 16), R("LT")))
+            lst = R("w2", 8 * h, 8 * h + 8)
+            for c in range(2):
+                mm(R(bank, 160 * c, 160 * c + 160), R("Ih"), R("RM", CC, CC + 160), c == 0, False)
+            mm(rows_, R("Ih"), R("RM", MH + s, MH + s + 128), False, False)
+            if h == HB:
+                mm(R("P7", 32, 40), own_, R("Gh", 0, 8), True, True)
+                ts(lst, R("P7", 32, 40), -1.0, OP.add)
+            mm(R(bank, 0, 320), own_, R("RM", M2, M2 + 320), False, False)
+            mm(R(bank, 0, 320), al, R("RM", M1, M1 + 320), False, False)
+            if h == HA:
+                mm(R(bank, 320, 328), own_, R("Gh", 0, 8), False, False)
+            mm(rows_, cc, R("Ih"), False, True)
+            if h == HA:
+                ts(lst, R(bank, 320, 328), -1.0, OP.add)
+            tt(R("Ag", 128 * h, 128 * h + 128), ind(R("Bf"), lst), R("NM", s, s + 128), OP.mult)
+            size_, low = R("rd", 640 * h, 640 * h + 320), R("rd", 640 * h + 320, 640 * h + 640)
+            exact = last or h not in RS
+            if h not in RED:
+                act(size_, R(bank, 0, 320), AF.Abs)
+            if not exact:
+                tt(R("crr", 128 * h, 128 * h + 128), R("Ag", 128 * h, 128 * h + 128), rows_, OP.max)
+            if h in RED:
+                for b in range(7, -1, -1):
+                    least(R("rd", 640 * h + b, 640 * h + b + 1), R(bank, *run(b)))
+                ts(R("oR", 16 * h, 16 * h + 8), R("rd", 640 * h, 640 * h + 8), -1.0, OP.mult, 1087.0, OP.add)
+            else:
+                scan(low, R("RSr"), size_, OP.max, OP.min)
+                ts(R("oR", 16 * h, 16 * h + 16), ind(low, R("LN", 0, 1)), -1.0, OP.mult, 1087.0, OP.add)
+            if exact:
+                act(R("crr", 128 * h, 128 * h + 128), rows_)
 
         def mask(h):
             o = R("op2", 128 * h, 128 * h + 128)
@@ -632,138 +814,209 @@ def rank_program(g, core, T, topo):
         def pick(h, lo, k):
             tt(R("Y2", lo + 128 * h, lo + 128 * h + 128), R(k, 128 * h, 128 * h + 128), MK[h], OP.mult)
 
-        rest = [lambda j=j: stage[j](0, 0, 128) for j in range(1 + len(EARLY), 8)]
-        rest += [lambda: chosen(0), lambda: payload(0), lambda: None, lambda: e_list(0), lambda: low_bits(0)]
-        for j in range(8):
-            if rest:
-                rest.pop(0)()
+        def pair(h):
+            for f in (payload, chosen, low_bits, parity, mask, flip, e_list, place_of):
+                f(h)
+            pick(h, 0, "kc")
+            pick(h, 256, "ke")
+            post(h)
+
+        def place_of(h):
+            tt(R("t1", 8 * h, 8 * h + 8), EW[h], R("W1", 16 + 8 * h, 24 + 8 * h), OP.subtract)
+
+        def first(h):
+            lo, hi = 128 * h, 128 * h + 128
+            m1 = R(M1B[h], 256 + lo, 256 + hi)
+            act(R("m2s", lo, hi), MK[h])
+            mm(m1, R("Perm"), R("m2s", lo, hi), True, True)
+            tt(R("Y1", lo, hi), R("ke", lo, hi), m1, OP.mult)
+            tt(R("Y1", 256 + lo, 256 + hi), R("kc", lo, hi), m1, OP.mult)
+
+        def pair_all():
+            col, slot = R("P7", 16, 32), R("so", 32 * t, 32 * t + 32)
+            ts(R("Pi"), R("ss", 15, 256, 16), 4096.0, OP.mult, 2040.125, OP.add)
+            ts(R("xp"), ind(R("ss"), R("LS")), MAGIC, OP.add, MAGIC, OP.subtract)
+            t_to_w(R("P7", 0, 16), "xp", True)
+            ts(R("pT", 0, 16), R("Pi"), 15, OP.bitwise_and)
+            ts(R("pT", 16, 32), R("Pi"), 1, OP.bitwise_and)
+            tt(R("op2"), ind(R("pT", 0, 16), R("LT", 0, 16)), R("xa1"), OP.is_equal)
+            for bank in ("P0", "P4"):
+                for h in range(2):
+                    mm(R(bank, 128 * h, 128 * h + 128), R("op2", 128 * h, 128 * h + 128), R("Ib"), True, True)
+            tt(R("hd", 32, 48), R("hd", 32, 48), R("pT", 16, 32), OP.not_equal)
+            ts(R("ly"), R("P7", 0, 16), -1.0, OP.add)
+            act(R("ke"), ind(R("KV"), R("ly")), scale=2.0, bias=1.5)
+            tt(R("t1"), R("P7", 0, 16), WC, OP.subtract)
+            tt(R("Y2", 0, 256), R("kc"), R("P0", 0, 256), OP.mult)
+            tt(R("Y2", 256, 512), R("ke"), R("P0", 0, 256), OP.mult)
+            mm(col, R("Ihalf"), R("one"), True, False)
+            mm(col, R("nIb"), R("hd", 32, 48), False, False)
+            for j in range(4):
+                o = 32 - 16 * (j // 2) + 8 * (j % 2)
+                mm(R("P7", o, o + 8), R("Y2", 128 * j, 128 * j + 128), R("Gh", 0, 8), False, j == 3)
+            act(slot, R("P7", 16, 48))
+            send(slot, "ro", "a%d" % (2 * t), dst, src)
+
+        def first_all():
+            act(R("m2s"), R("P4", 0, 256))
+            mm(R("P4", 256, 512), R("Perm"), R("m2s"), True, True)
+            tt(R("Y1", 0, 256), R("ke"), R("P4", 256, 512), OP.mult)
+            tt(R("Y1", 256, 512), R("kc"), R("P4", 256, 512), OP.mult)
+
+        def received_all():
+            lo, exact = 32 * t, last
+            tt(R("rx", 0, 256), ind(R("ro", lo, lo + 16), R("LT", 0, 16)), R("MM", 0, 256), OP.mult)
+            for j in range(2):
+                act(R("rx", 256 + 256 * j, 512 + 256 * j), ind(R("ro", lo + 16 * j, lo + 16 * j + 16), R("LT", 0, 16)))
+            for h in (HA, HB):
+                for c in range(2):
+                    mm(R(IN[h], 160 * c, 160 * c + 160), R("Ih"), R("RM", CC, CC + 160), c == 0, False)
+                mm(R(IN[h], 384, 512), R("Ih"), R("RM", MH + s, MH + s + 128), False, False)
+            for h in range(2):
+                mm(R("P7", 48 + 8 * h, 56 + 8 * h), R("rx", 128 * h, 128 * h + 128), R("Gh", 0, 8), True, True)
+            ts(R("w2"), R("P7", 48, 64), -1.0, OP.add)
+            tt(R("Ag"), ind(R("Bf"), R("w2")), R("NM", s, s + 256), OP.mult)
+            for h in (HA, HB):
+                part("in a" if h == HA else "in b")
+                bank, rows_ = IN[h], R(IN[h], 384, 512)
+                mm(R(bank, 0, 320), R("rx", 128 * h, 128 * h + 128), R("RM", M2, M2 + 320), False, False)
+                mm(R(bank, 0, 320), R("rx", 256 + 128 * h, 384 + 128 * h), R("RM", M1, M1 + 320), False, False)
+                mm(rows_, R("rx", 512 + 128 * h, 640 + 128 * h), R("Ih"), False, True)
+                size_, low = R("rd", 640 * h, 640 * h + 320), R("rd", 640 * h + 320, 640 * h + 640)
+                act(size_, R(bank, 0, 320), AF.Abs)
+                if exact:
+                    act(R("crr", 128 * h, 128 * h + 128), rows_)
+                else:
+                    tt(R("crr", 128 * h, 128 * h + 128), R("Ag", 128 * h, 128 * h + 128), rows_, OP.max)
+                scan(low, R("RSr"), size_, OP.max, OP.min)
+                ts(R("oR", 16 * h, 16 * h + 16), ind(low, R("LN", 0, 1)), -1.0, OP.mult, 1087.0, OP.add)
+
+        part("choice a")
+        if RA:
+            act(R("r1"), R(PH[HA], 0, 128), bias=MAGIC2)
+            act(R("r2", a0, a0 + 128), R("r1"), bias=-MAGIC2)
+        for j in range(RA, 8):
+            stage[j](HA, 0, 128)
+        if not J:
+            part("pair a")
+            pair(HA)
+            part("sx a")
+            if not last:
+                side(8 * HA, 8 * HA + 8)
+        part("choice b")
+        if RB:
+            act(R("r1"), R(PH[HB], 0, 128), bias=MAGIC2)
+            act(R("r2", b0, b0 + 128), R("r1"), bias=-MAGIC2)
+        for j in range(RB, 8):
             for lo in range(0, 128, PART):
-                stage[j](1, lo, lo + PART)
-            if j == 4:
-                act(R("hd", 0, 16), R("ks", 15, 256, 16), AF.Sign, bias=0.75 / 4096)
-                act(R("xs"), ind(R("hd"), R("LE", 0, 8)), scale=-128.0)
-                act(R("misT"), R("hd", 0, 16), scale=-0.5, bias=0.5)
-                t_to_w(R("P6", 256, 272), "xs", False)
-        for f in rest:
-            f()
-        act(R("yy", 0, 128), ind(R("X"), R("ly", 0, 8)))
-        if t == 0:
-            act(R("kc"), ind(R("Kc"), LCW))
-        PA = R("P4", 304, 305, p1=8)
-        for h in range(2):
-            mm(PA, R("misT", 8 * h, 8 * h + 8), R("one", 0, 1), h == 0, h == 1)
-        act(R("hitW"), R("P6", 256, 272), AF.Sign, scale=-1.0, bias=255.5)
-        act(R("ymb", t, t + 1, p1=8), PA)
+                stage[j](HB, lo, lo + PART)
+        part("pair b")
+        if J:
+            pair_all()
+        else:
+            pair(HB)
+        nsent += (2 - J) * neng
+        part("hit")
+        act(R("hd", 0, 16), R("ks", 15, 256, 16), AF.Sign, bias=0.75 / 4096)
+        act(R("xs"), ind(R("hd", 0, 32), R("LE")), scale=-64.0)
+        t_to_w(R("P6", 256, 272), "xs", False)
+        act(R("hitW"), R("P6", 256, 272), AF.Sign, scale=-1.0, bias=127.5)
         act(R("hitW"), R("hitW"), AF.Relu)
         cp(R("lsel"), R("P6", 256, 272))
-        chosen(1)
-        payload(1)
-        mask(0)
-        ts(R("parT"), R("Pi"), 1, OP.bitwise_and)
-        low_bits(1)
-        tt(R("hd", 16, 32), R("hd", 16, 32), R("parT"), OP.not_equal)
-        e_list(1)
-        act(R("xd"), ind(R("hd"), R("LE", 8, 16)))
-        mask(1)
-        tt(R("t1"), R("P7", 0, 16), WC, OP.subtract)
-        pick(0, 256, "ke")
-        tt(R("t2"), R("t1"), R("hitW"), OP.mult)
-        pick(0, 0, "kc")
-        mm(R("P4", 128, 256), R("op2", 128, 256), R("Ib"), True, True)
+        part("y a")
+        if J:
+            act(R("yy"), ind(R("X"), R("ly")))
+        else:
+            act(R("yy", a0, a0 + 128), ind(R("X"), R("ly", 8 * HA, 8 * HA + 8)))
+        part("misses")
+        PA = R("P6", 320, 321, p1=8)
+        for h in range(2):
+            mm(PA, R("hd", 8 * h, 8 * h + 8), R("one", 0, 1), h == 0, h == 1)
+        act(R("ymb", t, t + 1, p1=8), PA, scale=-0.5, bias=128.0)
+        for h, n, name, where in ((HA, 8, " a", ("P4", 256, 344)), (HB, 8, " b", ("P2", 256, 400))) if XH else ((0, 16, " b", ("P2", 256, 400)),):
+            part("place" + name)
+            tt(R("t2", 8 * h, 8 * h + n), R("t1", 8 * h, 8 * h + n), R("hitW", 8 * h, 8 * h + n), OP.mult)
+            tt(R("wp", 8 * h, 8 * h + n), R("t2", 8 * h, 8 * h + n), R("W1", 16 + 8 * h, 16 + 8 * h + n), OP.add)
+            part("rivals" + name)
+            rivals(h, n, *where)
+        part("first a")
+        if J:
+            first_all()
+        else:
+            first(HA)
+        part("side")
+        act(R("xd"), ind(R("hd", 32, 64), R("LE")))
         t_to_w(R("P6", 288, 304), "xd", True)
-        act(R("yy", 128, 256), ind(R("X"), R("ly", 8, 16)))
         act(R("dW"), R("P6", 288, 304), scale=2.0, bias=-1.0)
-        act(R("m2s"), R("P4", 0, 256))
-        pick(1, 256, "ke")
-        y_to_w(R("P7", 16, 32), "Y2", 256, 512, True, False)
-        mm(R("P7", 16, 32), R("hIh"), R("dW"), False, True)
-        pick(1, 0, "kc")
-        tt(R("wp"), R("t2"), WC, OP.add)
-        own(16 if t else MID0)
+        part("y b")
+        if not J:
+            act(R("yy", b0, b0 + 128), ind(R("X"), R("ly", 8 * HB, 8 * HB + 8)))
+            part("first")
+            first(HB)
+        part("values a")
+        values(HA)
+        part("values b")
+        values(HB)
+        part("whole")
         if last:
-            ts(R("Bf", 0, 512), R("Bf", 0, 512), MAGIC - OFF, OP.add, MAGIC, OP.subtract)
-        cp(R("so", 16 * t, 16 * t + 16), R("P7", 16, 32))
-        send(R("so", 16 * t, 16 * t + 16), "ro", "ao%d" % t, dst, src)
-        if last:
-            ts(R("Bf", 512, 1024), R("Bf", 512, 1024), MAGIC - OFF, OP.add, MAGIC, OP.subtract)
-        nx = [8]
-
-        def shape(n=1):
-            for _ in range(min(n, nx[0])):
-                nx[0] -= 1
-                put_x(nx[0])
-
-        if t == 0:
-            consts_late()
-        for a in range(16):
-            mm(R("P5", 256, 272), Lsl("L1", (5 * t + a) % 16), R("Y2", a, 256, 16), a == 0, a == 15)
-        mm(R("P1", 0, 256), R("Perm"), R("m2s"), True, True)
-        ts(R("sc", 16 * t, 16 * t + 16), R("P5", 256, 272), -1.0 if last else OFF - 1.0, OP.add)
-        send(R("sc", 16 * t, 16 * t + 16), "rc", "ac%d" % t, dst, src)
-        nsent += 2 * neng
-        mm(R("P3", 0, 256), R("Ib"), R("yy"), False, False)
-        mm(R("P3", 256, 512), R("Ihalf"), R("yy"), False, True)
-        tt(R("Y1", 0, 256), R("ke"), R("P1", 0, 256), OP.mult)
-        lists = rivals(R("wp"), "EQx", ("P0", 256), "P2", "P2", ("P2", 400), "oX", (DXC, DX2))
-        act(R("Um"), R("P3"), bias=MAGIC)
-        tt(R("Y1", 256, 512), R("kc"), R("P1", 0, 256), OP.mult)
-        own(1)
-        act(R("val"), ind(R("Um"), R("lsel")), AF.Abs, bias=-MAGIC)
-        own(16)
-        for f in lists:
-            f()
-        RO, s = R("ro", 16 * t, 16 * t + 16), (5 * t) % 16
-        ts(R("w2"), RO, -1.0, OP.add)
-        tt(R("Ag"), ind(R("Bf"), R("w2")), R("NM", s, s + 256), OP.mult)
-        lists = rivals(RO, "EQ", ("P5", 272), "P6", "P0", ("P4", 352), "oR", (DBC, DB2))
-        tt(R("crr"), ind(R("rc", 16 * t, 16 * t + 16), R("LT")), R("MM", s, s + 256), OP.mult)
-        shape(XPRE)
-        for f in lists:
-            f()
+            for lo in (0, 512):
+                ts(R("Bf", lo, lo + 512), R("Bf", lo, lo + 512), MAGIC - OFF, OP.add, MAGIC, OP.subtract)
+            act(R("RM", MH, MH + 144), R("NM", 0, 144), scale=-4096.0, bias=-1.0)
+        part("in a")
+        if not J:
+            received(HA)
+        part("shapes")
+        for b in range(7, -1, -1):
+            put_x(b)
+        part("in" if J else "in b")
+        if J:
+            received_all()
+        else:
+            received(HB)
+        part("puts")
+        for b in range(3, -1, -1):
+            put_r(b, last or b // 2 not in RS)
+        part("lists")
         if not last:
             y_to_w(R("P7", 96, 112), "Y1", 0, 256, True, False)
             mm(R("P7", 96, 112), R("hIh"), R("dW"), False, True)
             y_to_w(R("P7", 112, 128), "Y1", 256, 512, True)
-            A1, A2, A3 = [R("ac", j, j + 1, p1=8) for j in range(3)]
-            act(A1, R("ymb", t, t + 1, p1=8), scale=0.499, bias=MAGIC)
-            act(A2, A1, scale=-2.0, bias=2 * MAGIC)
-            act(A3, A2, bias=R("ymb", t, t + 1, p1=8))
-            act(R("CT", 0, 128, p1=8), R("m8", p1=8), scale=A3)
-            side()
             next_lists()
-            diff(WO)
+            ts(R("lw"), R("P7", 96, 144), -1.0, OP.add)
+            part("level")
+            A1, A3 = R("ah", 0, 1, p1=8), R("ac", 0, 1, p1=8)
+            act(A1, R("ymb", t, t + 1, p1=8), scale=0.499, bias=128.0)
+            act(A3, A1, scale=-2.0, bias=R("ymb", t, t + 1, p1=8))
+            act(R("CT", 0, 128, p1=8), R("m8", p1=8), scale=A3)
+            part("sx")
+            side(8 * HB, 8 * HB + 8 + 8 * J)
+            part("open sums")
             open_sums()
+            part("own rivals")
+            diff(WO)
+            part("own eq")
             eq_s()
-            rot("Y1", 256, t + 1)
             losers(R("P4", 320, 336), WO, "EQs", "dW")
+            part("own rot")
+            rot("Y1", 256, t + 1)
+            part("q")
+            prep_q()
         else:
-            act(R("Gh", 0, 8), R("G8"))
+            part("out")
             act(R("Gh", 8, 16), R("G8"), scale=0.5)
-            act(R("dh"), R("hd", 16, 32))
             mm(R("P5", 0, 256, p1=8), R("Gh", 0, 8), R("Y1", 256, 512), True, True)
             mm(R("P5", 256, 512, p1=8), R("Gh", 8, 16), R("Y1", 0, 256), True, True)
             for h in range(2):
-                mm(R("P1", 128 * h, 128 * h + 128, p1=8), R("dh", 8 * h, 8 * h + 8), R("Ih"), True, True)
+                mm(R("P7", 128 * h, 128 * h + 128, p1=8), R("hd", 32 + 8 * h, 40 + 8 * h), R("Ib"), True, True)
             act(R("o8", 0, 256, p1=8), R("P5", 0, 256, p1=8), bias=-1.0)
             act(R("o8", 256, 512, p1=8), R("P5", 256, 512, p1=8), bias=-0.75)
-            act(R("o8", 512, 768, p1=8), R("P1", 0, 256, p1=8))
-        done = []
-        for b in range(7, -1, -1):
-            if b == LWB and not last:
-                ts(R("lw"), R("P7", 96, 144), -1.0, OP.add)
-            put_r(b)
-            shape(16 if b == 0 else 1)
-            if not nx[0] and b <= LWB and not done:
-                done.append(b)
-                if not last:
-                    prep_q()
-                else:
-                    dma("S", "dout", 16 * 7, T.ym[:], T.ymb[0:8, 0:6], [R("ymb")], [])
-                    dma("S", "dout", 16 * 7, T.yc[:], T.o8[0:8, 0:256], [R("o8")], [])
-                    dma("S", "dout", 16 * 7, T.yv[:], T.o8[0:8, 256:512], [R("o8")], [])
-                    dma("S", "dout", 16 * 7, T.yd[:], T.o8[0:8, 512:768], [R("o8")], [])
-                    for j in range(YS):
-                        act(R("xe", 256 * j, 256 * j + 256), R("X", 256 * j, 256 * j + 256), acc=R("ysb", j, j + 1))
+            act(R("o8", 512, 768, p1=8), R("P7", 0, 256, p1=8))
+            dma("S", "dout", 16 * 7, T.ym[:], T.ymb[0:8, 0:6], [R("ymb")], [])
+            dma("S", "dout", 16 * 7, T.yc[:], T.o8[0:8, 0:256], [R("o8")], [])
+            dma("S", "dout", 16 * 7, T.yv[:], T.o8[0:8, 256:512], [R("o8")], [])
+            dma("S", "dout", 16 * 7, T.yd[:], T.o8[0:8, 512:768], [R("o8")], [])
+            for j in range(YS):
+                act(R("xe", 256 * j, 256 * j + 256), R("X", 256 * j, 256 * j + 256), acc=R("ysb", j, j + 1))
 
     tot = 16 * 7
     dma("Y", "dout", tot, T.yb[0:64, :], T.Bf[0:64, 0:1024], [R("Bf")], [], 3500.0)
@@ -771,7 +1024,9 @@ def rank_program(g, core, T, topo):
     for b in range(YS, 8):
         row_sum(R("ysb", b, b + 1), R("X", 256 * b, 256 * b + 256))
     dma("S", "dout", tot, T.ys[:], T.ysb[:], [R("ysb")], [])
-    for i in order():
+    if not ORDER:
+        ORDER.extend(order())
+    for i in ORDER:
         calls[i][5]()
     g.wait_ge(T.sem.sent, nsent)
     for e in ("V", "S", "P", "G"):

from concourse.mybir import AluOpType as OP, ActivationFunctionType as AF, AxisListType

ST = 6
H = "float16"
MAGIC = 12582912.0
MAGIC2 = MAGIC * 2048
OFF = 25.0
S0 = 66
S00 = 60
GD = 10
GB = 8
S1 = 114
PART = 64
YS = 4
RS = (0, 1)
RED = ()
J = 0
RA = 1
XH = 0
QV = 0
EQV = 1
TWO = 1
E16S = 0
RB = 0

CYCLE = 1.0
COLUMN = 0.43
CALL = 0.0
START = 50.0
GATHER = 1.3
SCATTER = 3.2
WAKE = 175.0
SAME = 220.0
GSLOW = 1.35
LOAD = 2600.0
COPY = 900.0
FLIGHT = 1400.0
FIRST = 1800.0
STEP = 20780.0
QUICK = 9
SLOW = 120.0
DUE = {'start': 5620, 'for choice': 7150, 'bounds': 8110, 'tables': 13950, 'own new': 14360, 'side': 17740, 'for rivals': 19890, 'misses': 21400}
TURNS = {'G': 'start*2 for_sums*2'}
PASSES = 2

F, B16, I32, U16 = "float32", "bfloat16", "int32", "uint16"
SCRATCH = {}
ORDER = []


def _sb(name, cols, dtype):
    SCRATCH[name] = ("sbuf", [128, cols], dtype)


for _n, _c, _d in [
    ("X", 2080, B16), ("Bi", 1024, I32), ("Bf", 1088, F), ("Bc", 2048, H), ("wf", 16, F), ("rep", 128, H), ("LR", 8, U16), ("Kc", 2048, I32), ("KV", 2048, I32), ("RSr", 320, B16),
    ("l8", 768, I32), ("Y8", 768, H), ("vv", 16, H),
    ("Eu", 256, U16), ("E16", 256, H), ("nAg", 256, H), ("newc", 256, F), ("xe", 4096, B16), ("tt", 4096, F), ("q", 256, B16), ("yy", 256, B16),
    ("kc", 256, F), ("ke", 256, F), ("sx", 256, B16),
    ("r1", 128, F), ("r2", 256, F), ("f2", 256, F), ("key", 256, F), ("ks", 256, F), ("oh", 256, F), ("sl", 256, F), ("ss", 272, F),
    ("Pi", 16, I32), ("pT", 32, I32), ("hd", 64, B16), ("ah", 2, B16), ("ac", 8, F),
    ("xp", 128, H), ("xs", 128, H), ("xd", 128, H), ("op2", 256, B16), ("m2s", 256, B16), ("Y2", 512, H), ("Y1", 512, H),
    ("ly", 16, U16), ("lsel", 16, U16), ("lw", 48, U16),
    ("W1", 32, H), ("w2", 16, U16), ("wp", 16, H), ("dW", 16, H), ("hitW", 16, F), ("t1", 16, F), ("t2", 16, F),
    ("EQs", 256, H), ("ab", 256, F), ("oX", 32, U16), ("oO", 32, U16), ("Ag", 256, F), ("Um", 512, F), ("val", 256, B16),
    ("o8", 768, F), ("ysb", 8, F), ("ymb", 8, F),
    ("so", 32 * ST, F), ("ro", 32 * ST, F), ("rx", 768, H), ("rd", 1280, F), ("RM", 952, H), ("nIb", 128, B16),
    ("crr", 256, F), ("oR", 32, U16), ("MM", 144 + 128 * J, F),
    ("row", 272, F), ("row1", 128, F), ("xg", 128, F), ("xa", 144 + 128 * J, F), ("xa1", 128 + 128 * J, F),
    ("pi", 8, I32), ("pc", 32, F),
    ("Ib", 128, B16), ("Ih", 128, H), ("nIh", 128, H), ("hIh", 128, H), ("pIh", 128, H), ("I2n", 128, H), ("LS", 4 + 4 * J, U16), ("I4k", 128, H), ("Isx", 128, B16),
    ("Iq", 128, B16), ("Ihalf", 128, B16), ("Perm", 128, B16), ("BM", 128, H),
    ("Gq", 256, B16), ("G8", 8, F), ("G32", 32, F), ("Gx", 16, B16), ("Gh", 16, H), ("IN", 128, H), ("Dm", 2048, H), ("Dg", 2048, H), ("s12", 32, F),
    ("L1", 144, H), ("L2", 240, H), ("L8", 144, H), ("NM", 144 + 128 * J, F), ("RST", 128, F), ("LN", 2, U16), ("zi", 32, F), ("CT", 512, H), ("on16", 128, H), ("m8", 128, H), ("cU", 256, B16), ("EQx", 512, H),
    ("lane", 16, H), ("one", 16, B16),
    ("LK", 8, U16), ("LT", 16, U16), ("LE", 8, U16),
]:
    _sb(_n, _c, _d)
for _b in range(8):
    SCRATCH["P%d" % _b] = ("psum", [128, 512], F)

SEMAPHORES = (["sV", "sS", "sP", "sG", "sent", "dl", "dx", "db", "dk", "dr1", "dr2", "dout"]
              + ["a%d" % _t for _t in range(2 * ST)])


def rank_program(g, core, T, topo):
    rank = T.rank_of(core)
    if rank is None:
        return
    N = len(T.cores)
    Q = {"V": g.vector, "S": g.scalar, "P": g.tensor, "G": g, "Y": g.sync}
    cnt = {"V": 0, "S": 0, "P": 0, "G": 0}
    seen = {e: {} for e in Q}
    hist = {}

    def R(name, lo=0, hi=None, step=1, p1=128):
        if hi is None:
            hi = SCRATCH[name][1][1]
        return (name, lo, hi, T[name][0:p1, lo:hi:step] if step != 1 else T[name][0:p1, lo:hi], step)

    def meet(r, s):
        return r[1] < s[2] and s[1] < r[2] and not (r[4] == s[4] > 1 and (r[1] - s[1]) % r[4])

    def covers(r, s):
        return r[1] <= s[1] and s[2] <= r[2] and (r[4] == 1 or (r[4] == s[4] and (r[1] - s[1]) % r[4] == 0))

    def wait(e, tok):
        if seen[e].get(tok[0], 0) < tok[1]:
            Q[e].wait_ge(T.sem[tok[0]], tok[1])
            seen[e][tok[0]] = tok[1]

    def deps(e, reads, writes):
        need = {}
        for regs, w in ((reads, False), (writes, True)):
            for r in regs:
                ps = SCRATCH[r[0]][0] == "psum"
                for (r2, e2, tok, w2) in hist.get(r[0], []):
                    clash = meet(r, r2) and (w or w2)
                    if e2 != e:
                        clash = clash or ps
                    elif e == "P":
                        clash = False
                    if clash:
                        need[tok[0]] = max(need.get(tok[0], 0), tok[1])
        for k in sorted(need):
            wait(e, (k, need[k]))

    def note(e, tok, reads, writes):
        for regs, w in ((reads, False), (writes, True)):
            for r in regs:
                old = hist.get(r[0], [])
                keep = [x for x in old if not (covers(r, x[0]) and x[1] == e and x[2][0] == tok[0] and (w or not x[3]))]
                hist[r[0]] = keep + [(r, e, tok, w)]

    calls = []

    marks, now = [], [0]

    def part(name, later=0.0):
        marks.append((len(calls), now[0], name, later))

    def emit(e, reads, writes, call, time):
        def issue():
            deps(e, reads, writes)
            cnt[e] += 1
            call().then_inc(T.sem["s" + e], 1)
            note(e, ("s" + e, cnt[e]), reads, writes)
        time = time * GSLOW if e == "G" else time + CALL if e in "VS" else time
        calls.append((e, reads, writes, time, time + WAKE, issue, None))

    def size(r):
        return len(range(r[1], r[2], r[4]))

    def wide(r):
        return SCRATCH[r[0]][2] in (F, I32)

    def span(e, o, ins, each):
        for x, c in ((ins[0] if ins else o, GATHER), (o, SCATTER)):
            if len(x) == 2:
                return (50.0 if e == "V" else 65.0) + 16 * size(x[0][1]) * c
        return CYCLE * max(64, size(o) * each)

    def order():
        n = len(calls)
        before, after, past, group = [{} for _ in calls], [[] for _ in calls], {}, {}
        for i, (e, reads, writes, _, _, _, sem) in enumerate(calls):
            for regs, w in ((reads, False), (writes, True)):
                for r in regs:
                    ps = SCRATCH[r[0]][0] == "psum"
                    for (r2, j, w2) in past.get(r[0], []):
                        e2 = calls[j][0]
                        if e == e2 == "P":
                            if ps:
                                before[i][j] = calls[j][3]
                        elif (ps and e != e2) or (meet(r, r2) and (w or w2)):
                            for k in group.get(calls[j][6], [j]):
                                if k != i:
                                    before[i][k] = calls[k][3] + SAME if e == e2 and e in "VS" and not calls[k][6] else calls[k][4]
            for regs, w in ((reads, False), (writes, True)):
                for r in regs:
                    keep = [x for x in past.get(r[0], []) if not (x[1] in before[i] and covers(r, x[0]) and (w or not x[2]))]
                    past[r[0]] = keep + [(r, i, w)]
            if sem:
                group.setdefault(sem, []).append(i)
            for j in before[i]:
                after[j].append(i)

        left = {}
        for (lo, t, name, _), hi in zip(marks, [m[0] for m in marks[1:]] + [n]):
            for i in range(lo, hi):
                left.setdefault((t, name.replace(" ", "_"), calls[i][0]), []).append(i)
        for e, turns in TURNS.items():
            j = None
            for t in range(ST + 1):
                for word in turns.split():
                    name, _, k = word.partition("*")
                    line = left.get((t - (name[0] == "-"), name.lstrip("-"), e), [])
                    for _ in range(min(int(k or 1), len(line))):
                        i = line.pop(0)
                        if j is not None and j not in before[i]:
                            before[i][j] = calls[j][3]
                            after[j].append(i)
                        j = i

        def place(turn, earliest):
            busy, at = {e: [] for e in Q}, [0.0] * n
            for i in turn:
                line, t, time = busy[calls[i][0]], earliest(i, at), calls[i][3]
                k = len(line)
                while k and line[k - 1][1] > t:
                    k -= 1
                while k < len(line) and line[k][0] < t + time:
                    t = max(t, line[k][1])
                    k += 1
                line.insert(k, (t, t + time))
                at[i] = t
            return at

        def forward(i, at):
            return max([0.0] + [at[j] + d for j, d in before[i].items()])

        def backward(i, at):
            time = calls[i][3]
            return max([calls[i][4] - time] + [at[k] + calls[k][3] + before[k][i] - time for k in after[i]])

        due = [0.0] * n
        for (lo, t, name, later), hi in zip(marks, [m[0] for m in marks[1:]] + [n]):
            for i in range(lo, hi):
                due[i] = STEP * t + DUE.get(name, -30000.0) + later
        open_, ready = [len(b) for b in before], [i for i in range(n) if not before[i]]
        for i in ready:
            due[i] = max(due[i], forward(i, due))
            for k in after[i]:
                open_[k] -= 1
                if not open_[k]:
                    ready.append(k)
        assert len(ready) == n
        turn, best = sorted(range(n), key=lambda i: (due[i], i)), None
        for _ in range(PASSES):
            at = place(turn, forward)
            end = max(at[i] + calls[i][4] for i in range(n))
            if best is None or end < best[0]:
                best = (end, at)
            back = place(sorted(range(n), key=lambda i: (-at[i] - calls[i][3], -i)), backward)
            turn = sorted(range(n), key=lambda i: (-back[i] - calls[i][3], i))
        return sorted(range(n), key=lambda i: (best[1][i], i))

    def ind(win, off):
        return ([win, off], win[3].indirect(off[3]))

    def sides(x):
        return (x[0], x[1]) if len(x) == 2 else ([x], x[3])

    def outs(o):
        return ([o[0][0]], [o[0][1]], o[1]) if len(o) == 2 else ([o], [], o[3])

    def cp(o, i):
        w, r0, oa = outs(o)
        r, ia = sides(i)
        emit("V", r + r0, w, lambda: g.vector.tensor_copy(oa, ia), span("V", o, [i], 1.0 if wide(w[0]) or wide(r[0]) else 0.5))

    def tt(o, a, b, op):
        w, r0, oa = outs(o)
        r, ia = sides(a)
        both = SCRATCH[r[0][0]][0] == SCRATCH[b[0]][0]
        emit("V", r + r0 + [b], w, lambda: g.vector.tensor_tensor(oa, ia, b[3], op), span("V", o, [a], 2.0 if both else 1.0))

    def ts(o, a, s1, op0, s2=None, op1=None):
        r, ia = sides(a)
        rs = [s for s in (s1, s2) if isinstance(s, tuple)]
        a1 = s1[3] if isinstance(s1, tuple) else s1
        a2 = s2[3] if isinstance(s2, tuple) else s2
        time = span("V", o, [a], 1.0 if wide(o) or wide(r[0]) else 0.5)
        if op1 is None:
            emit("V", r + rs, [o], lambda: g.vector.tensor_scalar(o[3], ia, a1, None, op0), time)
        else:
            emit("V", r + rs, [o], lambda: g.vector.tensor_scalar(o[3], ia, a1, a2, op0, op1), time)

    def scan(o, d0, d1, op0=OP.min, op1=OP.max):
        each = 1.0 if wide(o) or wide(d0) or wide(d1) else 0.5
        emit("V", [d0, d1], [o], lambda: g.vector.tensor_tensor_scan(o[3], d0[3], d1[3], 0.0, op0, op1), span("V", o, [d1], each))

    def mset(o, v):
        emit("V", [], [o], lambda: g.vector.memset(o[3], v), span("V", o, [], 1.0 if wide(o) else 0.5))

    def row_sum(o, i):
        emit("V", [i], [o], lambda: g.vector.tensor_reduce(o[3], i[3], AxisListType.X, OP.add), span("V", i, [i], 1.0))

    def least(o, i):
        emit("V", [i], [o], lambda: g.vector.tensor_reduce(o[3], i[3], AxisListType.X, OP.min, apply_absolute_value=True), span("V", i, [i], 1.0))

    def act(o, i, fn=AF.Identity, bias=0.0, scale=1.0, acc=None):
        w, r0, oa = outs(o)
        r, ia = sides(i)
        rs = [s for s in (bias, scale) if isinstance(s, tuple)]
        ba = bias[3] if isinstance(bias, tuple) else bias
        sa = scale[3] if isinstance(scale, tuple) else scale
        time = span("S", o, [i], 1.0)
        if fn == AF.Silu:
            emit("S", r + r0, w, lambda: g.scalar.activation(oa, ia, fn), time if len(o) == 2 else time + 1300.0)
        elif acc is None:
            emit("S", r + rs, w, lambda: g.scalar.activation(oa, ia, fn, bias=ba, scale=sa), time)
        else:
            emit("S", r + rs, w + [acc], lambda: g.scalar.activation(oa, ia, fn, bias=ba, scale=sa, accum_out=acc[3]), time)

    def mm(o, l, r, start, stop):
        emit("P", [l, r], [o], lambda: g.tensor.matmul(o[3], l[3], r[3], start, stop),
             COLUMN * max(min(64, size(l)), size(r)) * (4 if wide(l) else 1))

    def iota(o, pat, base=0, cm=0):
        time = 160.0 + 2 * CYCLE * size(o)
        if SCRATCH[o[0]][2] != I32:
            emit("G", [], [o], lambda: g.iota(o[3], pat, base, cm, allow_small_or_imprecise_dtypes=True), time)
        else:
            emit("G", [], [o], lambda: g.iota(o[3], pat, base, cm), time)

    def select(o, i, pat, base, cm):
        emit("G", [i], [o], lambda: g.affine_select(o[3], i[3], pat, OP.is_equal, 0.0, base, cm), 210.0 + 2 * CYCLE * size(o))

    def dma(e, sem, total, out_ap, in_ap, reads, writes, time=COPY):
        def issue():
            deps(e, reads, writes)
            Q[e].dma_start(out_ap, in_ap).then_inc(T.sem[sem], 16)
            note("D", (sem, total), reads, writes)
        calls.append((e, reads, writes, START, time, issue, sem))

    def send(reg, rname, sem, dst, src):
        land = R(rname, reg[1], reg[2])
        rid, pid = topo.addr(dst, core)

        def issue():
            deps("G", [reg], [])
            g.remote_dma(land[3], reg[3], T.sem[sem], T.sem.sent, pid, rid, topo.mask(core, dst))
            note("R", (sem, len(topo.engines(src, core))), [], [land])
        late = FIRST if now[0] == 0 and (J or reg[1] == 16 * HA) else 0.0
        calls.append(("G", [reg], [land], 300.0 + late, FLIGHT + late, issue, None))

    PCOL, ACOL, GCOL, HC, B7, L1C, L2C, L8C, LANEC, DXC, DBC, MC, E0C, E1C = [R("pc", j, j + 1) for j in range(14)]
    S0C, S1C, DX2 = [R("pc", j, j + 1) for j in range(16, 19)]
    M1, M2, CC, MH = 0, 320, 648, 808

    def run(b):
        lo = 160 * (b // 4) + 8 * (b % 4) * (b % 4 + 1)
        return lo, lo + 16 * (b % 4 + 1)

    HA, HB = 1, 0
    C1, C2 = R("pc", 14, 15, p1=16), R("pc", 15, 16, p1=16)
    LOPP, LCW, LOWN, WO, WC = R("lw", 0, 16), R("lw", 16, 32), R("lw", 32, 48), R("W1", 0, 16), R("W1", 16, 32)
    PH = ("P1", "P2")

    part("start")
    dma("Y", "dl", 48, T.l8[0:8, 0:256], T.lv[:], [], [R("l8", 0, 256)])
    dma("S", "dl", 48, T.l8[0:8, 256:512], T.ld[:], [], [R("l8", 256, 512)])
    dma("Y", "dl", 48, T.l8[0:8, 512:768], T.lc[:], [], [R("l8", 512, 768)])
    dma("S", "db", 16, T.Bi[:], T.bnd[:], [], [R("Bi")], LOAD)
    dma("Y", "dx", 16, T.X[:, 0:2048], T.x[:], [], [R("X", 0, 2048)], LOAD)
    dma("Y", "dk", 16, T.Kc[:, 0:512], T.kt[:], [R("Bi")], [R("Kc", 0, 512)], LOAD)

    pi = lambda j: R("pi", j, j + 1)
    iota(pi(0), [[0, 1]], 0, 1)
    iota(R("row", 0, 144), [[1, 144]])
    mset(R("ab", 0, 64), OFF)
    act(R("Bf", 1024, 1088), R("ab", 0, 64), AF.Silu)
    cp(PCOL, pi(0))
    ts(L8C, pi(0), 16.0, OP.mult, 15.0, OP.add)
    mset(R("X", 2048, 2080), 0.0)
    mset(R("hd"), 0.0)
    ts(R("L8", 0, 144), R("row", 0, 144), L8C, OP.is_equal)
    ts(R("Ih"), R("row", 0, 128), PCOL, OP.is_equal)
    ts(R("hIh"), R("Ih"), -0.5, OP.mult)
    ts(R("pIh"), R("Ih"), 0.5, OP.mult)
    cp(R("LT"), R("row", 0, 16))
    part("for sums")
    iota(R("xg"), [[1, 8], [0, 16]])
    iota(R("xa"), [[0, 9 + 8 * J], [1, 16]])
    mset(R("on16", p1=16), 1.0)
    ts(pi(1), pi(0), 15, OP.bitwise_and)
    ts(pi(2), pi(0), 4, OP.arith_shift_right)
    ts(pi(3), pi(0), 8, OP.bitwise_and)
    ts(pi(4), pi(0), 7, OP.bitwise_and)
    cp(R("pc", 1, 5), R("pi", 1, 5))
    ts(R("G8"), R("row", 0, 8), GCOL, OP.is_equal)
    ts(R("BM"), R("xg"), GCOL, OP.is_equal)
    ts(C1, R("pc", 0, 1, p1=16), 8.0, OP.is_equal, -2048.0, OP.mult)
    ts(C2, R("pc", 0, 1, p1=16), 8.0, OP.is_equal, -1.0 / 4096, OP.mult)
    ts(R("CT", 384, 512, p1=16), R("on16", p1=16), 2040.0, OP.mult, C2, OP.mult)
    part("for own")
    ts(R("s12", 16, 32), R("row", 0, 16), ACOL, OP.is_equal)
    ts(R("I2n"), R("Ih"), -2.0, OP.mult)
    ts(L1C, GCOL, 16.0, OP.mult, 15.0, OP.add)
    ts(R("s12", 0, 16), R("row", 0, 16), ACOL, OP.is_ge)
    for r in range(GD, 16):
        select(R("Dg", 128 * r, 128 * r + 128), R("Ih"), [[0, 8], [1, 16]], -r, 0)
    part("for choice")
    iota(R("row", 144, 272), [[1, 128]], 144)
    iota(R("xa1"), [[0, 8 + 8 * J], [2, 8], [-1, 2]], 1)
    iota(R("row1"), [[2, 64], [-1, 2]], 1)
    part("for rivals")
    for a in range(16):
        if a < GB:
            select(R("Bc", 128 * a, 128 * a + 128), R("BM"), [[-16, 8], [0, 16]], -a, 1)
        else:
            act(R("Bc", 128 * a, 128 * a + 128), R("BM"), scale=R("s12", 16 + a, 17 + a))

    def Lsl(name, a, p1=128):
        return R(name, 15 - a, 143 - a, p1=p1)

    def y_to_w(out, ybuf, lo, hi, start, stop=True, L="L1", p1=128):
        for a in range(16):
            mm(out, Lsl(L, a, p1), R(ybuf, lo + a, hi, 16, p1=p1), start and a == 0, stop and a == 15)

    def rot(ybuf, lo, t, L="L1", p1=128):
        for a in range(16):
            mm(R("P5", a, 256, 16), Lsl(L, (5 * t + a) % 16, p1), R(ybuf, lo + a, lo + 256, 16, p1=p1), a == 0, False)

    def old_rows(t):
        mm(R("P5", 0, 256), R("nIh"), R("nAg"), False, False)
        for a in range(16):
            r = (5 * t + a) % 16
            mm(R("P5", a, 256, 16), R("Dg", 128 * r, 128 * r + 128), R("nAg", a, 256, 16), False, a == 15)

    def t_to_w(out, xbuf, start, stop=True):
        for gg in range(8):
            mm(out, R("L2", 112 - 16 * gg, 240 - 16 * gg), R(xbuf, 16 * gg, 16 * gg + 16), start and gg == 0, stop and gg == 7)

    def diff(w, bank="P6", lo=1, hi=16):
        for a in range(lo, hi):
            mm(R(bank, 16 * a, 16 * a + 16), R("Dm", 128 * a, 128 * a + 128), w, True, True)

    def eq_s(bank="P6"):
        if EQV:
            ts(R("EQs", 16, 256), R(bank, 16, 256), 0.0, OP.is_equal, 4096.0, OP.mult)
        else:
            act(R("ab", 16, 256), R(bank, 16, 256), AF.Abs)
            act(R("EQs", 16, 256), R("ab", 16, 256), AF.Relu, scale=-4096.0, bias=4096.0)

    def losers(out, w, buf, sign=None, stop=True):
        mm(out, R("Ih"), w, True, False)
        if sign:
            mm(out, R("Ih"), R(sign), False, False)
        for a in range(1, 16):
            mm(out, Lsl("L1", a), R(buf, 16 * a, 16 * a + 16), False, stop and a == 15)

    def offs(o, src, dummy):
        ts(o, src, -1.0, OP.add, dummy, OP.min)

    def put_r(b, exact):
        o = 16 * (b // 2) + 4 * (b % 2)
        o = ind(R("Bf"), R("oR", o, o + 4))
        if exact:
            tt(o, R("Ag", 64 * b, 64 * b + 64), R("crr", 64 * b, 64 * b + 64), OP.max)
        else:
            act(o, R("crr", 64 * b, 64 * b + 64), AF.Silu)

    def put_o(b):
        act(ind(R("Bf"), R("oO", 2 * b, 2 * b + 1)), R("newc", 16 * b, 16 * b + 16), AF.Silu)

    def put_x(b):
        cp(ind(R("X"), R("oX", 2 * b, 2 * b + 2)), R("val", 32 * b, 32 * b + 32))

    def rivals(h, n, bank, across, out):
        lo, e = 8 * h, 256 * h
        w, wf, rep = R("wp", lo, lo + n), R("wf", lo, lo + n), R("rep", 8 * lo, 8 * (lo + n))
        act(wf, w)
        act(rep, ind(wf, R("LR", 0, n // 2)))
        for a in range(16):
            mm(R(bank, across + a, across + 8 * n, 16), R("Bc", 128 * a, 128 * a + 128), R("wp", lo, lo + n, 2), True, True)
        for a in range(1, 16):
            mm(R(bank, n * a, n * a + n), R("Dm", 128 * a, 128 * a + 128), w, True, True)
        tt(R("EQx", e + 16 * n, e + 24 * n), rep, R(bank, across, across + 8 * n), OP.is_equal)
        ts(R("EQx", e + n, e + 16 * n), R(bank, n, 16 * n), 0.0, OP.is_equal, 4096.0, OP.mult)
        scan(R("EQx", e + 24 * n, e + 32 * n), R("RST", 0, 8 * n), R("EQx", e + 16 * n, e + 24 * n))
        mm(R(bank, out, out + n), R("Ih"), w, True, False)
        for a in range(1, 16):
            mm(R(bank, out, out + n), Lsl("L1", a), R("EQx", e + n * a, e + n * a + n), False, False)
        mm(R(bank, out + 1, out + n, 2), R("I4k"), R("EQx", e + 24 * n + 15, e + 32 * n, 16), False, True)
        for j, spare in enumerate((DXC, DX2)):
            offs(R("oX", lo + j, lo + n, 2), R(bank, out + j, out + n, 2), spare)

    def side(lo=0, hi=16):
        act(R("sx", 16 * lo, 16 * hi), ind(R("hd", 32, 48), R("LT", lo, hi)), scale=1.0 / 256, bias=-1.0 / 512)

    def open_sums():
        for h in range(2):
            mm(R(PH[h]), R("on16", p1=16), R("CT", p1=16), True, False)
            mm(R(PH[h], 0, 128), R("Isx"), R("sx", 128 * h, 128 * h + 128), False, False)

    def prep_q():
        (cp if QV else act)(R("q"), ind(R("X"), LCW))
        for j in range(2 * TWO):
            h = j // TWO
            mm(R("P0", 128 * TWO * h + j % TWO, 128 * TWO * (h + 1), TWO), R("sx", 128 * h, 128 * h + 128), R("Ib"), j == 0, False)
        for j in range(TWO):
            mm(R("P0", j, 256 * TWO, TWO), R("Ib"), R("q"), False, j == TWO - 1)
        for h in (HA, HB):
            mm(R(PH[h], 256, 512), R("q", 128 * h, 128 * h + 128), R("Gq"), False, False)

    def next_lists():
        act(R("W1"), R("P7", 96, 128))
        mm(R("P7", 128, 144), R("Ih"), WO, True, False)
        mm(R("P7", 128, 144), R("Ih"), R("dW"), False, True)

    part("start")
    cp(R("Y8", 0, 512, p1=8), R("l8", 0, 512, p1=8))
    ts(R("Y8", 512, 768, p1=8), R("l8", 512, 768, p1=8), 1.0, OP.add)
    y_to_w(R("P7", 80, 128), "Y8", 0, 768, True, True, "L8", 8)
    for h in range(2):
        mm(R("P6", 304 + 8 * h, 312 + 8 * h), R("Y8", 256 + 128 * h, 384 + 128 * h, p1=8), R("Ih", 0, 8, p1=8), True, True)
    ts(R("vv"), R("P7", 80, 96), 2.0, OP.mult, 1.5, OP.add)
    ts(R("dW"), R("P7", 96, 112), 2.0, OP.mult, -1.0, OP.add)
    cp(R("hd", 32, 48), R("P6", 304, 320))
    for (lo, I) in ((96, "hIh"), (128, "pIh")):
        mm(R("P7", lo, lo + 16), R("Ih"), R("vv"), True, False)
        mm(R("P7", lo, lo + 16), R(I), R("dW"), False, True)
    ts(R("lw"), R("P7", 96, 144), -1.0, OP.add)
    part("for sums")
    act(R("Ib"), R("Ih"))
    act(R("Isx"), R("Ih"), scale=-262144.0)
    act(R("Gq", 0, 128), R("BM"), scale=-1.0 / 256)
    act(R("Gq", 128, 256), R("BM"), scale=1.0 / 4096)
    for j, s in enumerate((32768.0, 1.0 / 256, 1.0 / 128, -1.0 / 2048)):
        act(R("G32", 8 * j, 8 * j + 8), R("G8"), scale=s)
    act(R("Gx", 0, 8), R("G8"), scale=-1.0 / 256)
    act(R("Gx", 8, 16), R("G8"), scale=1.0 / 4096)
    xa16 = R("xa", 0, 128, p1=16)
    ts(R("CT", 0, 128, p1=16), xa16, -15.015625, OP.add, C1, OP.mult)
    ts(R("CT", 128, 256, p1=16), xa16, -15.0, OP.add, C2, OP.mult)
    ts(R("CT", 256, 384, p1=16), xa16, 2.0, OP.add, C2, OP.mult)
    part("for own")
    act(R("W1"), R("P7", 96, 128))
    act(R("nIh"), R("Ih"), scale=-1.0)
    for r in range(GD):
        act(R("Dg", 128 * r, 128 * r + 128), R("Ih"), scale=R("s12", 16 + r, 17 + r))
    rot("Y8", 512, 0, "L8", 8)

    def consts_d(lo, hi):
        for a in range(lo, hi):
            ts(R("Dm", 128 * a, 128 * a + 128), R("IN"), R("s12", a, a + 1), OP.mult, R("s12", 16 + a, 17 + a), OP.min)

    tt(R("IN"), R("BM"), R("I2n"), OP.add)
    consts_d(1, 10)
    part("for sums")
    side()
    open_sums()

    def table(s, sem):
        for j in range(1, 4):
            dma("Y", sem, 48, T[s][:, 512 * j:512 * j + 512], T[s][:, 0:512], [R(s, 0, 512)], [R(s, 512 * j, 512 * j + 512)])

    def consts_choice():
        act(R("RST", 0, 128), R("xa", 0, 128), scale=1.0e8, bias=-5.0e7)
        act(R("Gh", 0, 8), R("G8"))
        act(R("nIb"), R("Ib"), scale=-1.0)
        act(L2C, ACOL, bias=112.0)
        act(LANEC, ACOL, bias=64.0)
        act(S0C, HC, scale=16.0 if J else 2.0, bias=-241.0 if J else -113.0)
        act(E0C, HC, bias=-16.0)
        ts(MC, B7, GCOL, OP.is_equal)
        ts(R("LK"), R("row", 0, 8), 16.0, OP.mult, 15.0, OP.add)
        if J:
            mset(R("ss", 256, 272), 0.0)
        else:
            mset(R("ss", 128, 136), 0.0)
            mset(R("ss", 264, 272), 0.0)
        mset(R("one"), 1.0)
        act(E0C, E0C, scale=MC, bias=16.0)
        act(S0C, S0C, scale=MC, bias=256.0 if J else 128.0)
        act(S1C, MC, scale=16.0 if J else 32.0)
        for h in range(2):
            act(R("lane", 8 * h, 8 * h + 8), R("row", 0, 8), scale=16.0, bias=LANEC)
        act(R("Iq"), R("Ib"), scale=-0.25)
        act(R("Ihalf"), R("Ib"), scale=0.5)

    def consts_lists():
        ts(R("L2"), R("row", 0, 240), L2C, OP.is_equal)
        ts(R("LE", 0, 8), R("row", 0, 8), MC, OP.mult, E0C, OP.add)
        mset(R("cU", 0, 128), 0.375)
        mset(R("cU", 128, 256), -0.25)
        ts(R("LS"), R("row", 0, 4 + 4 * J), S1C, OP.mult, S0C, OP.add)

    def consts_late():
        ts(R("Perm"), R("row1"), PCOL, OP.is_equal)
        ts(R("NM"), R("xa"), ACOL, OP.not_equal)
        ts(R("MM"), R("xa"), ACOL, OP.is_equal)
        ts(R("m8", p1=8), R("xg", p1=8), R("pc", 0, 1, p1=8), OP.is_equal, 64.0, OP.mult)
        ts(DXC, ACOL, 2048.0, OP.add)
        ts(DX2, ACOL, 2064.0, OP.add)
        act(R("I4k"), R("Ih"), scale=4096.0)
        ts(R("LR"), R("row", 0, 8), 2.0, OP.mult, 1.0, OP.add)

    def consts_received():
        GE, SP = R("zi", 8, 24), R("zi", 24, 28)
        mset(R("RM", M1, M1 + 320), 0.0)
        act(R("zi", 0, 8), R("G8"), scale=-4096.0)
        ts(GE, R("row", 0, 16), ACOL, OP.is_ge, 2048.0, OP.mult)
        ts(SP, R("row", 0, 4), 16.0, OP.mult, ACOL, OP.add)
        mset(R("zi", 23, 24), 1088.0)
        for b in range(8):
            lo, hi = run(b)
            cp(R("RM", M1 + lo, M1 + hi - 1), R("I4k", 64 * (b // 4), 64 * (b // 4) + hi - lo - 1))
            act(R("RM", M2 + lo, M2 + hi), R("xa", 0, hi - lo), scale=0.0, bias=R("zi", b, b + 1))
        for u in range(4):
            lo, hi = run(u)
            act(R("RM", M2 + hi - 1, M2 + 320, 160), R("G8", u, 8, 4), scale=-1.0)
            if u:
                act(R("RM", CC + lo, CC + hi - 16), R("xa", 0, hi - lo - 16), scale=0.0, bias=R("zi", 24 + u, 25 + u))
            ts(R("RM", CC + hi - 16, CC + hi), GE, R("zi", 24 + u, 25 + u), OP.max)
        act(R("RM", MH, MH + 144), R("NM", 0, 144), scale=-4096.0, bias=OFF - 1.0)
        mset(R("RSr"), 0.0)
        for u in range(4):
            mset(R("RSr", run(u)[0], 320, 160), 4096.0)
        U, C4, Z = [R("zi", j, j + 1) for j in range(28, 31)]
        ts(pi(5), pi(0), 3, OP.bitwise_and)
        ts(pi(6), pi(0), 4, OP.bitwise_and)
        cp(R("zi", 28, 30), R("pi", 5, 7))
        act(Z, U, scale=8.0, bias=24.0)
        act(C4, C4, scale=40.0, bias=15.0)
        ts(R("LN", 0, 1), Z, U, OP.mult, C4, OP.add)

    def values(h):
        o, q, y = 256 * h, R("q", 128 * h, 128 * h + 128), R("yy", 128 * h, 128 * h + 128)
        mm(R("P3", o, o + 256), R("Ib"), R("cU"), True, False)
        mm(R("P3", o, o + 128), R("Iq"), q, False, False)
        mm(R("P3", o + 128, o + 256), R("Ihalf"), q, False, False)
        mm(R("P3", o, o + 128), R("Ib"), y, False, False)
        mm(R("P3", o + 128, o + 256), R("Ihalf"), y, False, True)
        act(R("Um", o, o + 256), R("P3", o, o + 256), bias=MAGIC)
        act(R("val", 128 * h, 128 * h + 128), ind(R("Um", o, o + 256), R("lsel", 8 * h, 8 * h + 8)), AF.Abs, bias=-MAGIC)

    nsent = 0
    for t in range(ST):
        last = t == ST - 1
        dst = T.cores[(rank + 1 + t % (N - 1)) % N]
        src = T.cores[(rank - 1 - t % (N - 1)) % N]
        neng = len(topo.engines(core, dst))

        BT, boff = (R("Bi"), 0.0) if t == 0 else (R("Bf"), OFF)
        a0, b0 = 128 * HA, 128 * HB
        now[0] = t
        part("bounds")
        ts(R("Eu", a0, a0 + 128), ind(BT, R("lw", 8 * HA, 8 * HA + 8)), 0.25 - boff, OP.add)
        s0, s1 = (S00, 128) if t == 0 else (S0, S1)
        if t == 0:
            prep_q()
        part("own old" if t else "first own")
        act(R("nAg"), ind(BT, LOWN), scale=-1.0, bias=boff - 1.0)
        part("rows a")
        act(R("xe", 16 * a0, 16 * (a0 + s0)), ind(R("X"), R("Eu", a0, a0 + s0)))
        part("bounds", 200)
        ts(R("Eu", b0, b0 + 128), ind(BT, R("lw", 8 * HB, 8 * HB + 8)), 0.25 - boff, OP.add)
        part("bounds", 430)
        cp(R("xe", 16 * (a0 + s0), 16 * a0 + 2048), ind(R("X"), R("Eu", a0 + s0, a0 + 128)))
        part("rows b")
        act(R("xe", 16 * b0, 16 * (b0 + s1)), ind(R("X"), R("Eu", b0, b0 + s1)))
        part("own old" if t else "first own")
        if t == 0:
            consts_d(10, 16)
            ts(R("L1"), R("row", 0, 144), L1C, OP.is_equal)
            diff(WO)
            eq_s()
            ts(DBC, ACOL, 1024.0, OP.add)
        old_rows(t)
        part("number")
        if E16S:
            act(R("E16"), ind(BT, LOPP), bias=1.0 - boff)
        else:
            ts(R("E16"), R("Eu"), 1.0, OP.add)
        part("own new")
        act(R("newc"), R("P5", 0, 256), bias=OFF - 1.0)

        kind = lambda h, j, lo, hi: R(PH[h], 128 * j + lo, 128 * j + hi)
        sb = lambda n, h, lo, hi: R(n, 128 * h + lo, 128 * h + hi)
        stage = [
            lambda h, lo, hi: ts(sb("r2", h, lo, hi), kind(h, 0, lo, hi), MAGIC2, OP.add, MAGIC2, OP.subtract),
            lambda h, lo, hi: tt(sb("f2", h, lo, hi), sb("r2", h, lo, hi), kind(h, 0, lo, hi), OP.subtract),
            lambda h, lo, hi: tt(sb("r2", h, lo, hi), sb("f2", h, lo, hi), kind(h, 1, lo, hi), OP.min),
            lambda h, lo, hi: tt(sb("key", h, lo, hi), sb("r2", h, lo, hi), kind(h, 2, lo, hi), OP.max),
            lambda h, lo, hi: scan(sb("ks", h, lo, hi), R("RST", lo, hi), sb("key", h, lo, hi)),
            lambda h, lo, hi: tt(sb("oh", h, lo, hi), ind(sb("ks", h, lo, hi), R("LK", 0, (hi - lo) // 16)), sb("key", h, lo, hi), OP.is_equal),
            lambda h, lo, hi: tt(sb("sl", h, lo, hi), sb("oh", h, lo, hi), kind(h, 3, lo, hi), OP.mult),
            lambda h, lo, hi: scan(R("ss", (136 - 8 * J) * h + lo, (136 - 8 * J) * h + hi), R("RST", lo, hi), sb("sl", h, lo, hi)),
        ]

        def sum_x(h, k):
            mm(R(PH[h], 256 + k, 512, 16), R("xe", 2048 * h + k, 2048 * h + 2048, 16), R("Gx"), False, False)

        def rows(h, k):
            n, k = k, k // TWO + 16 // TWO * (k % TWO)
            o, w = 2048 * h + 128 * (n - n % TWO), 128 * TWO
            if n % TWO == 0:
                tt(R("tt", o, o + w), R("xe", 2048 * h + k, 2048 * h + 2048, 16 // TWO), R("P0", w * h, w * h + w), OP.min)
            if h == HB:
                sum_x(h, k)
            mm(R(PH[h], k, 512, 16), R("tt", o + n % TWO, o + w, TWO), R("G32"), False, False)
            if h == HB and n in (1, 15):
                hh = HA if n == 1 else HB
                mm(R(PH[hh], 384, 512), R("E16", 128 * hh, 128 * hh + 128), R("Ih"), False, True)

        part("min a")
        for k in range(16):
            sum_x(HA, k)
        for k in range(16):
            part("min a", 133 * k)
            rows(HA, k)
        part("rest b")
        if s1 < 128:
            cp(R("xe", 16 * (b0 + s1), 16 * b0 + 2048), ind(R("X"), R("Eu", b0 + s1, b0 + 128)))
        for k in range(16):
            part("min b", 133 * k + SLOW * max(0, k - QUICK))
            rows(HB, k)
        part("tables")
        if t == 0:
            losers(R("P4", 320, 336), WO, "EQs", "dW")
            ts(R("KV", 0, 512), R("Kc", 0, 512), 511, OP.bitwise_and)
            table("KV", "dr2")
            table("Kc", "dr1")
            consts_choice()
            act(R("Bf", 0, 1024), R("Bi"), bias=OFF)
            consts_lists()
            consts_late()
            consts_received()
        part("own list")
        offs(R("oO", 0, 32, 2), R("P4", 320, 336), DBC)
        part("own put")
        for b in range(15, -1, -1):
            put_o(b)
        part("kc")
        act(R("kc"), ind(R("Kc"), LCW), bias=1.0)
        part("open values")
        mm(R("P6", 256, 272), R("Ih"), R("lane"), True, False)
        EW = {HA: R("P5", 352, 360), HB: R("P7", 0, 8)}

        def chosen(h):
            ts(R("xp", 64 * h, 64 * h + 64), ind(R("ss", 136 * h, 136 * h + 136), R("LS")), MAGIC, OP.add, MAGIC, OP.subtract)
            for gg in range(8):
                mm(EW[h], R("L2", 112 - 16 * gg, 240 - 16 * gg), R("xp", 64 * h + 8 * gg, 64 * h + 8 * gg + 8), gg == 0, gg == 7)

        def payload(h):
            ts(R("Pi", 8 * h, 8 * h + 8), R("ss", 136 * h + 15, 136 * h + 128, 16), 4096.0, OP.mult, 2040.125, OP.add)

        def low_bits(h):
            ts(R("pT", 8 * h, 8 * h + 8), R("Pi", 8 * h, 8 * h + 8), 15, OP.bitwise_and)

        def e_list(h):
            ts(R("ly", 8 * h, 8 * h + 8), EW[h], -1.0, OP.add)
            act(R("ke", 128 * h, 128 * h + 128), ind(R("KV"), R("ly", 8 * h, 8 * h + 8)), scale=2.0, bias=1.5)

        MK = {HA: R("P4", a0, a0 + 128), HB: R("P0", b0, b0 + 128)}
        OUT = {HA: ("P5", 336), HB: ("P7", 16)}
        IN = {HA: "P5", HB: PH[HB]}
        M1B = {HA: "P4", HB: "P0"}
        s = (5 * t) % 16

        def parity(h):
            ts(R("pT", 16 + 8 * h, 24 + 8 * h), R("Pi", 8 * h, 8 * h + 8), 1, OP.bitwise_and)

        def flip(h):
            d = R("hd", 32 + 8 * h, 40 + 8 * h)
            tt(d, d, R("pT", 16 + 8 * h, 24 + 8 * h), OP.not_equal)

        def post(h):
            bank, lo = OUT[h]
            col, slot = R(bank, lo, lo + 8), R("so", 32 * t + 16 * h, 32 * t + 16 * h + 16)
            mm(col, R("Ihalf"), R("one", 0, 8), True, False)
            mm(col, R("nIb"), R("hd", 32 + 8 * h, 40 + 8 * h), False, False)
            mm(R(bank, lo + 8, lo + 16), R("Y2", 128 * h, 128 * h + 128), R("Gh", 0, 8), False, False)
            mm(col, R("Y2", 256 + 128 * h, 384 + 128 * h), R("Gh", 0, 8), False, True)
            act(slot, R(bank, lo, lo + 16))
            send(slot, "ro", "a%d" % (2 * t + h), dst, src)

        def received(h):
            lo, bank = 32 * t + 16 * h, IN[h]
            col = ind(R("ro", lo, lo + 8), R("LT", 0, 8))
            own_, al, cc = [R("rx", 384 * h + 128 * j, 384 * h + 128 * j + 128) for j in range(3)]
            rows_ = R(bank, 384, 512)
            tt(own_, col, R("MM", 0, 128), OP.mult)
            act(R("rx", 384 * h + 128, 384 * h + 384), ind(R("ro", lo, lo + 16), R("LT")))
            lst = R("w2", 8 * h, 8 * h + 8)
            for c in range(2):
                mm(R(bank, 160 * c, 160 * c + 160), R("Ih"), R("RM", CC, CC + 160), c == 0, False)
            mm(rows_, R("Ih"), R("RM", MH + s, MH + s + 128), False, False)
            if h == HB:
                mm(R("P7", 32, 40), own_, R("Gh", 0, 8), True, True)
                ts(lst, R("P7", 32, 40), -1.0, OP.add)
            mm(R(bank, 0, 320), own_, R("RM", M2, M2 + 320), False, False)
            mm(R(bank, 0, 320), al, R("RM", M1, M1 + 320), False, False)
            if h == HA:
                mm(R(bank, 320, 328), own_, R("Gh", 0, 8), False, False)
            mm(rows_, cc, R("Ih"), False, True)
            if h == HA:
                ts(lst, R(bank, 320, 328), -1.0, OP.add)
            tt(R("Ag", 128 * h, 128 * h + 128), ind(R("Bf"), lst), R("NM", s, s + 128), OP.mult)
            size_, low = R("rd", 640 * h, 640 * h + 320), R("rd", 640 * h + 320, 640 * h + 640)
            exact = last or h not in RS
            if h not in RED:
                act(size_, R(bank, 0, 320), AF.Abs)
            if not exact:
                tt(R("crr", 128 * h, 128 * h + 128), R("Ag", 128 * h, 128 * h + 128), rows_, OP.max)
            if h in RED:
                for b in range(7, -1, -1):
                    least(R("rd", 640 * h + b, 640 * h + b + 1), R(bank, *run(b)))
                ts(R("oR", 16 * h, 16 * h + 8), R("rd", 640 * h, 640 * h + 8), -1.0, OP.mult, 1087.0, OP.add)
            else:
                scan(low, R("RSr"), size_, OP.max, OP.min)
                ts(R("oR", 16 * h, 16 * h + 16), ind(low, R("LN", 0, 1)), -1.0, OP.mult, 1087.0, OP.add)
            if exact:
                act(R("crr", 128 * h, 128 * h + 128), rows_)

        def mask(h):
            o = R("op2", 128 * h, 128 * h + 128)
            tt(o, ind(R("pT", 8 * h, 8 * h + 8), R("LT", 0, 8)), R("xa1"), OP.is_equal)
            mm(MK[h], o, R("Ib"), True, True)

        def pick(h, lo, k):
            tt(R("Y2", lo + 128 * h, lo + 128 * h + 128), R(k, 128 * h, 128 * h + 128), MK[h], OP.mult)

        def pair(h):
            for f in (payload, chosen, low_bits, parity, mask, flip, e_list, place_of):
                f(h)
            pick(h, 0, "kc")
            pick(h, 256, "ke")
            post(h)

        def place_of(h):
            tt(R("t1", 8 * h, 8 * h + 8), EW[h], R("W1", 16 + 8 * h, 24 + 8 * h), OP.subtract)

        def first(h):
            lo, hi = 128 * h, 128 * h + 128
            m1 = R(M1B[h], 256 + lo, 256 + hi)
            act(R("m2s", lo, hi), MK[h])
            mm(m1, R("Perm"), R("m2s", lo, hi), True, True)
            tt(R("Y1", lo, hi), R("ke", lo, hi), m1, OP.mult)
            tt(R("Y1", 256 + lo, 256 + hi), R("kc", lo, hi), m1, OP.mult)

        def pair_all():
            col, slot = R("P7", 16, 32), R("so", 32 * t, 32 * t + 32)
            ts(R("Pi"), R("ss", 15, 256, 16), 4096.0, OP.mult, 2040.125, OP.add)
            ts(R("xp"), ind(R("ss"), R("LS")), MAGIC, OP.add, MAGIC, OP.subtract)
            t_to_w(R("P7", 0, 16), "xp", True)
            ts(R("pT", 0, 16), R("Pi"), 15, OP.bitwise_and)
            ts(R("pT", 16, 32), R("Pi"), 1, OP.bitwise_and)
            tt(R("op2"), ind(R("pT", 0, 16), R("LT", 0, 16)), R("xa1"), OP.is_equal)
            for bank in ("P0", "P4"):
                for h in range(2):
                    mm(R(bank, 128 * h, 128 * h + 128), R("op2", 128 * h, 128 * h + 128), R("Ib"), True, True)
            tt(R("hd", 32, 48), R("hd", 32, 48), R("pT", 16, 32), OP.not_equal)
            ts(R("ly"), R("P7", 0, 16), -1.0, OP.add)
            act(R("ke"), ind(R("KV"), R("ly")), scale=2.0, bias=1.5)
            tt(R("t1"), R("P7", 0, 16), WC, OP.subtract)
            tt(R("Y2", 0, 256), R("kc"), R("P0", 0, 256), OP.mult)
            tt(R("Y2", 256, 512), R("ke"), R("P0", 0, 256), OP.mult)
            mm(col, R("Ihalf"), R("one"), True, False)
            mm(col, R("nIb"), R("hd", 32, 48), False, False)
            for j in range(4):
                o = 32 - 16 * (j // 2) + 8 * (j % 2)
                mm(R("P7", o, o + 8), R("Y2", 128 * j, 128 * j + 128), R("Gh", 0, 8), False, j == 3)
            act(slot, R("P7", 16, 48))
            send(slot, "ro", "a%d" % (2 * t), dst, src)

        def first_all():
            act(R("m2s"), R("P4", 0, 256))
            mm(R("P4", 256, 512), R("Perm"), R("m2s"), True, True)
            tt(R("Y1", 0, 256), R("ke"), R("P4", 256, 512), OP.mult)
            tt(R("Y1", 256, 512), R("kc"), R("P4", 256, 512), OP.mult)

        def received_all():
            lo, exact = 32 * t, last
            tt(R("rx", 0, 256), ind(R("ro", lo, lo + 16), R("LT", 0, 16)), R("MM", 0, 256), OP.mult)
            for j in range(2):
                act(R("rx", 256 + 256 * j, 512 + 256 * j), ind(R("ro", lo + 16 * j, lo + 16 * j + 16), R("LT", 0, 16)))
            for h in (HA, HB):
                for c in range(2):
                    mm(R(IN[h], 160 * c, 160 * c + 160), R("Ih"), R("RM", CC, CC + 160), c == 0, False)
                mm(R(IN[h], 384, 512), R("Ih"), R("RM", MH + s, MH + s + 128), False, False)
            for h in range(2):
                mm(R("P7", 48 + 8 * h, 56 + 8 * h), R("rx", 128 * h, 128 * h + 128), R("Gh", 0, 8), True, True)
            ts(R("w2"), R("P7", 48, 64), -1.0, OP.add)
            tt(R("Ag"), ind(R("Bf"), R("w2")), R("NM", s, s + 256), OP.mult)
            for h in (HA, HB):
                part("in a" if h == HA else "in b")
                bank, rows_ = IN[h], R(IN[h], 384, 512)
                mm(R(bank, 0, 320), R("rx", 128 * h, 128 * h + 128), R("RM", M2, M2 + 320), False, False)
                mm(R(bank, 0, 320), R("rx", 256 + 128 * h, 384 + 128 * h), R("RM", M1, M1 + 320), False, False)
                mm(rows_, R("rx", 512 + 128 * h, 640 + 128 * h), R("Ih"), False, True)
                size_, low = R("rd", 640 * h, 640 * h + 320), R("rd", 640 * h + 320, 640 * h + 640)
                act(size_, R(bank, 0, 320), AF.Abs)
                if exact:
                    act(R("crr", 128 * h, 128 * h + 128), rows_)
                else:
                    tt(R("crr", 128 * h, 128 * h + 128), R("Ag", 128 * h, 128 * h + 128), rows_, OP.max)
                scan(low, R("RSr"), size_, OP.max, OP.min)
                ts(R("oR", 16 * h, 16 * h + 16), ind(low, R("LN", 0, 1)), -1.0, OP.mult, 1087.0, OP.add)

        part("choice a")
        if RA:
            act(R("r1"), R(PH[HA], 0, 128), bias=MAGIC2)
            act(R("r2", a0, a0 + 128), R("r1"), bias=-MAGIC2)
        for j in range(RA, 8):
            stage[j](HA, 0, 128)
        if not J:
            part("pair a")
            pair(HA)
            part("sx a")
            if not last:
                side(8 * HA, 8 * HA + 8)
        part("choice b")
        if RB:
            act(R("r1"), R(PH[HB], 0, 128), bias=MAGIC2)
            act(R("r2", b0, b0 + 128), R("r1"), bias=-MAGIC2)
        for j in range(RB, 8):
            for lo in range(0, 128, PART):
                stage[j](HB, lo, lo + PART)
        part("pair b")
        if J:
            pair_all()
        else:
            pair(HB)
        nsent += (2 - J) * neng
        part("hit")
        act(R("hd", 0, 16), R("ks", 15, 256, 16), AF.Sign, bias=0.75 / 4096)
        act(R("xs"), ind(R("hd", 0, 32), R("LE")), scale=-64.0)
        t_to_w(R("P6", 256, 272), "xs", False)
        act(R("hitW"), R("P6", 256, 272), AF.Sign, scale=-1.0, bias=127.5)
        act(R("hitW"), R("hitW"), AF.Relu)
        cp(R("lsel"), R("P6", 256, 272))
        part("y a")
        if J:
            act(R("yy"), ind(R("X"), R("ly")))
        else:
            act(R("yy", a0, a0 + 128), ind(R("X"), R("ly", 8 * HA, 8 * HA + 8)))
        part("misses")
        PA = R("P6", 320, 321, p1=8)
        for h in range(2):
            mm(PA, R("hd", 8 * h, 8 * h + 8), R("one", 0, 1), h == 0, h == 1)
        act(R("ymb", t, t + 1, p1=8), PA, scale=-0.5, bias=128.0)
        for h, n, name, where in ((HA, 8, " a", ("P4", 256, 344)), (HB, 8, " b", ("P2", 256, 400))) if XH else ((0, 16, " b", ("P2", 256, 400)),):
            part("place" + name)
            tt(R("t2", 8 * h, 8 * h + n), R("t1", 8 * h, 8 * h + n), R("hitW", 8 * h, 8 * h + n), OP.mult)
            tt(R("wp", 8 * h, 8 * h + n), R("t2", 8 * h, 8 * h + n), R("W1", 16 + 8 * h, 16 + 8 * h + n), OP.add)
            part("rivals" + name)
            rivals(h, n, *where)
        part("first a")
        if J:
            first_all()
        else:
            first(HA)
        part("side")
        act(R("xd"), ind(R("hd", 32, 64), R("LE")))
        t_to_w(R("P6", 288, 304), "xd", True)
        act(R("dW"), R("P6", 288, 304), scale=2.0, bias=-1.0)
        part("y b")
        if not J:
            act(R("yy", b0, b0 + 128), ind(R("X"), R("ly", 8 * HB, 8 * HB + 8)))
            part("first")
            first(HB)
        part("values a")
        values(HA)
        part("values b")
        values(HB)
        part("whole")
        if last:
            for lo in (0, 512):
                ts(R("Bf", lo, lo + 512), R("Bf", lo, lo + 512), MAGIC - OFF, OP.add, MAGIC, OP.subtract)
            act(R("RM", MH, MH + 144), R("NM", 0, 144), scale=-4096.0, bias=-1.0)
        part("in a")
        if not J:
            received(HA)
        part("shapes")
        for b in range(7, -1, -1):
            put_x(b)
        part("in" if J else "in b")
        if J:
            received_all()
        else:
            received(HB)
        part("puts")
        for b in range(3, -1, -1):
            put_r(b, last or b // 2 not in RS)
        part("lists")
        if not last:
            y_to_w(R("P7", 96, 112), "Y1", 0, 256, True, False)
            mm(R("P7", 96, 112), R("hIh"), R("dW"), False, True)
            y_to_w(R("P7", 112, 128), "Y1", 256, 512, True)
            next_lists()
            ts(R("lw"), R("P7", 96, 144), -1.0, OP.add)
            part("level")
            A1, A3 = R("ah", 0, 1, p1=8), R("ac", 0, 1, p1=8)
            act(A1, R("ymb", t, t + 1, p1=8), scale=0.499, bias=128.0)
            act(A3, A1, scale=-2.0, bias=R("ymb", t, t + 1, p1=8))
            act(R("CT", 0, 128, p1=8), R("m8", p1=8), scale=A3)
            part("sx")
            side(8 * HB, 8 * HB + 8 + 8 * J)
            part("open sums")
            open_sums()
            part("own rivals")
            diff(WO)
            part("own eq")
            eq_s()
            losers(R("P4", 320, 336), WO, "EQs", "dW")
            part("own rot")
            rot("Y1", 256, t + 1)
            part("q")
            prep_q()
        else:
            part("out")
            act(R("Gh", 8, 16), R("G8"), scale=0.5)
            mm(R("P5", 0, 256, p1=8), R("Gh", 0, 8), R("Y1", 256, 512), True, True)
            mm(R("P5", 256, 512, p1=8), R("Gh", 8, 16), R("Y1", 0, 256), True, True)
            for h in range(2):
                mm(R("P7", 128 * h, 128 * h + 128, p1=8), R("hd", 32 + 8 * h, 40 + 8 * h), R("Ib"), True, True)
            act(R("o8", 0, 256, p1=8), R("P5", 0, 256, p1=8), bias=-1.0)
            act(R("o8", 256, 512, p1=8), R("P5", 256, 512, p1=8), bias=-0.75)
            act(R("o8", 512, 768, p1=8), R("P7", 0, 256, p1=8))
            dma("S", "dout", 16 * 7, T.ym[:], T.ymb[0:8, 0:6], [R("ymb")], [])
            dma("S", "dout", 16 * 7, T.yc[:], T.o8[0:8, 0:256], [R("o8")], [])
            dma("S", "dout", 16 * 7, T.yv[:], T.o8[0:8, 256:512], [R("o8")], [])
            dma("S", "dout", 16 * 7, T.yd[:], T.o8[0:8, 512:768], [R("o8")], [])
            for j in range(YS):
                act(R("xe", 256 * j, 256 * j + 256), R("X", 256 * j, 256 * j + 256), acc=R("ysb", j, j + 1))

    tot = 16 * 7
    dma("Y", "dout", tot, T.yb[0:64, :], T.Bf[0:64, 0:1024], [R("Bf")], [], 3500.0)
    dma("Y", "dout", tot, T.yb[64:128, :], T.Bf[64:128, 0:1024], [R("Bf")], [], 3500.0)
    for b in range(YS, 8):
        row_sum(R("ysb", b, b + 1), R("X", 256 * b, 256 * b + 256))
    dma("S", "dout", tot, T.ys[:], T.ysb[:], [R("ysb")], [])
    if not ORDER:
        ORDER.extend(order())
    for i in ORDER:
        calls[i][5]()
    g.wait_ge(T.sem.sent, nsent)
    for e in ("V", "S", "P", "G"):
        wait("G", ("s" + e, cnt[e]))
    g.wait_ge(T.sem.dout, tot)
